import numpy as np, ml_dtypes
CORES = [3,11,19,27,35,43,51,59]
N = 8
BF = ml_dtypes.bfloat16
O, S, FB, NB, ST = 2560, 2048, 48, 2, 4
W = O + S; F = FB * NB
def cut(n, p):
    return np.where(np.arange(16)[:, None] < n, p, -1)
def turns():
    return (np.arange(N)[:, None, None, None] + np.arange(F) // FB) % N
def parts(rng):
    lev = rng.integers(-60, 61, (N, 8, 1, W)) + rng.choice(np.array([-20, 0, 20]), (N, 8, 1, 1))
    D = np.clip(lev + rng.integers(-36, 37, (N, 8, 16, W)), -96, 96)
    x = rng.integers(0, W, (N, 8, 8, 2, O))
    v = rng.integers(0, 4, (N, 8, 16, F)) * (rng.random((N, 8, 1, F)) > 0.05)
    u = rng.random((N, 8, 16, F)); k = rng.integers(0, S, u.shape)
    p = np.where(u < 0.5, rng.integers(0, O, u.shape), O + np.where(u < 0.85, turns(), rng.integers(0, N, u.shape)) * S + k)
    return D, x, v, cut(rng.integers(0, 13, (N, 8, 1, F)), p)
def mend(x):
    c = np.arange(O); a, b = x[:, :, :, 0], x[:, :, :, 1]
    for _ in range(4): a = np.where((a == c) | (a == O + c), (a + 1) % W, a)
    for _ in range(4): b = np.where((b == c) | (b == O + c) | (b == a), (b + 1) % W, b)
    return np.stack([a, b], axis=3)
def pack(D, x, v, p):
    return {"dn": np.ascontiguousarray(D.reshape(N, 128, W)).astype(np.float32).astype(BF), "det": np.ascontiguousarray(mend(x).reshape(N, 128, O)).astype(np.int32),
            "fv": np.ascontiguousarray(v.reshape(N, 128, F)).astype(np.float32).astype(BF), "pth": np.ascontiguousarray(p.reshape(N, 128, F)).astype(np.int32)}
def setup_inputs(rng):
    D, x, v, p = parts(rng)
    return pack(D, x, v, p)
def setup_inputs_ties(rng):
    D, x, v, p = parts(rng); z = np.zeros((1, 1, 16, 1), np.int64)
    D = rng.integers(-3, 4, (N, 8, 1, W)) + z; v = rng.integers(1, 4, (N, 8, 1, F)) + z
    v[:, 1::2] = v[:, 1::2] * (np.arange(16)[:, None] == rng.integers(0, 16, (N, 4, 1, F)))
    x[:, 7, :, 0] = x[:, 7, :, 0] // 2 * 2; x[:, 7, :, 1] = x[:, 7, :, 1] // 2 * 2 + 1
    D[:, 7] = np.where(np.arange(W) % 2 == 1, 3, -3)
    return pack(D, x, v, p)
def setup_inputs_crowd(rng):
    D, x, v, p = parts(rng)
    pool = np.argsort(rng.random((N, 8, W)), axis=-1)[..., :400]; size = np.array([24, 400, 24, 400, 60, 400, 24, 200])[None, :, None]
    x = np.take_along_axis(pool, (rng.random((N, 8, 16 * O)) * size).astype(np.int64), 2).reshape(N, 8, 8, 2, O)
    few = rng.integers(0, O, (N, 8, 10)); np.put_along_axis(D, few[:, :, None, :], 90, 3)
    hot = np.take_along_axis(few, rng.integers(0, 10, (N, 8, 16 * F)), 2).reshape(N, 8, 16, F)
    m = (p >= 0) & (rng.random(p.shape) < np.array([0.7, 0.2, 0.5, 0.1, 0.9, 0.3, 0.4, 0.6])[None, :, None, None])
    return pack(D, x, v, np.where(m, hot, p))
def setup_inputs_full(rng):
    D, x, v, p = parts(rng); v[:, :, 0] = np.maximum(v[:, :, 0], 1); V = (ST + NB - 1) // NB
    for g in range(8):
        d = D[:, g]; xa, xb = x[:, g, :, 0], x[:, g, :, 1]
        if g % 4 == 0:
            z = rng.permutation(S)[:3 * FB * ST].reshape(3, ST, FB)
            d[:, :, O + z[0].reshape(-1)] = 96; d[:, :, O + z[1:].reshape(-1)] = -96
            for t in range(ST):
                xa[:, 0][:, z[0, t]] = O + z[1, t]; xb[:, 0][:, z[0, t]] = O + z[2, t]; b = t % NB
                for n in range(N): p[n, g, t // NB, b * FB:(b + 1) * FB] = O + ((n + t) % N) * S + z[0, t]
        elif g % 4 == 1:
            z = rng.permutation(O); e = z[:(V + 1) * F].reshape(V + 1, F); a = z[(V + 1) * F:(2 * V + 1) * F].reshape(V, F); dead = z[(2 * V + 1) * F:(2 * V + 1) * F + 64]
            v[:, g] = 3 * (v[:, g] > 0)
            d[:, :, e[0]] = 96; d[:, :, a.reshape(-1)] = -96; d[:, :, dead] = -96
            for u in range(V):
                d[:, :, e[u + 1]] = -(u + 1); xa[:, :, e[u]] = a[u]; xb[:, :, e[u]] = e[u + 1]
            p[:, g, :11] = rng.choice(dead, (N, 11, F)); p[:, g, 11] = e[0]; p[:, g, 12:] = -1
        elif g % 4 == 2:
            z = rng.permutation(S); y = z[:3 * F].reshape(3, NB, FB); dead = z[3 * F:3 * F + 64]
            d[:, :, O + y[0].reshape(-1)] = 96; d[:, :, O + y[1:].reshape(-1)] = -96; d[:, :, O + dead] = -96
            p[:, g, 12:] = -1
            for b in range(NB):
                xa[:, 0][:, y[0, b]] = O + y[1, b]; xb[:, 0][:, y[0, b]] = O + y[2, b]
                for n in range(N):
                    s = O + ((n + b) % N) * S
                    p[n, g, :11, b * FB:(b + 1) * FB] = s + rng.choice(dead, (11, FB)); p[n, g, 11, b * FB:(b + 1) * FB] = s + y[0, b]
        else:
            base = O if g == 7 else 0; z = rng.permutation(S)[:3 * FB].reshape(3, FB); w = np.where(rng.permutation(16) < 4, 96, -96)[:, None]
            v[:, g] = 3; p[:, g] = -1
            d[:, :, base + z[0]] = -w; d[:, :, base + z[1]] = w; d[:, :, base + z[2]] = -96
            xa[:, :, z[0]] = base + z[1]; xb[:, :, z[0]] = base + z[2]
            for t in range(ST):
                b = t % NB
                for n in range(N): p[n, g, t // NB, b * FB:(b + 1) * FB] = z[0] + (O + ((n + t) % N) * S if g == 7 else 0)
    return pack(D, x, v, p)
def setup_inputs_ends(rng):
    D, x, v, p = parts(rng); e = np.array([0, O - 1, O, W - 1])
    D[..., e] = rng.choice(np.array([-96, 96]), (N, 8, 1, 4)); x[:, ::2] = rng.choice(e, (N, 4, 8, 2, O))
    s = O + turns() * S; nxt = O + ((turns() + 1) % N) * S; prv = O + ((turns() - 1) % N) * S + S - 1; j = rng.integers(0, 7, p.shape)
    o = np.where(j == 0, 0, np.where(j == 1, O - 1, np.where(j == 2, s, np.where(j == 3, s + S - 1, np.where(j == 5, nxt, np.where(j == 6, prv, O + N * S - 1))))))
    p = cut(rng.choice(np.array([0, 1, 12]), (N, 8, 1, F)), np.where(rng.random(p.shape) < 0.6, o, rng.integers(0, O + N * S, p.shape)))
    v = 3 * rng.integers(0, 2, (N, 8, 1, F)) + np.zeros((1, 1, 16, 1), np.int64)
    D[rng.integers(0, N), 3] = -96; p[:, 5] = -1
    return pack(D, x, v, p)
def setup_inputs_spread(rng):
    D, x, v, p = parts(rng)
    D = np.clip(np.rint(np.exp2(6.6 * rng.random((N, 8, 1, W))) * (2 * rng.random((N, 8, 16, W)) - 1)), -96, 96)
    v = (rng.random((N, 8, 16, F)) < rng.random((N, 8, 1, F))) * rng.integers(1, 4, (N, 8, 16, F))
    return pack(D, x, v, p)
def check_inputs(d):
    bad = []
    for k, lo, hi in (("dn", -96, 96), ("fv", 0, 3)):
        w = np.asarray(d[k]).astype(np.float32)
        if not np.all((w == np.rint(w)) & (w >= lo) & (w <= hi)): bad.append("whole numbers and range of " + k)
    for k, lo, hi in (("det", 0, W - 1), ("pth", -1, O + N * S - 1)):
        if np.min(d[k]) < lo or np.max(d[k]) > hi: bad.append("range of " + k)
    x = np.asarray(d["det"]).reshape(N, 8, 8, 2, O); a, b, c = x[:, :, :, 0], x[:, :, :, 1], np.arange(O)
    if np.any((a == b) | (a == c) | (a == O + c) | (b == c) | (b == O + c)): bad.append("a detour's links differ from each other, from c and from O + c")
    q = np.asarray(d["pth"]).reshape(N, 8, 16, F) >= 0
    if np.any(q[:, :, 1:] & ~q[:, :, :-1]): bad.append("a path's links come before its empty rows")
    if np.any(q[:, :, 12:]): bad.append("at most 12 links a path")
    return bad
def reference(dn, det, fv, pth):
    D = dn.astype(np.float32).astype(np.int32).reshape(N, 8, 16, W)
    own = D[..., :O].copy(); blk = D[..., O:].copy()
    v = fv.astype(np.float32).astype(np.int32).reshape(N, 8, 16, F)
    p = pth.astype(np.int64).reshape(N, 8, 16, F); dd = det.astype(np.int64).reshape(N, 8, 16, O)
    lower = np.arange(FB)[None, :] < np.arange(FB)[:, None]
    gi, fi = np.arange(8)[:, None], np.arange(FB)[None, :]
    for t in range(ST):
        lo = (t % NB) * FB
        for r in range(N):
            B = (r + t) % N
            win = np.concatenate([own[r], blk[B]], axis=2)
            f = v[r, :, :, lo:lo + FB]; q = p[r, :, :, lo:lo + FB]
            mine = (q >= 0) & (q < O); turn = (q >= O + B * S) & (q < O + (B + 1) * S)
            col = np.where(mine, q, np.where(turn, q - B * S, 0)); site = np.where(col < O, col, col - O)
            ab = np.take_along_axis(dd[r], site.reshape(8, 1, 16 * FB), 2)
            Dab = np.take_along_axis(win, ab.reshape(8, 1, -1), 2).reshape(8, 16, 8, 2, 16, FB); ab = ab.reshape(8, 8, 2, 16, FB)
            add = np.add.reduce(np.maximum(Dab + f[:, :, None, None, None, :], 0) - np.maximum(Dab, 0), axis=1)
            Dl = np.take_along_axis(win, col.reshape(8, 1, -1), 2).reshape(8, 16, 16, FB)
            sub = np.add.reduce(np.maximum(Dl, 0) - np.maximum(Dl - f[:, :, None, :], 0), axis=1)
            sc = np.where((mine | turn)[:, None], add[:, :, 0] + add[:, :, 1] - sub[:, None], 10 ** 6)
            sc = sc.transpose(0, 3, 2, 1).reshape(8, FB, 128)
            best = np.argmin(sc, axis=2); cho = np.min(sc, axis=2) < 0; row, k = best >> 3, best & 7
            nm = np.stack([col[gi, row, fi], ab[gi, k, 0, row, fi], ab[gi, k, 1, row, fi]], axis=2)
            same = np.any(nm[:, :, None, :, None] == nm[:, None, :, None, :], axis=(3, 4))
            com = cho & ~np.any(same & lower[None] & cho[:, None, :], axis=2)
            g, j = np.nonzero(com); l, a, b = nm[g, j, 0], nm[g, j, 1], nm[g, j, 2]; df = f[g, :, j]
            win[g, :, l] -= df; win[g, :, a] += df; win[g, :, b] += df
            n = np.count_nonzero(q >= 0, axis=1)
            q[g, row[g, j], j] = np.where(a < O, a, a + B * S); q[g, n[g, j], j] = np.where(b < O, b, b + B * S)
            own[r] = win[..., :O]; blk[B] = win[..., O:]
    yd = np.stack([np.concatenate([own[r], blk[(r + ST - 1) % N]], axis=2) for r in range(N)])
    return {"yd": yd.reshape(N, 128, W).astype(np.float32).astype(BF), "yp": p.reshape(N, 128, F).astype(np.float32)}

@@ -1,0 +1,626 @@
+from concourse.mybir import AluOpType as A, AxisListType as AX, ActivationFunctionType as AF
+
+O, S, W, FB, ST = 2560, 2048, 4608, 48, 4
+WX = 5168
+J = WX
+WD = J + WX + O
+EMPTY = float(1 << 16)
+NV = [[8, 8, 6], [7, 8, 5], [7, 8, 5], [7, 8, 6]]
+GROUPS = [(0, 2), (2, 3)]
+NES = [True, True, True]
+NQ = "sssv"
+DETCH = 4
+NCH = [(O, W, "s"), (0, 1024, "v"), (1024, 2048, "v"), (2048, O, "v")]
+
+SCRATCH = {"G": ("sbuf", [128, 48, 240], "bfloat16")}
+for _dt, _bufs in (
+        ("bfloat16", dict(DW=WD, NW=WD, fvS=96, fpm=288, F16=1536, SF=288, tmp=768, X=384, Comb=224, Tm=768, ident=128, Sh=128, t1=128,
+                          t2=128, t3=128, ind=16, qm=192, NE=864, Dg=144, idS=768, one=48, sg=288, yb=96, ne=48, SV0=288, SV1=288,
+                          SV2=288, SV3=288, L0=S, L1=S, L2=S, RV0=288, RV1=288, RV2=288)),
+        ("float32", dict(detF=O + 48, Pf=96, Py=96, cw=480, cb=320, K=16, c=128, xc=128, hi=256, I2=104, I3=104, I4=32, bd=128, cv=48,
+                         dum=12, MC=12, M=12, nm=144, rs=96, fo=12, ny=12, nd=12, dd=12, idF=256, cB=48, pw=480, AB0=816, AB1=816,
+                         MK0=144, MK1=144, sel0=144, sel1=144, mR0=48, mR1=48, sd0=12, sd1=12)),
+        ("int32", dict(detI=O, pthI=96, pI=2)),
+        ("uint16", dict(col16=96, site16=96, IL=12, ML=12, RL=12, Fl=96, SFl=18, A160=768, A161=768, cm0=4, cm1=4, SO0=16, SO1=16,
+                        SO2=16, SO3=16, RO0=16, RO1=16, RO2=16))):
+    for _n, _w in _bufs.items():
+        SCRATCH[_n] = ("sbuf", [128, _w], _dt)
+for _n in ("P10", "P11", "P12", "P2", "QQ", "QD", "PA", "P3"):
+    SCRATCH[_n] = ("psum", [128, 512], "float32")
+
+SEMAPHORES = (["qv", "qs", "qp", "qg"] + ["dm%d" % i for i in range(24)] + ["ls%d" % i for i in range(9)]
+              + ["ar%d" % i for i in range(9)])
+
+CY = 1.04e-3
+HOP = 0.06
+BOOST = 8.0
+CB = 16.0
+BWL = 250e3
+FX = 0.03
+GA = 1.56
+SC = 3.8
+RL0 = 1.2
+PRI = {'sAB0': -8, 'sAB2': -11, 'vnd0': -17, 'vsel1': 48, 'gc': 22, 'gpI': 28, 'vNblk': -8, 'sne': 4.0, 'sidF': -31.0, 'vNown0': 25.0,
+       'vRL0': 55.0, 'vNown2': 27.0, 'gNdum': -13.0, 'vML1': -7.0, 'vIL1': -8.0, 'sF': 7.0, 'gxc': -25.0, 'gI4b': -18.0, 'vsd1': -17.0,
+       'sMK1': 44.0, 'vIL0': 23.0, 'vSVd0': -9.0, 'sX0': -6.0, 'sCm': -8.0, 'gGs': -37.0, 'gI': 32.0, 'sNE1': 11.0, 'vdetF': 9.0,
+       'vgrp': -61.0, 'sAB1': -5.0, 'vsd2': -17.0, 'vPy': -18.0, 'vt': -8.0, 'sX1': 18.0, 'sk': 21.0, 'vTm': 71.0, 'vm0': -7.0,
+       'vsd0': -9.0, 'vFl': -50.0, 'sNE0': 9.0, 'vsite': 11.0, 'vdum': -34.0, 'vnm1': 23.0, 'vpf': 29.0, 'vpm': -13.0, 'vdd1': -4.0,
+       'vML2': 22.0, 'vdd0': 5.0, 'vnm0': 16.0, 'vA2': 15.0, 'sNE2': -5.0, 'vGs': -3.0, 'vm2': 16.0, 'vpw': -7.0, 'vyb': -2.0, 'vs1': 12.0}
+
+
+def build(T, rank, topo, core):
+    ops = []
+    nd = [0]
+    nr = [0]
+    bo = [0.0]
+
+    def op(eng, fn, r, w, dur, **k):
+        d = dict(eng=eng, fn=fn, r=list(r), w=list(w), dur=dur, lat=0.0, sem=None, val=1, after=[], boost=bo[0])
+        d.update(k)
+        ops.append(d)
+        return len(ops) - 1
+
+    def small(n, f=1.0):
+        return FX + max(64, n * f) * CY
+
+    def ts(out, in0, s1, s2, o0, o1, r, w, n, f=1.0, dur=None):
+        if o1 is None:
+            fn = lambda g: g.vector.tensor_scalar(out, in0, s1, None, o0)
+        else:
+            fn = lambda g: g.vector.tensor_scalar(out, in0, s1, s2, o0, o1)
+        return op("v", fn, r, w, dur or small(n, f))
+
+    def tt(out, a, b, o, r, w, n, f=2.0, dur=None):
+        return op("v", lambda g: g.vector.tensor_tensor(out, a, b, o), r, w, dur or small(n, f))
+
+    def cp(out, a, r, w, n, f=1.0, dur=None):
+        return op("v", lambda g: g.vector.tensor_copy(out, a), r, w, dur or small(n, f))
+
+    def red(out, a, o, r, w, n, ab=False):
+        return op("v", lambda g: g.vector.tensor_reduce(out, a, AX.X, o, apply_absolute_value=ab), r, w, small(n))
+
+    def scan(out, a, b, r, w, n):
+        return op("v", lambda g: g.vector.tensor_tensor_scan(out, a, b, 0.0, A.add, A.min), r, w, small(n))
+
+    def ms(ap, val, w, n, f=1.0):
+        return op("v", lambda g: g.vector.memset(ap, val), [], w, small(n, f))
+
+    def act(out, a, fu, r, w, n, bias=None, scale=None, dur=None):
+        k = {}
+        if bias is not None:
+            k["bias"] = bias
+        if scale is not None:
+            k["scale"] = scale
+        return op("s", lambda g: g.scalar.activation(out, a, fu, **k), r, w, dur or (FX + 0.02 + max(64, n) * CY))
+
+    def aff(out, a, scale, bias, r, w, n):
+        return act(out, a, AF.Identity, r, w, n, bias=bias, scale=scale)
+
+    def mm(out, l, rh, st, sp, r, w, cyc):
+        return op("p", lambda g: g.tensor.matmul(out, l, rh, st, sp), r, w, cyc * 0.6e-3)
+
+    def pair(out, la, lb, rh, r, w):
+        def fn(g):
+            g.tensor.matmul(out, la, rh, True, False)
+            return g.tensor.matmul(out, lb, rh, False, True)
+        return op("p", fn, r, w, 128 * 0.6e-3, free=True)
+
+    def iota(out, pat, base, cmul, w, n, fl=True):
+        if fl:
+            fn = lambda g: g.iota(out, pat, base, cmul, allow_small_or_imprecise_dtypes=True)
+        else:
+            fn = lambda g: g.iota(out, pat, base, cmul)
+        return op("g", fn, [], w, 0.13 + 2 * n * CY)
+
+    bw = [0.0]
+
+    def dma(out, a, r, w, nbytes, queued=False):
+        s = "dm%d" % nd[0]
+        nd[0] += 1
+        t = nbytes / BWL
+        if queued:
+            bw[0] += t
+            t = bw[0]
+        return op("y", lambda g: g.sync.dma_start(out, a), r, w, 0.08, lat=1.8 + t, sem=s, val=16,
+                  chain="load" if queued else None)
+
+    dst = T.cores[(rank - 1) % len(T.cores)]
+    rid, pid, _se = topo.addr(dst)
+    mask = topo.mask(core, dst)
+    neng = len(topo.engines(core, dst))
+
+    def remote(out, a, r, land, nbytes):
+        k = nr[0]
+        nr[0] += 1
+        ls, ar = "ls%d" % k, "ar%d" % k
+        i = op("g", lambda g: g.remote_dma(out, a, T.sem[ar], T.sem[ls], pid, rid, mask), r, [], 0.25,
+               lat=RL0 + nbytes / 80e3, sem=ls, val=neng, own=True)
+        op(None, None, [], [land], 0.0, lat=0.6, sem=ar, val=neng, after=[i])
+        return i
+
+    def gv(n):
+        return 0.05 + n * GA * CY
+
+    def gs(n):
+        return 0.065 + n * GA * CY
+
+    def sc(n):
+        return 0.05 + n * SC * CY
+
+    DG = T.DW[:, J:J + WX]
+    NG = T.NW[:, J:J + WX]
+    parts = ["blk"] + ["own%d" % i for i in range(len(NCH) - 1)]
+    Do = ["D" + x for x in parts[1:]]
+    No = ["N" + x for x in parts[1:]]
+    Dr = Do + ["Dblk", "Ddum"]
+    Nr = No + ["Nblk", "Ndum"]
+    AB = [T.AB0, T.AB1]
+    A16 = [T.A160, T.A161]
+    P1 = [T.P10, T.P11, T.P12]
+
+    dma(T.pthI[:], T.pth[:], [], ["pthI"], 49152, True)
+    dma(T.fvS[:], T.fv[:], [], ["fv"], 24576, True)
+    cw = O // DETCH
+    for i in range(DETCH):
+        dma(T.detI[:, i * cw:(i + 1) * cw], T.det[:, i * cw:(i + 1) * cw], [], ["detI%d" % i], 512 * cw, True)
+    for (a, b, e), nme in zip(NCH, parts):
+        dma(T.DW[:, J + a:J + b], T.dn[:, a:b], [], ["D" + nme], 256 * (b - a), True)
+
+    bo[0] = CB
+    K = T.K
+    pf, pm, grp, i117, i118, i15 = (K[:, i:i + 1] for i in range(6))
+    iota(T.pI[:, 0:1], [[0, 1]], 0, 1, ["pI"], 1, False)
+    iota(T.c[:], [[1, 128]], 0, 0, ["c"], 128)
+    iota(T.xc[:], [[0, 8], [1, 16]], 0, 0, ["xc"], 128)
+    iota(T.I4[:, 0:18], [[48, 2], [16, 3], [96, 3]], 0, 0, ["I4a"], 18)
+    iota(T.I2[:], [[1, 13], [0, 8]], 104, 0, ["I2"], 104)
+    iota(T.I3[:], [[16, 13], [1, 8]], 0, 0, ["I3"], 104)
+    iota(T.hi[:], [[1, 16], [0, 16]], 0, 0, ["hi"], 256)
+    iota(T.I4[:, 20:29], [[-4096, 3], [256, 3]], 0, 0, ["I4b"], 9)
+    cp(pf, T.pI[:, 0:1], ["pI"], ["pf"], 1)
+    ts(T.pI[:, 1:2], T.pI[:, 0:1], 15, None, A.bitwise_and, None, ["pI"], ["pI1"], 1)
+    cp(pm, T.pI[:, 1:2], ["pI1"], ["pm"], 1)
+    ts(grp, pf, pm, 0.0625, A.subtract, A.mult, ["pf", "pm"], ["grp"], 1)
+    ts(i117, pf, 117.0, None, A.is_equal, None, ["pf"], ["i117"], 1)
+    ts(i118, pf, 118.0, None, A.is_equal, None, ["pf"], ["i118"], 1)
+    ts(i15, pm, 15.0, None, A.is_equal, None, ["pm"], ["i15"], 1)
+    ts(T.cw[:, 432:480], T.c[:, 0:48], 512.0, i15, A.add, A.mult, ["c", "i15"], ["cv0"], 48)
+    ts(T.cv[:], T.cw[:, 432:480], float(W), None, A.add, None, ["cv0"], ["cv"], 48)
+    ts(K[:, 6:7], pm, 48.0, 4624.0, A.mult, A.add, ["pm"], ["k6"], 1)
+    aff(T.detF[:, O:O + 48], T.c[:, 0:48], None, K[:, 6:7], ["c", "k6"], ["detFx"], 48)
+    iota(T.NW[:, J + W:J + WX], [[0, 560]], 0, 0, ["Ndum"], 560)
+    iota(T.DW[:, J + W:J + WX], [[0, 560]], 0, 0, ["Ddum"], 560)
+    for b in range(3):
+        iota(T.G[:, 16 * b:16 * b + 16, 192:208], [[0, 16], [0, 16]], 0, 0, ["G%d" % j for j in range(16 * b, 16 * b + 16)], 256)
+        iota(T.G[:, 16 * b:16 * b + 16, 209:240:2], [[0, 16], [0, 16]], 0, 0, ["Gs%d" % j for j in range(16 * b, 16 * b + 16)], 256)
+    for t in range(ST - 1):
+        ms(T["SO%d" % t][:], 0, ["SO%d" % t], 16)
+    cp(T.Fl[:], T.c[:, 0:96], ["c"], ["Fl"], 96)
+    ts(T.SFl[:], T.I4[:, 0:18], pm, None, A.add, None, ["I4a", "pm"], ["SFl"], 18)
+    ts(T.ind[:, 0:8], T.c[:, 0:8], grp, None, A.is_equal, None, ["c", "grp"], ["ind0"], 8)
+    aff(T.ind[:, 8:16], T.ind[:, 0:8], -1.0, None, ["ind0"], ["ind1"], 8)
+    for b in range(3):
+        aff(K[:, 7 + b:8 + b], i118, 16.0 * b, i117, ["i117", "i118"], ["k7%d" % b], 1)
+        aff(T.X[:, 128 * b:128 * b + 128], T.xc[:], i118, K[:, 7 + b:8 + b], ["xc", "i118", "k7%d" % b], ["X%d" % b], 128)
+    ts(T.t1[:], T.c[:], -1.0, pf, A.add, A.is_equal, ["c", "pf"], ["t1"], 128)
+    aff(T.cb[:, 0:104], T.t1[:, 1:105], 256.0, None, ["t1"], ["cb0"], 104)
+    ts(T.cb[:, 104:208], T.I2[:], pf, -256.0, A.is_equal, A.mult, ["I2", "pf"], ["cb1"], 104)
+    tt(T.cb[:, 0:104], T.cb[:, 0:104], T.cb[:, 104:208], A.add, ["cb0", "cb1"], ["cb0"], 104)
+    aff(T.cb[:, 208:312], T.I3[:], i117, None, ["I3", "i117"], ["cb2"], 104)
+    tt(T.Comb[:, 1:105], T.cb[:, 0:104], T.cb[:, 208:312], A.add, ["cb0", "cb2"], ["Cm0"], 104)
+    aff(K[:, 10:11], i118, -256.0, None, ["i118"], ["k10"], 1)
+    aff(T.Comb[:, 113:217], T.cb[:, 0:104], None, K[:, 10:11], ["cb0", "k10"], ["Cm1"], 104)
+    aff(T.Comb[:, 0:1], i117, -16.0, None, ["i117"], ["Cm2"], 1)
+    aff(T.Comb[:, 112:113], i117, -256.0, K[:, 10:11], ["i117", "k10"], ["Cm3"], 1)
+    Cm = ["Cm0", "Cm1", "Cm2", "Cm3"]
+    ts(T.Tm[:, 0:256], T.hi[:], pm, None, A.is_equal, None, ["hi", "pm"], ["Tm0"], 256)
+    ts(K[:, 11:12], pm, -1.0, None, A.add, None, ["pm"], ["k11"], 1)
+    ts(T.Tm[:, 256:384], T.xc[:], 2.0, pm, A.mult, A.is_equal, ["xc", "pm"], ["Tm10"], 128)
+    ts(T.Tm[:, 512:640], T.xc[:], 2.0, K[:, 11:12], A.mult, A.is_equal, ["xc", "k11"], ["Tm20"], 128)
+    act(T.Tm[:, 384:512], T.Tm[:, 256:384], AF.Copy, ["Tm10"], ["Tm11"], 128)
+    act(T.Tm[:, 640:768], T.Tm[:, 512:640], AF.Copy, ["Tm20"], ["Tm21"], 128)
+    Tmr = ["Tm0", "Tm10", "Tm11", "Tm20", "Tm21"]
+    ts(T.ident[:], T.c[:], pf, None, A.is_equal, None, ["c", "pf"], ["ident"], 128)
+    aff(T.idF[:, 0:128], T.ident[:], None, None, ["ident"], ["idF0"], 128)
+    aff(T.idF[:, 128:256], T.ident[:], -1.0, None, ["ident"], ["idF1"], 128)
+    aff(T.idS[:, 0:128], T.ident[:], 16384.0, None, ["ident"], ["idS0"], 128)
+    aff(T.idS[:, 128:256], T.ident[:], -O / 2, None, ["ident"], ["idS1"], 128)
+    for t in range(ST):
+        aff(T.idS[:, 256 + 128 * t:384 + 128 * t], T.ident[:], -16384.0 - (rank + t) % len(T.cores) * S / 2, None, ["ident"],
+            ["idS%d" % (2 + t)], 128)
+    aff(T.one[:], T.c[:, 0:48], 0.0, 1.0, ["c"], ["one"], 48)
+    ts(T.bd[:], T.hi[:, 0:128], grp, None, A.is_equal, None, ["hi", "grp"], ["bd"], 128)
+    ts(T.qm[:, 0:96], T.xc[:, 0:96], pm, 8192.0, A.is_ge, A.mult, ["xc", "pm"], ["qm0"], 96)
+    ts(T.qm[:, 96:192], T.xc[:, 0:96], pm, 8192.0, A.not_equal, A.mult, ["xc", "pm"], ["qm1"], 96)
+    ts(T.rs[:], T.xc[:, 0:96], 0.0, 65536.0, A.is_equal, A.mult, ["xc"], ["rs"], 96)
+    tt(T.t2[:], T.t1[:], T.ident[:], A.subtract, ["t1", "ident"], ["t2"], 128)
+    ts(T.t3[:], T.xc[:], 1.0, 0.5, A.is_ge, A.mult, ["xc"], ["t3"], 128)
+    tt(T.Sh[:], T.t2[:], T.t3[:], A.mult, ["t2", "t3"], ["Sh"], 128)
+    aff(K[:, 12:13], pm, -256.0, None, ["pm"], ["k12"], 1)
+    aff(T.MC[:, 0:9], T.I4[:, 20:29], None, K[:, 12:13], ["I4b", "k12"], ["MC"], 9)
+    aff(T.ny[:, 9:12], T.c[:, 0:3], 16.0, pm, ["c", "pm"], ["fl"], 3)
+    ts(T.IL[:, 0:9:3], T.ny[:, 9:12], 768.0, None, A.add, None, ["fl"], ["ILc"], 3)
+    for ty, base in enumerate((5120.0, 4624.0, 4672.0)):
+        ts(T.dum[:, ty:9:3], T.ny[:, 9:12], base, None, A.add, None, ["fl"], ["dum%d" % ty], 3)
+    dumr = ["dum0", "dum1", "dum2"]
+
+    bo[0] = 0.0
+    cp(T.Py[:], T.pthI[:], ["pthI"], ["Py"], 96)
+    ts(T.pw[:, 0:96], T.Py[:], 0.0, EMPTY + 1.0, A.is_lt, A.mult, ["Py"], ["pw0"], 96)
+    tt(T.Pf[:], T.Py[:], T.pw[:, 0:96], A.add, ["Py", "pw0"], ["P0", "P1"], 96)
+    for i in range(DETCH):
+        cp(T.detF[:, i * cw:(i + 1) * cw], T.detI[:, i * cw:(i + 1) * cw], ["detI%d" % i], ["detF%d" % i], cw)
+    detr = ["detF%d" % i for i in range(DETCH)] + ["detFx"]
+    for (a, b, e), nme in zip(NCH, parts):
+        if e == "s":
+            act(T.NW[:, J + a:J + b], T.DW[:, J + a:J + b], AF.Relu, ["D" + nme], ["N" + nme], b - a, scale=-1.0)
+        else:
+            ts(T.NW[:, J + a:J + b], T.DW[:, J + a:J + b], -1.0, 0.0, A.mult, A.max, ["D" + nme], ["N" + nme], b - a, 0.5)
+    act(T.fpm[:, 0:96], T.fvS[:], AF.Copy, ["fv"], ["fp0"], 96, scale=-1.0)
+    act(T.fpm[:, 96:192], T.fvS[:], AF.Copy, ["fv"], ["fp1"], 96)
+    act(T.fpm[:, 192:288], T.fvS[:], AF.Copy, ["fv"], ["fp2"], 96)
+    bo[0] = 15.0
+    act(T.SF[:], T.fpm[:, 0:288].indirect(T.SFl[:, 0:18]), AF.Copy, ["fp0", "fp1", "fp2", "SFl"], ["SF"], 0, dur=gs(288))
+    bo[0] = 0.0
+    for q in range(6):
+        act(T.F16[:, 256 * q:256 * q + 256], T.fvS[:, 0:96].indirect(T.Fl[:, 16 * q:16 * q + 16]), AF.Copy, ["fv", "Fl"],
+            ["F16%d" % q], 0, dur=gs(256))
+
+    def lists(t):
+        m = t % 2
+        B = (rank + t) % len(T.cores)
+        p = T.Pf[:, 48 * m:48 * m + 48]
+        col = AB[m][:, 768:816]
+        sg = [T.sg[:, 144 * m + 48 * i:144 * m + 48 * i + 48] for i in range(3)]
+        n = ["sg%d%d" % (m, i) for i in range(3)]
+        pn = "P%d" % m
+        act(sg[0], p, AF.Sign, [pn], [n[0]], 48, bias=0.5 - O)
+        act(sg[1], p, AF.Sign, [pn], [n[1]], 48, bias=0.5 - O - B * S)
+        q, hi_, lo_ = T.PA[:, 288:336], T.idS[:, 0:128], T.idS[:, 256 + 128 * t:384 + 128 * t]
+        mm(q, T.idF[:, 0:128], p, True, False, ["idF0", pn], ["ps:PA"], 256)
+        mm(q, hi_, T.one[:], False, False, ["idS0", "one"], ["ps:PA"], 64)
+        mm(q, lo_, T.one[:], False, False, ["idS%d" % (2 + t), "one"], ["ps:PA"], 64)
+        mm(q, hi_, sg[0], False, False, ["idS0", n[0]], ["ps:PA"], 64)
+        mm(q, lo_, sg[1], False, True, ["idS%d" % (2 + t), n[1]], ["ps:PA"], 64)
+        tt(col, q, T.cv[:], A.min, ["ps:PA", "cv"], ["col%d" % m], 48, 1.0)
+        act(sg[2], col, AF.Sign, ["col%d" % m], [n[2]], 48, bias=0.5 - O)
+        q = T.PA[:, 336:384]
+        mm(q, T.idF[:, 0:128], col, True, False, ["idF0", "col%d" % m], ["ps:PA"], 256)
+        mm(q, T.idS[:, 128:256], T.one[:], False, False, ["idS1", "one"], ["ps:PA"], 64)
+        mm(q, T.idS[:, 128:256], sg[2], False, True, ["idS1", n[2]], ["ps:PA"], 64)
+        cp(T.site16[:, 48 * m:48 * m + 48], q, ["ps:PA"], ["site%d" % m], 48)
+        cp(T.col16[:, 48 * m:48 * m + 48], col, ["col%d" % m], ["c16%d" % m], 48)
+        for b in range(3):
+            src = T.detF[:, 0:O + 48].indirect(T.site16[:, 48 * m + 16 * b:48 * m + 16 * b + 16])
+            act(AB[m][:, 256 * b:256 * b + 256], src, AF.Copy, detr + ["site%d" % m], ["AB%d%d" % (m, b)], 0, dur=gs(256))
+            if t == 0 and b == 0:
+                cp(A16[m][:, 256 * b:256 * b + 256], src, detr + ["site%d" % m], ["A16%d%d" % (m, b)], 0, dur=gv(256))
+            else:
+                cp(A16[m][:, 256 * b:256 * b + 256], AB[m][:, 256 * b:256 * b + 256], ["AB%d%d" % (m, b)], ["A16%d%d" % (m, b)], 256)
+
+    lists(0)
+    lists(1)
+
+    for t in range(ST):
+        m = t % 2
+        B = (rank + t) % len(T.cores)
+        R = 12 + t // 2
+        NP = 8 * R + 1
+        last = t == ST - 1
+        SV, SO = T["SV%d" % t], T["SO%d" % t]
+        MK, selb, mR, sd, cm = (T[x + str(m)] for x in ("MK", "sel", "mR", "sd", "cm"))
+        if not last:
+            remote(T["L%d" % t][:], T.DW[:, J + O:J + W], ["Dblk"] + (Do if t == 0 else []), "L%d" % t, 256 * S)
+        ABr = ["AB%d%d" % (m, b) for b in range(3)] + ["col%d" % m]
+        for gi, (b0, b1) in enumerate(GROUPS):
+            bo[0] = BOOST
+            tt(T.tmp[:, 256 * b0:256 * b1], DG.indirect(T.col16[:, 48 * m + 16 * b0:48 * m + 16 * b1]),
+               T.F16[:, 768 * m + 256 * b0:768 * m + 256 * b1], A.min,
+               Dr + ["c16%d" % m] + ["F16%d" % (3 * m + b) for b in range(b0, b1)], ["tmp%d" % gi], 0, dur=gv(256 * (b1 - b0)))
+            onv = [(j % 16 < NV[t][j // 16]) if j // 16 == 1 else (j % 16 >= 16 - NV[t][j // 16]) for j in range(48)]
+            j0 = 16 * b0
+            for j in range(j0 + 1, 16 * b1 + 1):
+                if j == 16 * b1 or onv[j] != onv[j0]:
+                    ts(T.G[:, j0:j, 208:240:2], T.tmp[:, 16 * j0:16 * j], 0.0, -1.0 if onv[j0] else 1.0, A.max, A.mult, ["tmp%d" % gi],
+                       ["Gs%d" % i for i in range(j0, j)], 16 * (j - j0), 0.5)
+                    j0 = j
+            for b in range(b0, b1):
+                f0 = 16 * b
+                for x in range(16):
+                    j = f0 + x
+                    src = NG.indirect(A16[m][:, 16 * j:16 * j + R])
+                    f = T.fvS[:, 48 * m + j:48 * m + j + 1]
+                    rr = Nr + ["A16%d%d" % (m, b), "fv"]
+                    if onv[j]:
+                        ts(T.G[:, j, 0:16 * R], src, f, 0.0, A.subtract, A.min, rr, ["G%d" % j], 0, dur=gv(16 * R))
+                        rh, rn = T.ind[:, 8:16], "ind1"
+                    else:
+                        act(T.G[:, j, 0:16 * R], src, AF.Relu, rr, ["G%d" % j], 0, bias=f, scale=-1.0, dur=gs(16 * R))
+                        rh, rn = T.ind[:, 0:8], "ind0"
+                    ops[-1]["chain"] = ops[-1]["eng"]
+                    ops[-1]["boost"] = 0.0
+                    pair(P1[b][0:117, x:128:16], T.G[:, j, 0:234:2], T.G[:, j, 1:234:2], rh, ["G%d" % j, "Gs%d" % j, rn], ["ps:P1%d" % b])
+                act(T.X[0:117, 128 * b:128 * b + 128], P1[b][0:117, 0:128], AF.Copy, ["ps:P1%d" % b], ["X%d" % b], 128)
+                Xb = T.X[0:119, 128 * b:128 * b + 128]
+                P2, p2 = (T.P2, "ps:P2") if b % 2 == 0 else (T.P3, "ps:P3")
+                mm(P2[:, 0:NP], Xb, T.Comb[0:119, 0:NP], True, True, ["X%d" % b] + Cm, [p2], NP)
+                mm(P2[:, 128:128 + NP], Xb, T.Comb[0:119, 112:112 + NP], True, True, ["X%d" % b] + Cm, [p2], NP)
+                m1, m2 = T.M[:, 4 * b:4 * b + 1], T.M[:, 4 * b + 1:4 * b + 2]
+                red(m1, P2[:, 0:NP], A.min, [p2], ["m1%d" % b], NP)
+                red(m2, P2[:, 128:128 + NP], A.min, [p2], ["m2%d" % b], NP)
+                mr = ["m1%d" % b, "m2%d" % b]
+                ts(T.ML[:, 3 * b:3 * b + 3], T.MC[:, 3 * b:3 * b + 3], m1, m2, A.add, A.subtract, mr + ["MC"], ["ML%d" % b], 3)
+                for h in (1, 2):
+                    ts(T.IL[:, 3 * b + h:3 * b + h + 1], m1, m2, 0.0625, A.subtract, A.mult, mr, ["IL%d%d" % (b, h)], 1)
+            bs = range(b0, b1)
+            c0, c1, n0, n1 = 3 * b0, 3 * b1, 48 * b0, 48 * b1
+            n = n1 - n0
+            mk, sn = "MK%d%d" % (m, gi), "sel%d%d" % (m, gi)
+            act(MK[:, n0:n1], T.Tm[:, 0:768].indirect(T.ML[:, c0:c1]), AF.Copy, Tmr + ["ML%d" % b for b in bs], [mk], 0, dur=gs(n))
+            sel = selb[:, n0:n1]
+            tt(sel, AB[m][:, 0:816].indirect(T.IL[:, c0:c1]), MK[:, n0:n1], A.mult,
+               ABr + ["ILc", mk] + ["IL%d%d" % (b, h) for b in bs for h in (1, 2)], [sn], 0, dur=gv(n))
+            qo = (0, 48, 192)[b0]
+            mm(T.QD[:, 0:n], T.ident[:], T.qm[:, 96:96 + n], True, False, ["ident", "qm1"], ["ps:QD"], max(64, n))
+            mm(T.QQ[:, qo:qo + n], T.ident[:], T.qm[:, 0:n], True, False, ["ident", "qm0"], ["ps:QQ"], max(64, n))
+            mm(T.QD[:, 0:n], T.bd[:], sel, False, True, ["bd", sn], ["ps:QD"], 4 * max(64, n))
+            mm(T.QQ[:, qo:qo + n], T.bd[:], sel, False, True, ["bd", sn], ["ps:QQ"], 4 * max(64, n))
+            if b0 < 2:
+                mm(T.QQ[:, 96 + n0:96 + n1], T.bd[:], sel, True, True, ["bd", sn], ["ps:QQ"], 4 * max(64, n))
+            nmr = ["nm%d" % gi]
+            scan(T.nm[:, n0:n1], T.rs[:, 0:n], T.QD[:, 0:n], ["rs", "ps:QD"], nmr, n)
+            nm = T.nm[:, n0 + 15:n1:16]
+            cp(T.RL[:, c0:c1], nm, nmr, ["RL%d" % gi], 3)
+            act(T.Dg[:, n0:n1], DG.indirect(T.RL[:, c0:c1]), AF.Copy, Dr + ["RL%d" % gi], ["Dg%d" % gi], 0, dur=gs(n))
+            for b in bs:
+                lo, hi = ((0, 48), (48, 144), (96, 240))[b]
+                k, e0 = hi - lo, (0, 144, 432)[b]
+                for ty in range(3):
+                    x = T.nm[:, 48 * b + 16 * ty + 15:48 * b + 16 * ty + 16]
+                    if NES[b]:
+                        act(T.NE[:, e0 + k * ty:e0 + k * ty + k], T.QQ[:, lo:hi], AF.Sign, ["ps:QQ"] + nmr, ["NE%d%d" % (b, ty)], k,
+                            bias=x, scale=-1.0)
+                    else:
+                        ts(T.NE[:, e0 + k * ty:e0 + k * ty + k], T.QQ[:, lo:hi], x, None, A.not_equal, None, ["ps:QQ"] + nmr,
+                           ["NE%d%d" % (b, ty)], k)
+            tt(SV[:, n0:n1], T.Dg[:, n0:n1], T.SF[:, 144 * m + n0:144 * m + n1], A.add, ["Dg%d" % gi, "SF"], ["SVd%d%d" % (t, gi)], n)
+            dd = T.dd[:, c0:c1]
+            if not last:
+                act(SV[:, 144 + n0:144 + n1], SV[:, n0:n1], AF.Relu, ["SVd%d%d" % (t, gi)], ["SVn%d%d" % (t, gi)], n, scale=-1.0)
+                ts(T.ny[:, c0:c1], nm, float(O), float(J), A.is_lt, A.mult, nmr, ["ny%d" % gi], 3)
+                tt(T.nd[:, c0:c1], nm, T.dum[:, c0:c1], A.subtract, nmr + dumr, ["nd%d" % gi], 3)
+                tt(dd, T.nd[:, c0:c1], T.ny[:, c0:c1], A.add, ["nd%d" % gi, "ny%d" % gi], ["dd%d" % gi], 3)
+            else:
+                tt(dd, nm, T.dum[:, c0:c1], A.subtract, nmr + dumr, ["dd%d" % gi], 3)
+            for b in bs:
+                k, e0 = 144 * (b + 1), (0, 144, 432)[b]
+                s = T.M[:, 4 * b + 2:4 * b + 3]
+                red(s, T.NE[:, e0:e0 + k], A.min, ["NE%d%d" % (b, ty) for ty in range(3)], ["s%d" % b], k, True)
+                ts(sd[:, 3 * b:3 * b + 3], T.dd[:, 3 * b:3 * b + 3], s, None, A.mult, None, ["s%d" % b, "dd%d" % gi], ["sd%d%d" % (m, b)], 3)
+            bo[0] = 0.0
+            for b in bs:
+                act(mR[:, 16 * b:16 * b + 16], MK[:, 48 * b:48 * b + 16], AF.Copy, [mk], ["mR%d%d" % (m, b)], 16)
+        sdr = ["sd%d%d" % (m, b) for b in range(3)]
+        tt(T.fo[:, 0:9], sd[:, 0:9], T.dum[:, 0:9], A.add, sdr + dumr, ["fo"], 9)
+        cp(SO[:, 0:9], T.fo[:, 0:9], ["fo"], ["SO%d" % t], 9)
+        ts(cm[:, 0:3], sd[:, 0:9:3], 0.0, None, A.not_equal, None, sdr, ["cm%d" % m], 3)
+        SOr = ["SO%d" % t]
+        SVd = ["SVd%d%d" % (t, gi) for gi in range(len(GROUPS))]
+        SVn = ["SVn%d%d" % (t, gi) for gi in range(len(GROUPS))]
+        selr = ["sel%d%d" % (m, gi) for gi in range(len(GROUPS))]
+        if not last:
+            remote(T["RV%d" % t][:], SV[:], SVd + SVn, "RV%d" % t, 128 * 576)
+            sent = remote(T["RO%d" % t][:], SO[:], SOr, "RO%d" % t, 128 * 32)
+            L, RV, RO = T["L%d" % t], T["RV%d" % t], T["RO%d" % t]
+            dma(T.DW[:, J + O:J + W], L[:], ["L%d" % t], ["Dblk"], 256 * S)
+            ops[-1]["after"] = [sent]
+            for q in range(4):
+                out, src, w = T.NW[:, J + O + 512 * q:J + O + 512 * q + 512], L[:, 512 * q:512 * q + 512], ["Nblk" + (str(q) if q else "")]
+                if NQ[q] == "s":
+                    act(out, src, AF.Relu, ["L%d" % t], w, 512, scale=-1.0)
+                else:
+                    ts(out, src, -1.0, 0.0, A.mult, A.max, ["L%d" % t], w, 512, 0.5)
+                if q:
+                    ops[-1]["after"] = [len(ops) - 1 - q]
+            nb = ["Nblk1", "Nblk2", "Nblk3"]
+            cp(T.NW[:, 0:J + O].indirect(SO[:, 0:9]), SV[:, 144:288], SOr + SVn, No, 0, dur=sc(144))
+            cp(T.DW[:, 0:J + O].indirect(SO[:, 0:9]), SV[:, 0:144], SOr + SVd, Do, 0, dur=sc(144))
+            cp(T.NW[:, J:WD].indirect(RO[:, 0:9]), RV[:, 144:288], ["RO%d" % t, "RV%d" % t], Nr + nb, 0, dur=sc(144))
+            cp(T.DW[:, J:WD].indirect(RO[:, 0:9]), RV[:, 0:144], ["RO%d" % t, "RV%d" % t], Dr, 0, dur=sc(144))
+        else:
+            cp(DG.indirect(SO[:, 0:9]), SV[:, 0:144], SOr + SVd, Dr, 0, dur=sc(144))
+            dma(T.yd[:], T.DW[:, J:J + W], Dr, [], 256 * W)
+        p = T.Pf[:, 48 * m:48 * m + 48]
+        pn = "P%d" % m
+        act(T.ne[:], p, AF.Sign, [pn], ["ne"], 48, bias=EMPTY / 2, scale=-1.0)
+        mm(T.PA[:, 96:144], T.Sh[:], T.ne[:], True, True, ["Sh", "ne"], ["ps:PA"], 64)
+        for b in range(3):
+            for ty in (1, 2):
+                o = 48 * (ty - 1) + 16 * b
+                mm(T.PA[:, o:o + 16], T.bd[:], selb[:, 48 * b + 16 * ty:48 * b + 16 * ty + 16], True, True, ["bd"] + selr, ["ps:PA"], 256)
+        act(T.cB[:], T.c[:, 0:16].indirect(cm[:, 0:3]), AF.Copy, ["c", "cm%d" % m], ["cB"], 0, dur=gs(48))
+        pw = T.pw
+        ts(T.yb[:], T.PA[:, 0:96], float(O), float(B * S), A.is_ge, A.mult, ["ps:PA"], ["yb"], 96)
+        tt(pw[:, 336:384], T.PA[:, 96:144], T.cB[:], A.mult, ["ps:PA", "cB"], ["pw5"], 48, 1.0)
+        tt(pw[:, 288:336], mR[:], T.cB[:], A.mult, ["mR%d%d" % (m, b) for b in range(3)] + ["cB"], ["pw4"], 48)
+        mm(T.PA[:, 144:240], T.ident[:], T.yb[:], True, False, ["ident", "yb"], ["ps:PA"], 96)
+        for b in range(3):
+            for ty in (1, 2):
+                o = 144 + 48 * (ty - 1) + 16 * b
+                mm(T.PA[:, o:o + 16], T.bd[:], selb[:, 48 * b + 16 * ty:48 * b + 16 * ty + 16], False, False, ["bd"] + selr, ["ps:PA"], 256)
+        for h in range(2):
+            mm(T.PA[:, 144 + 48 * h:192 + 48 * h], T.idF[:, 128:256], p, False, h == 1, ["idF1", pn], ["ps:PA"], 256)
+        tt(pw[:, 384:480], T.PA[:, 144:240], pw[:, 288:384], A.mult, ["ps:PA", "pw4", "pw5"], ["pw6"], 96, 1.0)
+        mm(T.PA[:, 240:288], T.idF[:, 0:128], p, True, False, ["idF0", pn], ["ps:PA"], 256)
+        for h in range(2):
+            mm(T.PA[:, 240:288], T.idF[:, 0:128], pw[:, 384 + 48 * h:432 + 48 * h], False, h == 1, ["idF0", "pw6"], ["ps:PA"], 256)
+        act(p, T.PA[:, 240:288], AF.Copy, ["ps:PA"], [pn], 48)
+        if t + 2 < ST:
+            lists(t + 2)
+        else:
+            y = T.cw[:, 192 * m:192 * m + 48]
+            ts(y, p, EMPTY / 2, -EMPTY - 1.0, A.is_ge, A.mult, [pn], ["cw%d0" % m], 48)
+            tt(T.Py[:, 48 * m:48 * m + 48], p, y, A.add, [pn, "cw%d0" % m, "Py"], ["Py%d" % m], 48)
+            dma(T.yp[:, 48 * m:48 * m + 48], T.Py[:, 48 * m:48 * m + 48], ["Py%d" % m], [], 128 * 192)
+    return ops
+
+
+def depend(ops):
+    lw, rd, ps, ch = {}, {}, {}, {}
+    for i, o in enumerate(ops):
+        hard, soft = set(), set()
+        if o.get("chain"):
+            if o["chain"] in ch:
+                soft.add(ch[o["chain"]])
+            ch[o["chain"]] = i
+        for a in o["after"]:
+            (soft if o["eng"] is None else hard).add(a)
+        for x in o["r"] + o["w"]:
+            if x.startswith("ps:"):
+                prev, cur = ps.get(x, ([], []))
+                if cur and ops[cur[-1]]["eng"] != o["eng"]:
+                    prev, cur = cur, []
+                hard.update(prev)
+                if cur and o["eng"] == "p" and not o.get("free"):
+                    soft.add(cur[-1])
+                ps[x] = (prev, cur + [i])
+        for x in o["r"]:
+            if not x.startswith("ps:") and x in lw:
+                hard.add(lw[x])
+        for x in o["w"]:
+            if not x.startswith("ps:"):
+                if x in lw:
+                    hard.add(lw[x])
+                hard.update(rd.get(x, []))
+        for x in o["r"]:
+            if not x.startswith("ps:"):
+                rd.setdefault(x, []).append(i)
+        for x in o["w"]:
+            if not x.startswith("ps:"):
+                lw[x] = i
+                rd[x] = []
+        hard.discard(i)
+        o["hard"], o["soft"] = sorted(hard), sorted(soft - hard)
+
+
+def kind(o):
+    if o.get("chain"):
+        return None
+    n = (o["w"] + o["r"])[0]
+    a = n.rstrip("0123456789")
+    d = n[len(a):]
+    if a in ("NE", "IL"):
+        d = d[:1]
+    elif a in ("SO", "SVd", "SVn", "sd", "sel", "MK", "nm", "m", "s", "ML", "RL", "fo", "dd", "ny", "nd", "Dg", "X", "tmp", "AB", "A", "Nown", "Down"):
+        d = d[-1:]
+    else:
+        d = ""
+    return (o["eng"] or "x") + a + d
+
+
+def schedule(ops):
+    n = len(ops)
+    succ = [[] for _ in range(n)]
+    for i, o in enumerate(ops):
+        for k in o["hard"] + o["soft"]:
+            succ[k].append(i)
+    pr = [0.0] * n
+    for i in range(n - 1, -1, -1):
+        pr[i] = ops[i]["dur"] + ops[i]["lat"] + HOP + max([pr[k] for k in succ[i]], default=0.0)
+    pr = [pr[i] + ops[i]["boost"] + PRI.get(kind(ops[i]), 0.0) for i in range(n)]
+    left = [len(o["hard"]) + len(o["soft"]) for o in ops]
+    rdy = [0.0] * n
+    st = [0.0] * n
+    free = {}
+    cand = {}
+    order = []
+
+    def place(i, t0):
+        o = ops[i]
+        st[i] = t0
+        order.append(i)
+        end = t0 + o["dur"] + o["lat"]
+        for k in succ[i]:
+            if i in ops[k]["soft"] and ops[k]["eng"] is not None:
+                rdy[k] = max(rdy[k], t0)
+            else:
+                rdy[k] = max(rdy[k], end + HOP)
+            left[k] -= 1
+            if left[k] == 0:
+                enter(k)
+
+    def enter(i):
+        if ops[i]["eng"] is None:
+            place(i, rdy[i])
+        else:
+            cand.setdefault(ops[i]["eng"], []).append(i)
+
+    for i in range(n):
+        if left[i] == 0:
+            enter(i)
+    while any(cand.values()):
+        best = None
+        for e, c in cand.items():
+            if not c:
+                continue
+            now = max(free.get(e, 0.0), min(rdy[i] for i in c))
+            pick = max((i for i in c if rdy[i] <= now), key=lambda i: (pr[i], -i))
+            for i in c:
+                if rdy[i] > now and pr[i] > pr[pick] + 0.3 and rdy[i] - now < 0.5 * ops[pick]["dur"]:
+                    pick = i
+            t0 = max(now, rdy[pick])
+            if best is None or t0 < best[0]:
+                best = (t0, e, pick)
+        t0, e, pick = best
+        cand[e].remove(pick)
+        free[e] = t0 + ops[pick]["dur"]
+        place(pick, t0)
+    return order, st
+
+
+def emit(g, T, ops, order):
+    q = {"v": g.vector, "s": g.scalar, "p": g.tensor, "g": g, "y": g.sync}
+    cnt = {}
+    clock = {e: {} for e in q}
+    done = {}
+    for i in order:
+        o = ops[i]
+        e = o["eng"]
+        if e is None:
+            cnt[o["sem"]] = o["val"]
+            done[i] = (o["sem"], o["val"], {o["sem"]: o["val"]})
+            continue
+        ck = clock[e]
+        need = {}
+        for k in o["hard"]:
+            s, v, _c = done[k]
+            if ck.get(s, 0) < v and (s not in need or need[s][0] < v):
+                need[s] = (v, k)
+        for s, (v, k) in sorted(need.items(), key=lambda z: -z[1][1]):
+            if ck.get(s, 0) >= v:
+                continue
+            q[e].wait_ge(T.sem[s], v)
+            for s2, v2 in done[k][2].items():
+                if ck.get(s2, 0) < v2:
+                    ck[s2] = v2
+        ins = o["fn"](g)
+        s = o["sem"] or "q" + e
+        cnt[s] = cnt.get(s, 0) + o["val"]
+        if not o.get("own"):
+            ins.then_inc(T.sem[s], o["val"])
+        c = dict(ck)
+        c[s] = cnt[s]
+        done[i] = (s, cnt[s], c)
+    for s, v in cnt.items():
+        if max(clock[e].get(s, 0) for e in q) < v:
+            g.wait_ge(T.sem[s], v)
+
+
+def rank_program(g, core, T, topo):
+    rank = T.rank_of(core)
+    if rank is None:
+        return
+    ops = build(T, rank, topo, core)
+    depend(ops)
+    order, _st = schedule(ops)
+    emit(g, T, ops, order)

@@ -1,51 +1,61 @@
+import numpy as np
 from concourse.mybir import AluOpType as A, AxisListType as AX, ActivationFunctionType as AF
 
 O, S, W, FB, ST = 2560, 2048, 4608, 48, 4
-WX = 5168
-J = WX
-WD = J + WX + O
+LO = 160
+AL = 2432
+J = LO + 2 * AL
+WX = W + 16
+WB = (ST - 1) * (J + WX) + J - LO + O - WX
+NSEND = False
+PASSES = 2
+TRIES = 300
+URGE = (0.0, 0.25, 0.5, 1.0, 2.0)
+KEPT = {}
+CO = O - 0.5
 EMPTY = float(1 << 16)
-NV = [[8, 8, 6], [7, 8, 5], [7, 8, 5], [7, 8, 6]]
-GROUPS = [(0, 2), (2, 3)]
-NES = [True, True, True]
-NQ = "sssv"
+KS = 32768.0
+RC = 1.5 * 2.0 ** 38
+NV = [[7, 7, 5]] * ST
+NQ = "ssss"
 DETCH = 4
 NCH = [(O, W, "s"), (0, 1024, "v"), (1024, 2048, "v"), (2048, O, "v")]
+GROUPS = [dict(bs=(0, 1), c0=0, c1=6, d0=4, f0=0, v0=0, k0=96), dict(bs=(2,), c0=6, c1=9, d0=6, f0=192, v0=48, k0=0)]
+LCOL = [slice(0, 5, 2), slice(1, 6, 2), slice(6, 9)]
 
-SCRATCH = {"G": ("sbuf", [128, 48, 240], "bfloat16")}
+SCRATCH = {"G": ("sbuf", [128, 48, 208], "bfloat16")}
 for _dt, _bufs in (
-        ("bfloat16", dict(DW=WD, NW=WD, fvS=96, fpm=288, F16=1536, SF=288, tmp=768, X=384, Comb=224, Tm=768, ident=128, Sh=128, t1=128,
-                          t2=128, t3=128, ind=16, qm=192, NE=864, Dg=144, idS=768, one=48, sg=288, yb=96, ne=48, SV0=288, SV1=288,
-                          SV2=288, SV3=288, L0=S, L1=S, L2=S, RV0=288, RV1=288, RV2=288)),
-        ("float32", dict(detF=O + 48, Pf=96, Py=96, cw=480, cb=320, K=16, c=128, xc=128, hi=256, I2=104, I3=104, I4=32, bd=128, cv=48,
-                         dum=12, MC=12, M=12, nm=144, rs=96, fo=12, ny=12, nd=12, dd=12, idF=256, cB=48, pw=480, AB0=816, AB1=816,
-                         MK0=144, MK1=144, sel0=144, sel1=144, mR0=48, mR1=48, sd0=12, sd1=12)),
-        ("int32", dict(detI=O, pthI=96, pI=2)),
-        ("uint16", dict(col16=96, site16=96, IL=12, ML=12, RL=12, Fl=96, SFl=18, A160=768, A161=768, cm0=4, cm1=4, SO0=16, SO1=16,
-                        SO2=16, SO3=16, RO0=16, RO1=16, RO2=16))):
+        ("bfloat16", dict(D0=WX, N0=W, DB=WB, NB=WB, fvS=96, F16=1536, tmp=768, Gs=768, X=128, Ex=104, Tm=512, Z=288,
+                          ident=256, Sh=128, t1=128, t2=128, t3=128, ind=8, qm=384, E=768, Dg=144, idS=768, one=48, sg=288, ne=96,
+                          bdH=512, MK=144, sn=96, SV0=288, SV1=288, SV2=288, SV3=288, RV0=288, RV1=288, RV2=288)),
+        ("float32", dict(detF=O + 48, Pf=96, Py=96, cw=480, K=24, c=144, xc=128, x3=384, hi=256, I2=104, I4=32, bd=512, cv=48, KT=336,
+                         dum=12, MC=12, C3=4, M=4, r3=12, nm=144, rs=288, CF=288, S2=288, idF=256, cB=48, pw=192, AB0=768, AB1=768,
+                         col=96, colD=288, selL=144, selA0=144, selA1=144, yb=48, mN=96)),
+        ("int32", dict(detI=O, pthI=96, pI=4)),
+        ("uint16", dict(col16=96, site16=96, IL=12, ML0=12, ML1=12, RL=12, CL=12, A160=768, A161=768, cm=4))):
     for _n, _w in _bufs.items():
         SCRATCH[_n] = ("sbuf", [128, _w], _dt)
-for _n in ("P10", "P11", "P12", "P2", "QQ", "QD", "PA", "P3"):
+for _t in range(ST):
+    for _g in range(2):
+        SCRATCH["SO%d%d" % (_t, _g)] = ("sbuf", [128, 16], "uint16")
+        if _t < ST - 1:
+            SCRATCH["RO%d%d" % (_t, _g)] = ("sbuf", [128, 16], "uint16")
+for _n in ("P0", "P1", "P2", "Q0", "Q1", "F0", "F1", "PA"):
     SCRATCH[_n] = ("psum", [128, 512], "float32")
 
-SEMAPHORES = (["qv", "qs", "qp", "qg"] + ["dm%d" % i for i in range(24)] + ["ls%d" % i for i in range(9)]
-              + ["ar%d" % i for i in range(9)])
+SEMAPHORES = (["qv", "qs", "qp", "qg"] + ["dm%d" % i for i in range(24)] + ["ls%d" % i for i in range(18)]
+              + ["ar%d" % i for i in range(18)])
 
 CY = 1.04e-3
-HOP = 0.06
-BOOST = 8.0
-CB = 16.0
+PC = 0.55e-3
+HOP = 0.16
+FX = 0.0
 BWL = 250e3
-FX = 0.03
 GA = 1.56
 SC = 3.8
 RL0 = 1.2
-PRI = {'sAB0': -8, 'sAB2': -11, 'vnd0': -17, 'vsel1': 48, 'gc': 22, 'gpI': 28, 'vNblk': -8, 'sne': 4.0, 'sidF': -31.0, 'vNown0': 25.0,
-       'vRL0': 55.0, 'vNown2': 27.0, 'gNdum': -13.0, 'vML1': -7.0, 'vIL1': -8.0, 'sF': 7.0, 'gxc': -25.0, 'gI4b': -18.0, 'vsd1': -17.0,
-       'sMK1': 44.0, 'vIL0': 23.0, 'vSVd0': -9.0, 'sX0': -6.0, 'sCm': -8.0, 'gGs': -37.0, 'gI': 32.0, 'sNE1': 11.0, 'vdetF': 9.0,
-       'vgrp': -61.0, 'sAB1': -5.0, 'vsd2': -17.0, 'vPy': -18.0, 'vt': -8.0, 'sX1': 18.0, 'sk': 21.0, 'vTm': 71.0, 'vm0': -7.0,
-       'vsd0': -9.0, 'vFl': -50.0, 'sNE0': 9.0, 'vsite': 11.0, 'vdum': -34.0, 'vnm1': 23.0, 'vpf': 29.0, 'vpm': -13.0, 'vdd1': -4.0,
-       'vML2': 22.0, 'vdd0': 5.0, 'vnm0': 16.0, 'vA2': 15.0, 'sNE2': -5.0, 'vGs': -3.0, 'vm2': 16.0, 'vpw': -7.0, 'vyb': -2.0, 'vs1': 12.0}
+BOOST = 8.0
+CB = 16.0
 
 
 def build(T, rank, topo, core):
@@ -76,8 +86,8 @@ def build(T, rank, topo, core):
     def cp(out, a, r, w, n, f=1.0, dur=None):
         return op("v", lambda g: g.vector.tensor_copy(out, a), r, w, dur or small(n, f))
 
-    def red(out, a, o, r, w, n, ab=False):
-        return op("v", lambda g: g.vector.tensor_reduce(out, a, AX.X, o, apply_absolute_value=ab), r, w, small(n))
+    def red(out, a, r, w, n):
+        return op("v", lambda g: g.vector.tensor_reduce(out, a, AX.X, A.min), r, w, small(n))
 
     def scan(out, a, b, r, w, n):
         return op("v", lambda g: g.vector.tensor_tensor_scan(out, a, b, 0.0, A.add, A.min), r, w, small(n))
@@ -91,19 +101,22 @@ def build(T, rank, topo, core):
             k["bias"] = bias
         if scale is not None:
             k["scale"] = scale
-        return op("s", lambda g: g.scalar.activation(out, a, fu, **k), r, w, dur or (FX + 0.02 + max(64, n) * CY))
+        return op("s", lambda g: g.scalar.activation(out, a, fu, **k), r, w, dur or small(n))
 
     def aff(out, a, scale, bias, r, w, n):
         return act(out, a, AF.Identity, r, w, n, bias=bias, scale=scale)
 
     def mm(out, l, rh, st, sp, r, w, cyc):
-        return op("p", lambda g: g.tensor.matmul(out, l, rh, st, sp), r, w, cyc * 0.6e-3)
+        return op("p", lambda g: g.tensor.matmul(out, l, rh, st, sp), r, w, cyc * PC)
 
-    def pair(out, la, lb, rh, r, w):
+    def acc(parts, key, r, w, cyc):
+        flag = [False]
+
         def fn(g):
-            g.tensor.matmul(out, la, rh, True, False)
-            return g.tensor.matmul(out, lb, rh, False, True)
-        return op("p", fn, r, w, 128 * 0.6e-3, free=True)
+            for i, (out, l, rh) in enumerate(parts):
+                ins = g.tensor.matmul(out, l, rh, False, flag[0] and i == len(parts) - 1)
+            return ins
+        return op("p", fn, r, w, cyc * PC, free=True, group=key, flag=flag)
 
     def iota(out, pat, base, cmul, w, n, fl=True):
         if fl:
@@ -147,135 +160,147 @@ def build(T, rank, topo, core):
     def sc(n):
         return 0.05 + n * SC * CY
 
-    DG = T.DW[:, J:J + WX]
-    NG = T.NW[:, J:J + WX]
-    parts = ["blk"] + ["own%d" % i for i in range(len(NCH) - 1)]
-    Do = ["D" + x for x in parts[1:]]
-    No = ["N" + x for x in parts[1:]]
-    Dr = Do + ["Dblk", "Ddum"]
-    Nr = No + ["Nblk", "Ndum"]
+    def dw(t, a, b):
+        return T.D0[:, a:b] if t == 0 else T.DB[:, t * (J + WX) - WX + a:t * (J + WX) - WX + b]
+
+    def nw(t, a, b):
+        return T.N0[:, a:b] if t == 0 else T.NB[:, t * (J + WX) - WX + a:t * (J + WX) - WX + b]
+
+    nown = len(NCH) - 1
+    Do = [["D0o%d" % i for i in range(nown)]] + [["D%do" % t] for t in range(1, ST)]
+    No = [["N0o%d" % i for i in range(nown)]] + [["N%do" % t] for t in range(1, ST)]
+    Nb = [["N%db%d" % (t, q) for q in range(1 if NSEND else 4)] for t in range(ST)]
+    Dr = [Do[t] + ["D%db" % t, "D%dz" % t] for t in range(ST)]
+    Nr = [No[t] + Nb[t] for t in range(ST)]
     AB = [T.AB0, T.AB1]
     A16 = [T.A160, T.A161]
-    P1 = [T.P10, T.P11, T.P12]
+    PK = [T.P0, T.P1, T.P2]
 
     dma(T.pthI[:], T.pth[:], [], ["pthI"], 49152, True)
     dma(T.fvS[:], T.fv[:], [], ["fv"], 24576, True)
     cw = O // DETCH
     for i in range(DETCH):
         dma(T.detI[:, i * cw:(i + 1) * cw], T.det[:, i * cw:(i + 1) * cw], [], ["detI%d" % i], 512 * cw, True)
-    for (a, b, e), nme in zip(NCH, parts):
-        dma(T.DW[:, J + a:J + b], T.dn[:, a:b], [], ["D" + nme], 256 * (b - a), True)
+    for (a, b, e), nme in zip(NCH, ["D0b"] + Do[0]):
+        dma(T.D0[:, a:b], T.dn[:, a:b], [], [nme], 256 * (b - a), True)
 
     bo[0] = CB
     K = T.K
-    pf, pm, grp, i117, i118, i15 = (K[:, i:i + 1] for i in range(6))
+    pf, pm, grp, i15, pe, po, ph, kz, k6, k12, k13, k15 = (K[:, i:i + 1] for i in range(12))
     iota(T.pI[:, 0:1], [[0, 1]], 0, 1, ["pI"], 1, False)
-    iota(T.c[:], [[1, 128]], 0, 0, ["c"], 128)
+    iota(T.c[:], [[1, 144]], 0, 0, ["c"], 144)
     iota(T.xc[:], [[0, 8], [1, 16]], 0, 0, ["xc"], 128)
-    iota(T.I4[:, 0:18], [[48, 2], [16, 3], [96, 3]], 0, 0, ["I4a"], 18)
-    iota(T.I2[:], [[1, 13], [0, 8]], 104, 0, ["I2"], 104)
-    iota(T.I3[:], [[16, 13], [1, 8]], 0, 0, ["I3"], 104)
     iota(T.hi[:], [[1, 16], [0, 16]], 0, 0, ["hi"], 256)
-    iota(T.I4[:, 20:29], [[-4096, 3], [256, 3]], 0, 0, ["I4b"], 9)
+    iota(T.I4[:, 0:6], [[0, 3], [16, 2]], 0, 0, ["I4a"], 6)
+    iota(T.I4[:, 6:10], [[0, 4]], 32, 0, ["I4b"], 4)
+    iota(T.I4[:, 12:21], [[-4096, 3], [0, 3]], 0, 0, ["I4c"], 9)
+    iota(T.I2[:], [[1, 13], [0, 8]], 0, 0, ["I2"], 104)
+    iota(T.KT[:], [[4096, 3], [16, 14], [1, 8]], 0, 0, ["KT"], 336)
+    iota(T.KT[:, 104:336:112], [[4096, 3]], 240 - int(KS), 0, ["KT"], 3)
+    iota(T.x3[:], [[0, 8], [1, 16], [0, 3]], 0, 0, ["x3"], 384)
+    for t in range(ST):
+        iota(dw(t, W, WX), [[0, 16]], 0, 0, ["D%dz" % t], 16)
     cp(pf, T.pI[:, 0:1], ["pI"], ["pf"], 1)
     ts(T.pI[:, 1:2], T.pI[:, 0:1], 15, None, A.bitwise_and, None, ["pI"], ["pI1"], 1)
+    ts(T.pI[:, 2:3], T.pI[:, 0:1], 1, None, A.bitwise_and, None, ["pI"], ["pI2"], 1)
     cp(pm, T.pI[:, 1:2], ["pI1"], ["pm"], 1)
+    cp(po, T.pI[:, 2:3], ["pI2"], ["po"], 1)
+    aff(pe, po, -1.0, 1.0, ["po"], ["pe"], 1)
+    ts(ph, pm, po, 0.5, A.subtract, A.mult, ["pm", "po"], ["ph"], 1)
     ts(grp, pf, pm, 0.0625, A.subtract, A.mult, ["pf", "pm"], ["grp"], 1)
-    ts(i117, pf, 117.0, None, A.is_equal, None, ["pf"], ["i117"], 1)
-    ts(i118, pf, 118.0, None, A.is_equal, None, ["pf"], ["i118"], 1)
     ts(i15, pm, 15.0, None, A.is_equal, None, ["pm"], ["i15"], 1)
+    aff(kz, grp, 16.0, 15.0, ["grp"], ["kz"], 1)
     ts(T.cw[:, 432:480], T.c[:, 0:48], 512.0, i15, A.add, A.mult, ["c", "i15"], ["cv0"], 48)
-    ts(T.cv[:], T.cw[:, 432:480], float(W), None, A.add, None, ["cv0"], ["cv"], 48)
-    ts(K[:, 6:7], pm, 48.0, 4624.0, A.mult, A.add, ["pm"], ["k6"], 1)
-    aff(T.detF[:, O:O + 48], T.c[:, 0:48], None, K[:, 6:7], ["c", "k6"], ["detFx"], 48)
-    iota(T.NW[:, J + W:J + WX], [[0, 560]], 0, 0, ["Ndum"], 560)
-    iota(T.DW[:, J + W:J + WX], [[0, 560]], 0, 0, ["Ddum"], 560)
-    for b in range(3):
-        iota(T.G[:, 16 * b:16 * b + 16, 192:208], [[0, 16], [0, 16]], 0, 0, ["G%d" % j for j in range(16 * b, 16 * b + 16)], 256)
-        iota(T.G[:, 16 * b:16 * b + 16, 209:240:2], [[0, 16], [0, 16]], 0, 0, ["Gs%d" % j for j in range(16 * b, 16 * b + 16)], 256)
+    aff(T.cv[:], T.cw[:, 432:480], None, W - CO, ["cv0"], ["cv"], 48)
+    aff(k6, pm, 48.0, 4624.0, ["pm"], ["k6"], 1)
+    aff(T.detF[:, O:O + 48], T.c[:, 0:48], None, k6, ["c", "k6"], ["detFx"], 48)
     for t in range(ST - 1):
-        ms(T["SO%d" % t][:], 0, ["SO%d" % t], 16)
-    cp(T.Fl[:], T.c[:, 0:96], ["c"], ["Fl"], 96)
-    ts(T.SFl[:], T.I4[:, 0:18], pm, None, A.add, None, ["I4a", "pm"], ["SFl"], 18)
-    ts(T.ind[:, 0:8], T.c[:, 0:8], grp, None, A.is_equal, None, ["c", "grp"], ["ind0"], 8)
-    aff(T.ind[:, 8:16], T.ind[:, 0:8], -1.0, None, ["ind0"], ["ind1"], 8)
-    for b in range(3):
-        aff(K[:, 7 + b:8 + b], i118, 16.0 * b, i117, ["i117", "i118"], ["k7%d" % b], 1)
-        aff(T.X[:, 128 * b:128 * b + 128], T.xc[:], i118, K[:, 7 + b:8 + b], ["xc", "i118", "k7%d" % b], ["X%d" % b], 128)
-    ts(T.t1[:], T.c[:], -1.0, pf, A.add, A.is_equal, ["c", "pf"], ["t1"], 128)
-    aff(T.cb[:, 0:104], T.t1[:, 1:105], 256.0, None, ["t1"], ["cb0"], 104)
-    ts(T.cb[:, 104:208], T.I2[:], pf, -256.0, A.is_equal, A.mult, ["I2", "pf"], ["cb1"], 104)
-    tt(T.cb[:, 0:104], T.cb[:, 0:104], T.cb[:, 104:208], A.add, ["cb0", "cb1"], ["cb0"], 104)
-    aff(T.cb[:, 208:312], T.I3[:], i117, None, ["I3", "i117"], ["cb2"], 104)
-    tt(T.Comb[:, 1:105], T.cb[:, 0:104], T.cb[:, 208:312], A.add, ["cb0", "cb2"], ["Cm0"], 104)
-    aff(K[:, 10:11], i118, -256.0, None, ["i118"], ["k10"], 1)
-    aff(T.Comb[:, 113:217], T.cb[:, 0:104], None, K[:, 10:11], ["cb0", "k10"], ["Cm1"], 104)
-    aff(T.Comb[:, 0:1], i117, -16.0, None, ["i117"], ["Cm2"], 1)
-    aff(T.Comb[:, 112:113], i117, -256.0, K[:, 10:11], ["i117", "k10"], ["Cm3"], 1)
-    Cm = ["Cm0", "Cm1", "Cm2", "Cm3"]
-    ts(T.Tm[:, 0:256], T.hi[:], pm, None, A.is_equal, None, ["hi", "pm"], ["Tm0"], 256)
-    ts(K[:, 11:12], pm, -1.0, None, A.add, None, ["pm"], ["k11"], 1)
-    ts(T.Tm[:, 256:384], T.xc[:], 2.0, pm, A.mult, A.is_equal, ["xc", "pm"], ["Tm10"], 128)
-    ts(T.Tm[:, 512:640], T.xc[:], 2.0, K[:, 11:12], A.mult, A.is_equal, ["xc", "k11"], ["Tm20"], 128)
-    act(T.Tm[:, 384:512], T.Tm[:, 256:384], AF.Copy, ["Tm10"], ["Tm11"], 128)
-    act(T.Tm[:, 640:768], T.Tm[:, 512:640], AF.Copy, ["Tm20"], ["Tm21"], 128)
-    Tmr = ["Tm0", "Tm10", "Tm11", "Tm20", "Tm21"]
-    ts(T.ident[:], T.c[:], pf, None, A.is_equal, None, ["c", "pf"], ["ident"], 128)
-    aff(T.idF[:, 0:128], T.ident[:], None, None, ["ident"], ["idF0"], 128)
-    aff(T.idF[:, 128:256], T.ident[:], -1.0, None, ["ident"], ["idF1"], 128)
-    aff(T.idS[:, 0:128], T.ident[:], 16384.0, None, ["ident"], ["idS0"], 128)
-    aff(T.idS[:, 128:256], T.ident[:], -O / 2, None, ["ident"], ["idS1"], 128)
+        for gi in range(2):
+            ms(T["SO%d%d" % (t, gi)][:], 0, ["SO%d%d%d" % (t, gi, i) for i in range(6)], 16)
+    ts(T.CL[:, 0:10], T.I4[:, 0:10], pm, None, A.add, None, ["I4a", "I4b", "pm"], ["CL"], 10)
+    ts(T.ind[:], T.c[:, 0:8], grp, None, A.is_equal, None, ["c", "grp"], ["ind"], 8)
+    ts(T.Z[:, 0:144], T.c[:], kz, KS, A.is_equal, A.mult, ["c", "kz"], ["Z0"], 144)
+    aff(T.Z[:, 144:288], T.Z[:, 0:144], -1.0, None, ["Z0"], ["Z1"], 144)
+    ts(T.Ex[:], T.I2[:], pm, -KS, A.is_equal, A.mult, ["I2", "pm"], ["Ex"], 104)
+    aff(k13, pm, 256.0, None, ["pm"], ["k13"], 1)
+    aff(T.KT[:], T.KT[:], None, k13, ["KT", "k13"], ["KT"], 336)
+    ts(T.Tm[:, 0:256], T.hi[:], pm, None, A.is_equal, None, ["hi", "pm"], ["TmR"], 256)
+    ts(T.Tm[:, 256:384], T.xc[:], ph, None, A.is_equal, None, ["xc", "ph"], ["TmK0"], 128)
+    act(T.Tm[:, 384:512], T.Tm[:, 256:384], AF.Copy, ["TmK0"], ["TmK1"], 128)
+    TmR, TmK = T.Tm[:, 0:256], T.Tm[:, 256:512]
+    idp, idn = T.ident[:, 0:128], T.ident[:, 128:256]
+    ts(idp, T.c[:, 0:128], pf, None, A.is_equal, None, ["c", "pf"], ["idp"], 128)
+    aff(idn, idp, -1.0, None, ["idp"], ["idn"], 128)
+    aff(T.idF[:, 0:128], idp, None, None, ["idp"], ["idF0"], 128)
+    aff(T.idF[:, 128:256], idp, -1.0, None, ["idp"], ["idF1"], 128)
+    aff(T.idS[:, 0:128], idp, 16384.0, None, ["idp"], ["idS0"], 128)
+    aff(T.idS[:, 128:256], idp, -O / 2, None, ["idp"], ["idS1"], 128)
     for t in range(ST):
-        aff(T.idS[:, 256 + 128 * t:384 + 128 * t], T.ident[:], -16384.0 - (rank + t) % len(T.cores) * S / 2, None, ["ident"],
+        aff(T.idS[:, 256 + 128 * t:384 + 128 * t], idp, -16384.0 - (rank + t) % len(T.cores) * S / 2, None, ["idp"],
             ["idS%d" % (2 + t)], 128)
     aff(T.one[:], T.c[:, 0:48], 0.0, 1.0, ["c"], ["one"], 48)
-    ts(T.bd[:], T.hi[:, 0:128], grp, None, A.is_equal, None, ["hi", "grp"], ["bd"], 128)
-    ts(T.qm[:, 0:96], T.xc[:, 0:96], pm, 8192.0, A.is_ge, A.mult, ["xc", "pm"], ["qm0"], 96)
-    ts(T.qm[:, 96:192], T.xc[:, 0:96], pm, 8192.0, A.not_equal, A.mult, ["xc", "pm"], ["qm1"], 96)
-    ts(T.rs[:], T.xc[:, 0:96], 0.0, 65536.0, A.is_equal, A.mult, ["xc"], ["rs"], 96)
-    tt(T.t2[:], T.t1[:], T.ident[:], A.subtract, ["t1", "ident"], ["t2"], 128)
+    bd = [T.bd[:, 128 * i:128 * i + 128] for i in range(4)]
+    bdH = [T.bdH[:, 128 * i:128 * i + 128] for i in range(4)]
+    ts(bd[0], T.hi[:, 0:128], grp, None, A.is_equal, None, ["hi", "grp"], ["bd0"], 128)
+    aff(bd[1], bd[0], pe, None, ["bd0", "pe"], ["bd1"], 128)
+    aff(bd[2], bd[0], po, None, ["bd0", "po"], ["bd2"], 128)
+    aff(k15, i15, -16.0, None, ["i15"], ["k15"], 1)
+    aff(bd[3], bd[0], k15, None, ["bd0", "k15"], ["bd3"], 128)
+    for i in range(3):
+        aff(bdH[i], bd[i], -float(AL), None, ["bd%d" % i], ["bdH%d" % i], 128)
+    aff(bdH[3], bd[0], -KS, None, ["bd0"], ["bdH3"], 128)
+    ms(T.qm[:], 0.0, ["qm"], 384, 0.5)
+    for u in (0, 3, 7):
+        ts(T.qm[:, 48 * u:48 * u + 48], T.x3[:, 0:48], pm, 16384.0, A.is_le, A.mult, ["x3", "pm"], ["qm"], 48)
+    ts(T.qm[:, 192:288], T.x3[:, 0:96], pm, 16384.0, A.not_equal, A.mult, ["x3", "pm"], ["qm"], 96)
+    ms(T.rs[:], 0.0, ["rs"], 288)
+    for sl in (slice(0, 96, 16), slice(96, 240, 48), slice(240, 288, 16)):
+        ms(T.rs[:, sl], 2.0 ** 25, ["rs"], 8)
+    for a, b, src, nme, cst in ((0, 96, T.xc, "xc", CO + LO + AL), (96, 240, T.x3, "x3", 16384.0), (240, 288, T.xc, "xc", CO + LO + AL)):
+        ts(T.CF[:, a:b], src[:, 0:b - a], pm, 2.0 ** 22, A.not_equal, A.mult, [nme, "pm"], ["CF%d" % a], b - a)
+        aff(T.CF[:, a:b], T.CF[:, a:b], None, cst, ["CF%d" % a], ["CF%d" % a], b - a)
+    ts(T.t1[:], T.c[:, 0:128], -1.0, pf, A.add, A.is_equal, ["c", "pf"], ["t1"], 128)
+    tt(T.t2[:], T.t1[:], idp, A.subtract, ["t1", "idp"], ["t2"], 128)
     ts(T.t3[:], T.xc[:], 1.0, 0.5, A.is_ge, A.mult, ["xc"], ["t3"], 128)
     tt(T.Sh[:], T.t2[:], T.t3[:], A.mult, ["t2", "t3"], ["Sh"], 128)
-    aff(K[:, 12:13], pm, -256.0, None, ["pm"], ["k12"], 1)
-    aff(T.MC[:, 0:9], T.I4[:, 20:29], None, K[:, 12:13], ["I4b", "k12"], ["MC"], 9)
-    aff(T.ny[:, 9:12], T.c[:, 0:3], 16.0, pm, ["c", "pm"], ["fl"], 3)
-    ts(T.IL[:, 0:9:3], T.ny[:, 9:12], 768.0, None, A.add, None, ["fl"], ["ILc"], 3)
-    for ty, base in enumerate((5120.0, 4624.0, 4672.0)):
-        ts(T.dum[:, ty:9:3], T.ny[:, 9:12], base, None, A.add, None, ["fl"], ["dum%d" % ty], 3)
-    dumr = ["dum0", "dum1", "dum2"]
+    aff(k12, pm, -256.0, None, ["pm"], ["k12"], 1)
+    aff(T.MC[:, 0:9], T.I4[:, 12:21], None, k12, ["I4c", "k12"], ["MC"], 9)
+    ms(T.C3[:], RC, ["C3"], 4)
+    aff(T.dum[:, 0:9], T.c[:, 0:9], 16.0, pm, ["c", "pm"], ["dum"], 9)
 
     bo[0] = 0.0
-    cp(T.Py[:], T.pthI[:], ["pthI"], ["Py"], 96)
-    ts(T.pw[:, 0:96], T.Py[:], 0.0, EMPTY + 1.0, A.is_lt, A.mult, ["Py"], ["pw0"], 96)
-    tt(T.Pf[:], T.Py[:], T.pw[:, 0:96], A.add, ["Py", "pw0"], ["P0", "P1"], 96)
+    ts(T.pw[:, 0:96], T.pthI[:], 0.0, EMPTY + CO + 1.0, A.is_lt, A.mult, ["pthI"], ["pwA", "pwB"], 96)
+    ts(T.Py[:], T.pthI[:], -CO, None, A.add, None, ["pthI"], ["Py"], 96)
+    tt(T.Pf[:], T.Py[:], T.pw[:, 0:96], A.add, ["Py", "pwA", "pwB"], ["P0", "P1"], 96)
     for i in range(DETCH):
         cp(T.detF[:, i * cw:(i + 1) * cw], T.detI[:, i * cw:(i + 1) * cw], ["detI%d" % i], ["detF%d" % i], cw)
     detr = ["detF%d" % i for i in range(DETCH)] + ["detFx"]
-    for (a, b, e), nme in zip(NCH, parts):
+    for (a, b, e), dn_, nn in zip(NCH, [["D0b"]] + [[x] for x in Do[0]], [Nb[0]] + [[x] for x in No[0]]):
         if e == "s":
-            act(T.NW[:, J + a:J + b], T.DW[:, J + a:J + b], AF.Relu, ["D" + nme], ["N" + nme], b - a, scale=-1.0)
+            act(T.N0[:, a:b], T.D0[:, a:b], AF.Relu, dn_, nn, b - a, scale=-1.0)
         else:
-            ts(T.NW[:, J + a:J + b], T.DW[:, J + a:J + b], -1.0, 0.0, A.mult, A.max, ["D" + nme], ["N" + nme], b - a, 0.5)
-    act(T.fpm[:, 0:96], T.fvS[:], AF.Copy, ["fv"], ["fp0"], 96, scale=-1.0)
-    act(T.fpm[:, 96:192], T.fvS[:], AF.Copy, ["fv"], ["fp1"], 96)
-    act(T.fpm[:, 192:288], T.fvS[:], AF.Copy, ["fv"], ["fp2"], 96)
-    bo[0] = 15.0
-    act(T.SF[:], T.fpm[:, 0:288].indirect(T.SFl[:, 0:18]), AF.Copy, ["fp0", "fp1", "fp2", "SFl"], ["SF"], 0, dur=gs(288))
-    bo[0] = 0.0
-    for q in range(6):
-        act(T.F16[:, 256 * q:256 * q + 256], T.fvS[:, 0:96].indirect(T.Fl[:, 16 * q:16 * q + 16]), AF.Copy, ["fv", "Fl"],
-            ["F16%d" % q], 0, dur=gs(256))
+            ts(T.N0[:, a:b], T.D0[:, a:b], -1.0, 0.0, A.mult, A.max, dn_, nn, b - a, 0.5)
+    for r_ in range(16):
+        cp(T.F16[:, r_:1536:16], T.fvS[:], ["fv"], ["F16%d" % r_], 96, 0.5)
+    F16r = ["F16%d" % r_ for r_ in range(16)]
+
+    def first_empty(m):
+        p, pn = T.Pf[:, 48 * m:48 * m + 48], "P%d" % m
+        ne = T.ne[:, 48 * m:48 * m + 48]
+        act(ne, p, AF.Sign, [pn], ["ne%d" % m], 48, bias=EMPTY / 2, scale=-1.0)
+        mm(T.PA[:, 96:144], T.Sh[:], ne, True, True, ["Sh", "ne%d" % m], ["ps:PA"], 64)
+        act(T.mN[:, 48 * m:48 * m + 48], T.PA[:, 96:144], AF.Copy, ["ps:PA"], ["mN%d" % m], 48)
 
     def lists(t):
         m = t % 2
         B = (rank + t) % len(T.cores)
         p = T.Pf[:, 48 * m:48 * m + 48]
-        col = AB[m][:, 768:816]
+        col = T.col[:, 48 * m:48 * m + 48]
         sg = [T.sg[:, 144 * m + 48 * i:144 * m + 48 * i + 48] for i in range(3)]
         n = ["sg%d%d" % (m, i) for i in range(3)]
         pn = "P%d" % m
-        act(sg[0], p, AF.Sign, [pn], [n[0]], 48, bias=0.5 - O)
-        act(sg[1], p, AF.Sign, [pn], [n[1]], 48, bias=0.5 - O - B * S)
+        act(sg[0], p, AF.Sign, [pn], [n[0]], 48)
+        act(sg[1], p, AF.Sign, [pn], [n[1]], 48, bias=-float(B * S))
         q, hi_, lo_ = T.PA[:, 288:336], T.idS[:, 0:128], T.idS[:, 256 + 128 * t:384 + 128 * t]
         mm(q, T.idF[:, 0:128], p, True, False, ["idF0", pn], ["ps:PA"], 256)
         mm(q, hi_, T.one[:], False, False, ["idS0", "one"], ["ps:PA"], 64)
@@ -283,20 +308,23 @@ def build(T, rank, topo, core):
         mm(q, hi_, sg[0], False, False, ["idS0", n[0]], ["ps:PA"], 64)
         mm(q, lo_, sg[1], False, True, ["idS%d" % (2 + t), n[1]], ["ps:PA"], 64)
         tt(col, q, T.cv[:], A.min, ["ps:PA", "cv"], ["col%d" % m], 48, 1.0)
-        act(sg[2], col, AF.Sign, ["col%d" % m], [n[2]], 48, bias=0.5 - O)
+        act(sg[2], col, AF.Sign, ["col%d" % m], [n[2]], 48)
         q = T.PA[:, 336:384]
         mm(q, T.idF[:, 0:128], col, True, False, ["idF0", "col%d" % m], ["ps:PA"], 256)
         mm(q, T.idS[:, 128:256], T.one[:], False, False, ["idS1", "one"], ["ps:PA"], 64)
         mm(q, T.idS[:, 128:256], sg[2], False, True, ["idS1", n[2]], ["ps:PA"], 64)
-        cp(T.site16[:, 48 * m:48 * m + 48], q, ["ps:PA"], ["site%d" % m], 48)
-        cp(T.col16[:, 48 * m:48 * m + 48], col, ["col%d" % m], ["c16%d" % m], 48)
+        ts(T.site16[:, 48 * m:48 * m + 48], q, CO, None, A.add, None, ["ps:PA"], ["site%d" % m], 48)
+        ts(T.col16[:, 48 * m:48 * m + 48], col, CO, float(W), A.add, A.min, ["col%d" % m], ["c16%d" % m], 48)
         for b in range(3):
             src = T.detF[:, 0:O + 48].indirect(T.site16[:, 48 * m + 16 * b:48 * m + 16 * b + 16])
-            act(AB[m][:, 256 * b:256 * b + 256], src, AF.Copy, detr + ["site%d" % m], ["AB%d%d" % (m, b)], 0, dur=gs(256))
+            act(AB[m][:, 256 * b:256 * b + 256], src, AF.Identity, detr + ["site%d" % m], ["AB%d%d" % (m, b)], 0, bias=-CO, dur=gs(256))
             if t == 0 and b == 0:
                 cp(A16[m][:, 256 * b:256 * b + 256], src, detr + ["site%d" % m], ["A16%d%d" % (m, b)], 0, dur=gv(256))
             else:
-                cp(A16[m][:, 256 * b:256 * b + 256], AB[m][:, 256 * b:256 * b + 256], ["AB%d%d" % (m, b)], ["A16%d%d" % (m, b)], 256)
+                ts(A16[m][:, 256 * b:256 * b + 256], AB[m][:, 256 * b:256 * b + 256], CO, None, A.add, None, ["AB%d%d" % (m, b)],
+                   ["A16%d%d" % (m, b)], 256)
+        act(T.colD[:, 144 * m:144 * m + 144], col.indirect(T.CL[:, 0:9]), AF.Copy, ["col%d" % m, "CL"], ["colD%d" % m], 0, dur=gs(144))
+        first_empty(m)
 
     lists(0)
     lists(1)
@@ -305,162 +333,182 @@ def build(T, rank, topo, core):
         m = t % 2
         B = (rank + t) % len(T.cores)
         R = 12 + t // 2
-        NP = 8 * R + 1
         last = t == ST - 1
-        SV, SO = T["SV%d" % t], T["SO%d" % t]
-        MK, selb, mR, sd, cm = (T[x + str(m)] for x in ("MK", "sel", "mR", "sd", "cm"))
+        SV, ML, selA = T["SV%d" % t], T["ML%d" % m], T["selA%d" % m]
+        DG, NG = dw(t, 0, WX), nw(t, 0, W)
         if not last:
-            remote(T["L%d" % t][:], T.DW[:, J + O:J + W], ["Dblk"] + (Do if t == 0 else []), "L%d" % t, 256 * S)
-        ABr = ["AB%d%d" % (m, b) for b in range(3)] + ["col%d" % m]
-        for gi, (b0, b1) in enumerate(GROUPS):
-            bo[0] = BOOST
-            tt(T.tmp[:, 256 * b0:256 * b1], DG.indirect(T.col16[:, 48 * m + 16 * b0:48 * m + 16 * b1]),
-               T.F16[:, 768 * m + 256 * b0:768 * m + 256 * b1], A.min,
-               Dr + ["c16%d" % m] + ["F16%d" % (3 * m + b) for b in range(b0, b1)], ["tmp%d" % gi], 0, dur=gv(256 * (b1 - b0)))
-            onv = [(j % 16 < NV[t][j // 16]) if j // 16 == 1 else (j % 16 >= 16 - NV[t][j // 16]) for j in range(48)]
-            j0 = 16 * b0
-            for j in range(j0 + 1, 16 * b1 + 1):
-                if j == 16 * b1 or onv[j] != onv[j0]:
-                    ts(T.G[:, j0:j, 208:240:2], T.tmp[:, 16 * j0:16 * j], 0.0, -1.0 if onv[j0] else 1.0, A.max, A.mult, ["tmp%d" % gi],
-                       ["Gs%d" % i for i in range(j0, j)], 16 * (j - j0), 0.5)
-                    j0 = j
-            for b in range(b0, b1):
-                f0 = 16 * b
+            if NSEND:
+                remote(nw(t + 1, O, W), nw(t, O, W), Nb[t] + (Do[0] if t == 0 else []), Nb[t + 1][0], 256 * S)
+            remote(dw(t + 1, O, W), dw(t, O, W), ["D%db" % t] + (Do[0] if t == 0 else []), "D%db" % (t + 1), 256 * S * (1 + NSEND))
+            dma(nw(t + 1, 0, O), nw(t, 0, O), No[t], No[t + 1], 256 * O)
+            dma(dw(t + 1, 0, O), dw(t, 0, O), Do[t], Do[t + 1], 256 * O)
+            for q in range(0 if NSEND else 4):
+                out, src = nw(t + 1, O + 512 * q, O + 512 * q + 512), dw(t + 1, O + 512 * q, O + 512 * q + 512)
+                if NQ[q] == "s":
+                    act(out, src, AF.Relu, ["D%db" % (t + 1)], [Nb[t + 1][q]], 512, scale=-1.0)
+                else:
+                    ts(out, src, -1.0, 0.0, A.mult, A.max, ["D%db" % (t + 1)], [Nb[t + 1][q]], 512, 0.5)
+        bo[0] = BOOST
+        tt(T.tmp[:], DG.indirect(T.col16[:, 48 * m:48 * m + 48]), T.F16[:, 768 * m:768 * m + 768], A.min,
+           Dr[t] + ["c16%d" % m] + F16r, ["tmp"], 0, dur=gv(768))
+        ts(T.Gs[:], T.tmp[:], 0.0, None, A.max, None, ["tmp"], ["Gs"], 768, 0.5)
+        for b in range(3):
+            w_ = 32 if b < 2 else 16
+
+            def subs(g, b=b, w_=w_):
                 for x in range(16):
-                    j = f0 + x
+                    j = 16 * b + x
+                    ins = g.tensor.matmul(T.F1[32 * b:32 * b + w_, x:128:16], T.Gs[:, 16 * j:16 * j + w_], T.ind[:], True, True)
+                return ins
+            op("p", subs, ["Gs", "ind"], ["ps:F1"], 16 * 40 * PC)
+        act(T.X[0:80, :], T.F1[0:80, 0:128], AF.Copy, ["ps:F1"], ["X"], 128)
+        onv = [(j % 16 < NV[t][j // 16]) if j // 16 == 1 else (j % 16 >= 16 - NV[t][j // 16]) for j in range(48)]
+        for gi, gr in enumerate(GROUPS):
+            bs, c0, c1, d0 = gr["bs"], gr["c0"], gr["c1"], gr["d0"]
+            nb = len(bs)
+            for b in bs:
+                pk, key = "ps:P%d" % b, (t, b)
+                mm(PK[b][:, 0:112], T.idF[:, 0:128], T.KT[:, 112 * b:112 * b + 112], True, False, ["idF0", "KT"], [pk], 448)
+                acc([(PK[b][:, 0:8 * R], T.X[32 * b:32 * b + 16, :], T.Ex[32 * b:32 * b + 16, 0:8 * R])], key, ["X", "Ex"], [pk], 8 * R)
+                for x in range(16):
+                    j = 16 * b + x
                     src = NG.indirect(A16[m][:, 16 * j:16 * j + R])
                     f = T.fvS[:, 48 * m + j:48 * m + j + 1]
-                    rr = Nr + ["A16%d%d" % (m, b), "fv"]
+                    rr = Nr[t] + ["A16%d%d" % (m, b), "fv"]
                     if onv[j]:
                         ts(T.G[:, j, 0:16 * R], src, f, 0.0, A.subtract, A.min, rr, ["G%d" % j], 0, dur=gv(16 * R))
-                        rh, rn = T.ind[:, 8:16], "ind1"
                     else:
                         act(T.G[:, j, 0:16 * R], src, AF.Relu, rr, ["G%d" % j], 0, bias=f, scale=-1.0, dur=gs(16 * R))
-                        rh, rn = T.ind[:, 0:8], "ind0"
                     ops[-1]["chain"] = ops[-1]["eng"]
                     ops[-1]["boost"] = 0.0
-                    pair(P1[b][0:117, x:128:16], T.G[:, j, 0:234:2], T.G[:, j, 1:234:2], rh, ["G%d" % j, "Gs%d" % j, rn], ["ps:P1%d" % b])
-                act(T.X[0:117, 128 * b:128 * b + 128], P1[b][0:117, 0:128], AF.Copy, ["ps:P1%d" % b], ["X%d" % b], 128)
-                Xb = T.X[0:119, 128 * b:128 * b + 128]
-                P2, p2 = (T.P2, "ps:P2") if b % 2 == 0 else (T.P3, "ps:P3")
-                mm(P2[:, 0:NP], Xb, T.Comb[0:119, 0:NP], True, True, ["X%d" % b] + Cm, [p2], NP)
-                mm(P2[:, 128:128 + NP], Xb, T.Comb[0:119, 112:112 + NP], True, True, ["X%d" % b] + Cm, [p2], NP)
-                m1, m2 = T.M[:, 4 * b:4 * b + 1], T.M[:, 4 * b + 1:4 * b + 2]
-                red(m1, P2[:, 0:NP], A.min, [p2], ["m1%d" % b], NP)
-                red(m2, P2[:, 128:128 + NP], A.min, [p2], ["m2%d" % b], NP)
-                mr = ["m1%d" % b, "m2%d" % b]
-                ts(T.ML[:, 3 * b:3 * b + 3], T.MC[:, 3 * b:3 * b + 3], m1, m2, A.add, A.subtract, mr + ["MC"], ["ML%d" % b], 3)
-                for h in (1, 2):
-                    ts(T.IL[:, 3 * b + h:3 * b + h + 1], m1, m2, 0.0625, A.subtract, A.mult, mr, ["IL%d%d" % (b, h)], 1)
-            bs = range(b0, b1)
-            c0, c1, n0, n1 = 3 * b0, 3 * b1, 48 * b0, 48 * b1
-            n = n1 - n0
-            mk, sn = "MK%d%d" % (m, gi), "sel%d%d" % (m, gi)
-            act(MK[:, n0:n1], T.Tm[:, 0:768].indirect(T.ML[:, c0:c1]), AF.Copy, Tmr + ["ML%d" % b for b in bs], [mk], 0, dur=gs(n))
-            sel = selb[:, n0:n1]
-            tt(sel, AB[m][:, 0:816].indirect(T.IL[:, c0:c1]), MK[:, n0:n1], A.mult,
-               ABr + ["ILc", mk] + ["IL%d%d" % (b, h) for b in bs for h in (1, 2)], [sn], 0, dur=gv(n))
-            qo = (0, 48, 192)[b0]
-            mm(T.QD[:, 0:n], T.ident[:], T.qm[:, 96:96 + n], True, False, ["ident", "qm1"], ["ps:QD"], max(64, n))
-            mm(T.QQ[:, qo:qo + n], T.ident[:], T.qm[:, 0:n], True, False, ["ident", "qm0"], ["ps:QQ"], max(64, n))
-            mm(T.QD[:, 0:n], T.bd[:], sel, False, True, ["bd", sn], ["ps:QD"], 4 * max(64, n))
-            mm(T.QQ[:, qo:qo + n], T.bd[:], sel, False, True, ["bd", sn], ["ps:QQ"], 4 * max(64, n))
-            if b0 < 2:
-                mm(T.QQ[:, 96 + n0:96 + n1], T.bd[:], sel, True, True, ["bd", sn], ["ps:QQ"], 4 * max(64, n))
-            nmr = ["nm%d" % gi]
-            scan(T.nm[:, n0:n1], T.rs[:, 0:n], T.QD[:, 0:n], ["rs", "ps:QD"], nmr, n)
-            nm = T.nm[:, n0 + 15:n1:16]
-            cp(T.RL[:, c0:c1], nm, nmr, ["RL%d" % gi], 3)
-            act(T.Dg[:, n0:n1], DG.indirect(T.RL[:, c0:c1]), AF.Copy, Dr + ["RL%d" % gi], ["Dg%d" % gi], 0, dur=gs(n))
-            for b in bs:
-                lo, hi = ((0, 48), (48, 144), (96, 240))[b]
-                k, e0 = hi - lo, (0, 144, 432)[b]
-                for ty in range(3):
-                    x = T.nm[:, 48 * b + 16 * ty + 15:48 * b + 16 * ty + 16]
-                    if NES[b]:
-                        act(T.NE[:, e0 + k * ty:e0 + k * ty + k], T.QQ[:, lo:hi], AF.Sign, ["ps:QQ"] + nmr, ["NE%d%d" % (b, ty)], k,
-                            bias=x, scale=-1.0)
-                    else:
-                        ts(T.NE[:, e0 + k * ty:e0 + k * ty + k], T.QQ[:, lo:hi], x, None, A.not_equal, None, ["ps:QQ"] + nmr,
-                           ["NE%d%d" % (b, ty)], k)
-            tt(SV[:, n0:n1], T.Dg[:, n0:n1], T.SF[:, 144 * m + n0:144 * m + n1], A.add, ["Dg%d" % gi, "SF"], ["SVd%d%d" % (t, gi)], n)
-            dd = T.dd[:, c0:c1]
+                    z = T.Z[:, 144 * onv[j] + 15 - x:144 * onv[j] + 143 - x]
+                    acc([(PK[b][:, 0:8 * R], z, T.G[:, j, h:16 * R:2]) for h in range(2)], key, ["G%d" % j, "Z0", "Z1"], [pk], 16 * R)
+                mb, r3 = T.M[:, b:b + 1], T.r3[:, 3 * b:3 * b + 3]
+                red(mb, PK[b][:, 0:105], [pk], ["m%d" % b], 105)
+                ts(r3, T.C3[:, 0:3], mb, RC, A.add, A.subtract, ["C3", "m%d" % b], ["r%d" % b], 3)
+                ts(ML[:, LCOL[b]], T.MC[:, 3 * b:3 * b + 3], mb, T.r3[:, 3 * b:3 * b + 1], A.add, A.subtract,
+                   ["MC", "m%d" % b, "r%d" % b], ["ML%d%d" % (m, b)], 3)
+                ts(T.IL[:, LCOL[b]], r3, mb, -0.0625, A.subtract, A.mult, ["m%d" % b, "r%d" % b], ["IL%d" % b], 3)
+            n0, n1, n = 16 * c0, 16 * c1, 16 * (c1 - c0)
+            e0, e1 = 16 * d0, 16 * (d0 + nb)
+            h0, h1, hn = 48 * bs[0], 48 * (bs[-1] + 1), 48 * nb
+            MLr = ["ML%d%d" % (m, b) for b in bs]
+            sl, sa = "selL%d" % gi, "selA%d%d" % (m, gi)
+            Qp, Fp, qn, fn_ = T["Q%d" % gi], T["F%d" % gi], "ps:Q%d" % gi, "ps:F%d" % gi
+            act(T.MK[:, n0:n1], TmK.indirect(ML[:, c0:c1]), AF.Copy, ["TmK0", "TmK1"] + MLr, ["MK%d" % gi], 0, dur=gs(n))
+            tt(T.selL[:, n0:n1], TmR.indirect(ML[:, c0:c1]), T.colD[:, 144 * m + n0:144 * m + n1], A.mult,
+               ["TmR", "colD%d" % m] + MLr, [sl], 0, dur=gv(n))
+            tt(selA[:, n0:n1], AB[m][:, 0:768].indirect(T.IL[:, c0:c1]), T.MK[:, n0:n1], A.mult,
+               ["AB%d%d" % (m, b) for b in range(3)] + ["IL%d" % b for b in bs] + ["MK%d" % gi], [sa], 0, dur=gv(n))
+            srcs = [(T.selL, sl), (selA, sa), (selA, sa)]
+            mm(Qp[:, 0:3 * n], idp, T.qm[:, 3 * n0 - 48 * gi:3 * n1 - 48 * gi], True, False, ["idp", "qm"], [qn], 3 * n)
+            for ty, (s_, sn_) in enumerate(srcs):
+                mm(Qp[:, ty:3 * n:3], bd[ty], s_[:, n0:n1], False, ty == 2, ["bd%d" % ty, sn_], [qn], 4 * max(64, n))
+            u0 = 3 * (e0 - n0)
+            for ty in range(3):
+                scan(T.nm[:, h0 + 16 * nb * ty:h0 + 16 * nb * (ty + 1)], T.rs[:, 0:16 * nb], Qp[:, u0 + ty:u0 + hn:3], ["rs", qn],
+                     ["nm%d%d" % (gi, ty)], 16 * nb)
+            nmr = ["nm%d%d" % (gi, ty) for ty in range(3)]
+            l0 = 6 * gi
+            ts(T.RL[:, l0:l0 + 3 * nb], T.nm[:, h0 + 15:h1:16], CO, float(W), A.add, A.min, nmr, ["RL%d" % gi], 6)
+            act(T.Dg[:, h0:h1], DG.indirect(T.RL[:, l0:l0 + 3 * nb]), AF.Copy, Dr[t] + ["RL%d" % gi], ["Dg%d" % gi], 0, dur=gs(hn))
+            pv, pvn = PK[gi][:, 128:128 + hn], "ps:P%d" % gi
+            mm(pv, idp, T.Dg[:, h0:h1], True, False, ["idp", "Dg%d" % gi], [pvn], max(64, hn))
+            for ty in range(3):
+                mm(PK[gi][:, 128 + 16 * nb * ty:128 + 16 * nb * (ty + 1)], idp if ty else idn,
+                   T.fvS[:, 48 * m + 16 * bs[0]:48 * m + 16 * bs[0] + 16 * nb], False, ty == 2, ["idp", "idn", "fv"], [pvn], 64)
+            svd, svn = SV[:, 2 * h0:2 * h0 + hn], SV[:, 2 * h0 + hn:2 * h1]
+            vd, vn = "SVd%d%d" % (t, gi), "SVn%d%d" % (t, gi)
             if not last:
-                act(SV[:, 144 + n0:144 + n1], SV[:, n0:n1], AF.Relu, ["SVd%d%d" % (t, gi)], ["SVn%d%d" % (t, gi)], n, scale=-1.0)
-                ts(T.ny[:, c0:c1], nm, float(O), float(J), A.is_lt, A.mult, nmr, ["ny%d" % gi], 3)
-                tt(T.nd[:, c0:c1], nm, T.dum[:, c0:c1], A.subtract, nmr + dumr, ["nd%d" % gi], 3)
-                tt(dd, T.nd[:, c0:c1], T.ny[:, c0:c1], A.add, ["nd%d" % gi, "ny%d" % gi], ["dd%d" % gi], 3)
-            else:
-                tt(dd, nm, T.dum[:, c0:c1], A.subtract, nmr + dumr, ["dd%d" % gi], 3)
-            for b in bs:
-                k, e0 = 144 * (b + 1), (0, 144, 432)[b]
-                s = T.M[:, 4 * b + 2:4 * b + 3]
-                red(s, T.NE[:, e0:e0 + k], A.min, ["NE%d%d" % (b, ty) for ty in range(3)], ["s%d" % b], k, True)
-                ts(sd[:, 3 * b:3 * b + 3], T.dd[:, 3 * b:3 * b + 3], s, None, A.mult, None, ["s%d" % b, "dd%d" % gi], ["sd%d%d" % (m, b)], 3)
-            bo[0] = 0.0
-            for b in bs:
-                act(mR[:, 16 * b:16 * b + 16], MK[:, 48 * b:48 * b + 16], AF.Copy, [mk], ["mR%d%d" % (m, b)], 16)
-        sdr = ["sd%d%d" % (m, b) for b in range(3)]
-        tt(T.fo[:, 0:9], sd[:, 0:9], T.dum[:, 0:9], A.add, sdr + dumr, ["fo"], 9)
-        cp(SO[:, 0:9], T.fo[:, 0:9], ["fo"], ["SO%d" % t], 9)
-        ts(cm[:, 0:3], sd[:, 0:9:3], 0.0, None, A.not_equal, None, sdr, ["cm%d" % m], 3)
-        SOr = ["SO%d" % t]
-        SVd = ["SVd%d%d" % (t, gi) for gi in range(len(GROUPS))]
-        SVn = ["SVn%d%d" % (t, gi) for gi in range(len(GROUPS))]
-        selr = ["sel%d%d" % (m, gi) for gi in range(len(GROUPS))]
-        if not last:
-            remote(T["RV%d" % t][:], SV[:], SVd + SVn, "RV%d" % t, 128 * 576)
-            sent = remote(T["RO%d" % t][:], SO[:], SOr, "RO%d" % t, 128 * 32)
-            L, RV, RO = T["L%d" % t], T["RV%d" % t], T["RO%d" % t]
-            dma(T.DW[:, J + O:J + W], L[:], ["L%d" % t], ["Dblk"], 256 * S)
-            ops[-1]["after"] = [sent]
-            for q in range(4):
-                out, src, w = T.NW[:, J + O + 512 * q:J + O + 512 * q + 512], L[:, 512 * q:512 * q + 512], ["Nblk" + (str(q) if q else "")]
-                if NQ[q] == "s":
-                    act(out, src, AF.Relu, ["L%d" % t], w, 512, scale=-1.0)
+                act(svn, pv, AF.Relu, [pvn], [vn], hn, scale=-1.0)
+            act(svd, pv, AF.Copy, [pvn], [vd], hn)
+            v0, k0, f0 = gr["v0"], gr["k0"], gr["f0"]
+            mm(Fp[:, 0:2 * hn], T.idF[:, 0:128], T.CF[:, f0:f0 + 2 * hn], True, False, ["idF0", "CF0", "CF96", "CF240"], [fn_], 8 * hn)
+            for ty, (s_, sn_) in enumerate(srcs):
+                mm(Fp[:, v0 + 16 * nb * ty:v0 + 16 * nb * (ty + 1)], bd[ty], s_[:, e0:e1], False, False, ["bd%d" % ty, sn_], [fn_], 256)
+            mm(Fp[:, k0:k0 + hn:3], bd[3], T.selL[:, e0:e1], False, False, ["bd3", sl], [fn_], 256)
+            sgA = T.sn[:, 48 + e0 - 64:48 + e1 - 64]
+            act(sgA, selA[:, e0:e1], AF.Sign, [sa], ["snA%d" % gi], 32)
+            if not last:
+                sgL = T.sn[:, e0 - 64:e1 - 64]
+                act(sgL, T.selL[:, e0:e1], AF.Sign, [sl], ["snL%d" % gi], 32)
+                for ty in range(3):
+                    mm(Fp[:, v0 + 16 * nb * ty:v0 + 16 * nb * (ty + 1)], bdH[ty], sgA if ty else sgL, False, False,
+                       ["bdH%d" % ty, ("snA%d" if ty else "snL%d") % gi], [fn_], 64)
+            cmpl = [(0, 0, 96, 0), (1, 144, 48, 48)] if gi == 0 else [(0, 48, 48, 0), (1, 48, 48, 0), (2, 96, 48, 0)]
+            eo = 432 * gi
+            for ci, (bl, q0, w_, o_) in enumerate(cmpl):
+                for ty in range(3):
+                    gl = 0 if bl < 2 else 1
+                    x_ = (32 * ty + 16 * bl + 15) if bl < 2 else (96 + 16 * ty + 15)
+                    en = "E%d" % eo
+                    if eo + w_ > 768:
+                        eo = 0
+                        en = "E0"
+                    ts(T.E[:, eo:eo + w_], Qp[:, q0:q0 + w_], T.nm[:, x_:x_ + 1], None, A.is_equal, None, [qn, "nm%d%d" % (gl, ty)],
+                       ["E%d" % i for i in range(eo, eo + w_, 48)], w_)
+                    mm(Fp[:, k0 + o_:k0 + o_ + w_], bdH[3], T.E[:, eo:eo + w_], False, ci == len(cmpl) - 1 and ty == 2,
+                       ["bdH3"] + ["E%d" % i for i in range(eo, eo + w_, 48)], [fn_], max(64, w_))
+                    eo += w_
+            scan(T.S2[:, f0:f0 + 2 * hn], T.rs[:, f0:f0 + 2 * hn], Fp[:, 0:2 * hn], ["rs", fn_], ["S2%d" % gi], 2 * hn)
+            SO = T["SO%d%d" % (t, gi)]
+            SOr = ["SO%d%d%d" % (t, gi, i) for i in range(3 * nb)]
+            for i in range(3 * nb):
+                v_ = f0 + v0 + 16 * i + 15
+                s_ = 143 + 48 * bs[i % nb]
+                ts(SO[:, i:i + 1], T.S2[:, v_:v_ + 1], T.S2[:, s_:s_ + 1], T.dum[:, i:i + 1], A.min, A.max, ["S2%d" % gi, "dum"],
+                   [SOr[i]], 1)
+            so = SO[:, 0:3 * nb]
+            if last:
+                cp(dw(t, -LO - AL, WX).indirect(so), svd, SOr + [vd], ["fin", "jD"] + (Dr[t] if gi else []), 0, dur=sc(hn))
+                if gi == 0:
+                    fin = ops.pop()
                 else:
-                    ts(out, src, -1.0, 0.0, A.mult, A.max, ["L%d" % t], w, 512, 0.5)
-                if q:
-                    ops[-1]["after"] = [len(ops) - 1 - q]
-            nb = ["Nblk1", "Nblk2", "Nblk3"]
-            cp(T.NW[:, 0:J + O].indirect(SO[:, 0:9]), SV[:, 144:288], SOr + SVn, No, 0, dur=sc(144))
-            cp(T.DW[:, 0:J + O].indirect(SO[:, 0:9]), SV[:, 0:144], SOr + SVd, Do, 0, dur=sc(144))
-            cp(T.NW[:, J:WD].indirect(RO[:, 0:9]), RV[:, 144:288], ["RO%d" % t, "RV%d" % t], Nr + nb, 0, dur=sc(144))
-            cp(T.DW[:, J:WD].indirect(RO[:, 0:9]), RV[:, 0:144], ["RO%d" % t, "RV%d" % t], Dr, 0, dur=sc(144))
-        else:
-            cp(DG.indirect(SO[:, 0:9]), SV[:, 0:144], SOr + SVd, Dr, 0, dur=sc(144))
-            dma(T.yd[:], T.DW[:, J:J + W], Dr, [], 256 * W)
+                    fin["w"] = ["fin", "jD"] + Dr[t]
+                    ops.insert(len(ops) - 1, fin)
+                continue
+            RV, RO = T["RV%d" % t], T["RO%d%d" % (t, gi)]
+            rv, ro = "RV%d%d" % (t, gi), "RO%d%d" % (t, gi)
+            remote(RV[:, 2 * h0:2 * h1], SV[:, 2 * h0:2 * h1], [vd, vn], rv, 512 * hn)
+            remote(RO[:], SO[:], SOr, ro, 128 * 32)
+            bo[0] = 0.0
+            cp(nw(t + 1, -J, O).indirect(so), svn, SOr + [vn], No[t + 1] + ["jN"], 0, dur=sc(hn))
+            cp(dw(t + 1, -J, O).indirect(so), svd, SOr + [vd], Do[t + 1] + ["jD"], 0, dur=sc(hn))
+            cp(nw(t + 1, -LO, J + O - LO).indirect(RO[:, 0:3 * nb]), RV[:, 2 * h0 + hn:2 * h1], [rv, ro], Nr[t + 1] + ["jN"], 0,
+               dur=sc(hn))
+            cp(dw(t + 1, -LO, J + O - LO).indirect(RO[:, 0:3 * nb]), RV[:, 2 * h0:2 * h0 + hn], [rv, ro], Dr[t + 1] + ["jD"], 0,
+               dur=sc(hn))
+            bo[0] = BOOST
+        bo[0] = 0.0
+        if last:
+            dma(T.yd[:], dw(t, 0, W), Dr[t], [], 256 * W)
         p = T.Pf[:, 48 * m:48 * m + 48]
         pn = "P%d" % m
-        act(T.ne[:], p, AF.Sign, [pn], ["ne"], 48, bias=EMPTY / 2, scale=-1.0)
-        mm(T.PA[:, 96:144], T.Sh[:], T.ne[:], True, True, ["Sh", "ne"], ["ps:PA"], 64)
-        for b in range(3):
-            for ty in (1, 2):
-                o = 48 * (ty - 1) + 16 * b
-                mm(T.PA[:, o:o + 16], T.bd[:], selb[:, 48 * b + 16 * ty:48 * b + 16 * ty + 16], True, True, ["bd"] + selr, ["ps:PA"], 256)
-        act(T.cB[:], T.c[:, 0:16].indirect(cm[:, 0:3]), AF.Copy, ["c", "cm%d" % m], ["cB"], 0, dur=gs(48))
         pw = T.pw
-        ts(T.yb[:], T.PA[:, 0:96], float(O), float(B * S), A.is_ge, A.mult, ["ps:PA"], ["yb"], 96)
-        tt(pw[:, 336:384], T.PA[:, 96:144], T.cB[:], A.mult, ["ps:PA", "cB"], ["pw5"], 48, 1.0)
-        tt(pw[:, 288:336], mR[:], T.cB[:], A.mult, ["mR%d%d" % (m, b) for b in range(3)] + ["cB"], ["pw4"], 48)
-        mm(T.PA[:, 144:240], T.ident[:], T.yb[:], True, False, ["ident", "yb"], ["ps:PA"], 96)
-        for b in range(3):
-            for ty in (1, 2):
-                o = 144 + 48 * (ty - 1) + 16 * b
-                mm(T.PA[:, o:o + 16], T.bd[:], selb[:, 48 * b + 16 * ty:48 * b + 16 * ty + 16], False, False, ["bd"] + selr, ["ps:PA"], 256)
+        sar = ["selA%d0" % m, "selA%d1" % m]
+        ts(T.cm[:, 0:3], T.S2[:, 143:240:48], 0.0, None, A.is_gt, None, ["S20", "S21"], ["cm"], 3)
+        act(T.cB[:], T.c[:, 0:16].indirect(T.cm[:, 0:3]), AF.Copy, ["c", "cm"], ["cB"], 0, dur=gs(48))
+        act(T.yb[:], T.sn[:, 48:96], AF.Relu, ["snA0", "snA1"], ["yb"], 48, scale=float(B * S))
+        tt(pw[:, 0:48], TmR.indirect(ML[:, 4:7]), T.cB[:], A.mult, ["TmR", "cB"] + ["ML%d%d" % (m, b) for b in range(3)], ["pwA"], 0,
+           dur=gv(48))
+        tt(pw[:, 48:96], T.mN[:, 48 * m:48 * m + 48], T.cB[:], A.mult, ["mN%d" % m, "cB"], ["pwB"], 48)
         for h in range(2):
-            mm(T.PA[:, 144 + 48 * h:192 + 48 * h], T.idF[:, 128:256], p, False, h == 1, ["idF1", pn], ["ps:PA"], 256)
-        tt(pw[:, 384:480], T.PA[:, 144:240], pw[:, 288:384], A.mult, ["ps:PA", "pw4", "pw5"], ["pw6"], 96, 1.0)
+            o_ = T.PA[:, 48 * h:48 * h + 48]
+            mm(o_, bd[1 + h], selA[:, 64:112], True, False, ["bd%d" % (1 + h)] + sar, ["ps:PA"], 256)
+            mm(o_, bd[1 + h], T.yb[:], False, False, ["bd%d" % (1 + h), "yb"], ["ps:PA"], 256)
+            mm(o_, T.idF[:, 128:256], p, False, True, ["idF1", pn], ["ps:PA"], 256)
+        tt(pw[:, 96:192], T.PA[:, 0:96], pw[:, 0:96], A.mult, ["ps:PA", "pwA", "pwB"], ["pwU"], 96, 1.0)
         mm(T.PA[:, 240:288], T.idF[:, 0:128], p, True, False, ["idF0", pn], ["ps:PA"], 256)
         for h in range(2):
-            mm(T.PA[:, 240:288], T.idF[:, 0:128], pw[:, 384 + 48 * h:432 + 48 * h], False, h == 1, ["idF0", "pw6"], ["ps:PA"], 256)
+            mm(T.PA[:, 240:288], T.idF[:, 0:128], pw[:, 96 + 48 * h:144 + 48 * h], False, h == 1, ["idF0", "pwU"], ["ps:PA"], 256)
         act(p, T.PA[:, 240:288], AF.Copy, ["ps:PA"], [pn], 48)
         if t + 2 < ST:
             lists(t + 2)
         else:
-            y = T.cw[:, 192 * m:192 * m + 48]
-            ts(y, p, EMPTY / 2, -EMPTY - 1.0, A.is_ge, A.mult, [pn], ["cw%d0" % m], 48)
-            tt(T.Py[:, 48 * m:48 * m + 48], p, y, A.add, [pn, "cw%d0" % m, "Py"], ["Py%d" % m], 48)
+            y, y2 = T.cw[:, 192 * m:192 * m + 48], T.cw[:, 192 * m + 48:192 * m + 96]
+            ts(y, p, EMPTY / 2, -EMPTY - CO - 1.0, A.is_ge, A.mult, [pn], ["cw%d0" % m], 48)
+            aff(y2, p, None, CO, [pn], ["cw%d1" % m], 48)
+            tt(T.Py[:, 48 * m:48 * m + 48], y2, y, A.add, ["cw%d0" % m, "cw%d1" % m, "Py"], ["Py%d" % m], 48)
             dma(T.yp[:, 48 * m:48 * m + 48], T.Py[:, 48 * m:48 * m + 48], ["Py%d" % m], [], 128 * 192)
     return ops
 
@@ -481,8 +529,8 @@ def depend(ops):
                 if cur and ops[cur[-1]]["eng"] != o["eng"]:
                     prev, cur = cur, []
                 hard.update(prev)
-                if cur and o["eng"] == "p" and not o.get("free"):
-                    soft.add(cur[-1])
+                if cur and o["eng"] == "p":
+                    soft.add(cur[0] if o.get("free") else cur[-1])
                 ps[x] = (prev, cur + [i])
         for x in o["r"]:
             if not x.startswith("ps:") and x in lw:
@@ -503,79 +551,81 @@ def depend(ops):
         o["hard"], o["soft"] = sorted(hard), sorted(soft - hard)
 
 
-def kind(o):
-    if o.get("chain"):
-        return None
-    n = (o["w"] + o["r"])[0]
-    a = n.rstrip("0123456789")
-    d = n[len(a):]
-    if a in ("NE", "IL"):
-        d = d[:1]
-    elif a in ("SO", "SVd", "SVn", "sd", "sel", "MK", "nm", "m", "s", "ML", "RL", "fo", "dd", "ny", "nd", "Dg", "X", "tmp", "AB", "A", "Nown", "Down"):
-        d = d[-1:]
-    else:
-        d = ""
-    return (o["eng"] or "x") + a + d
-
-
 def schedule(ops):
     n = len(ops)
+    pred = [[] for _ in range(n)]
     succ = [[] for _ in range(n)]
-    for i, o in enumerate(ops):
-        for k in o["hard"] + o["soft"]:
-            succ[k].append(i)
+    for k, o in enumerate(ops):
+        for i in o["hard"] + o["soft"]:
+            lag = 0.0 if i in o["soft"] and o["eng"] is not None else ops[i]["lat"] + HOP
+            pred[k].append((i, lag))
+            succ[i].append((k, lag))
+
+    def sweep(key, before, after, head):
+        left = [len(x) for x in before]
+        rdy = list(head)
+        st = [0.0] * n
+        busy = {}
+        heap = sorted((key[i], i) for i in range(n) if left[i] == 0)
+        while heap:
+            i = heap.pop(0)[1]
+            t0, d = rdy[i], ops[i]["dur"]
+            if ops[i]["eng"] is not None:
+                q = busy.setdefault(ops[i]["eng"], [])
+                lo, hi = 0, len(q)
+                while lo < hi:
+                    mid = (lo + hi) // 2
+                    if q[mid][1] <= t0:
+                        lo = mid + 1
+                    else:
+                        hi = mid
+                while lo < len(q) and q[lo][0] < t0 + d - 1e-9:
+                    t0 = max(t0, q[lo][1])
+                    lo += 1
+                q.insert(lo, (t0, t0 + d))
+            st[i] = t0
+            new = []
+            for k, lag in after[i]:
+                rdy[k] = max(rdy[k], t0 + d + lag)
+                left[k] -= 1
+                if left[k] == 0:
+                    new.append((key[k], k))
+            if new:
+                heap = sorted(heap + new)
+        return st
+
     pr = [0.0] * n
     for i in range(n - 1, -1, -1):
-        pr[i] = ops[i]["dur"] + ops[i]["lat"] + HOP + max([pr[k] for k in succ[i]], default=0.0)
-    pr = [pr[i] + ops[i]["boost"] + PRI.get(kind(ops[i]), 0.0) for i in range(n)]
-    left = [len(o["hard"]) + len(o["soft"]) for o in ops]
-    rdy = [0.0] * n
-    st = [0.0] * n
-    free = {}
-    cand = {}
-    order = []
-
-    def place(i, t0):
-        o = ops[i]
-        st[i] = t0
-        order.append(i)
-        end = t0 + o["dur"] + o["lat"]
-        for k in succ[i]:
-            if i in ops[k]["soft"] and ops[k]["eng"] is not None:
-                rdy[k] = max(rdy[k], t0)
-            else:
-                rdy[k] = max(rdy[k], end + HOP)
-            left[k] -= 1
-            if left[k] == 0:
-                enter(k)
-
-    def enter(i):
-        if ops[i]["eng"] is None:
-            place(i, rdy[i])
-        else:
-            cand.setdefault(ops[i]["eng"], []).append(i)
-
-    for i in range(n):
-        if left[i] == 0:
-            enter(i)
-    while any(cand.values()):
+        pr[i] = ops[i]["dur"] + max([lag + pr[k] for k, lag in succ[i]], default=ops[i]["lat"])
+    if n not in KEPT:
         best = None
-        for e, c in cand.items():
-            if not c:
-                continue
-            now = max(free.get(e, 0.0), min(rdy[i] for i in c))
-            pick = max((i for i in c if rdy[i] <= now), key=lambda i: (pr[i], -i))
-            for i in c:
-                if rdy[i] > now and pr[i] > pr[pick] + 0.3 and rdy[i] - now < 0.5 * ops[pick]["dur"]:
-                    pick = i
-            t0 = max(now, rdy[pick])
-            if best is None or t0 < best[0]:
-                best = (t0, e, pick)
-        t0, e, pick = best
-        cand[e].remove(pick)
-        free[e] = t0 + ops[pick]["dur"]
-        place(pick, t0)
-    return order, st
+        rng = np.random.default_rng(0)
+        for trial in range(len(URGE) + TRIES):
+            if trial < len(URGE):
+                key = [-pr[i] - URGE[trial] * ops[i]["boost"] for i in range(n)]
+            else:
+                mid, amp = float(rng.random()) * best[0], float(rng.random()) * 2.0
+                z = rng.random(n)
+                key = [best[1][i] + (amp * float(z[i]) if abs(best[1][i] - mid) < 6.0 else 0.0) for i in range(n)]
+            for _ in range(PASSES):
+                st = sweep(key, pred, succ, [0.0] * n)
+                end = max(st[i] + ops[i]["dur"] + ops[i]["lat"] for i in range(n))
+                if best is None or end < best[0] + 1e-6:
+                    best = (end, st)
+                back = sweep([-st[i] - ops[i]["dur"] for i in range(n)], succ, pred, [o["lat"] for o in ops])
+                key = [-back[i] - ops[i]["dur"] for i in range(n)]
+        KEPT[n] = best[1]
+    st = KEPT[n]
+    return sorted(range(n), key=lambda i: (st[i], i)), st
+
+
+def mark(ops, order):
+    end = {}
+    for i in order:
+        if ops[i].get("group"):
+            end[ops[i]["group"]] = i
+    for i in end.values():
+        ops[i]["flag"][0] = True
 
 
 def emit(g, T, ops, order):
@@ -623,4 +673,5 @@ def rank_program(g, core, T, topo):
     ops = build(T, rank, topo, core)
     depend(ops)
     order, _st = schedule(ops)
+    mark(ops, order)
     emit(g, T, ops, order)

@@ -16,7 +16,7 @@ CO = O - 0.5
 EMPTY = float(1 << 16)
 KS = 32768.0
 RC = 1.5 * 2.0 ** 38
-NV = [[7, 7, 5]] * ST
+NV = [[8, 7, 7]] * ST
 NQ = "ssss"
 DETCH = 4
 NCH = [(O, W, "s"), (0, 1024, "v"), (1024, 2048, "v"), (2048, O, "v")]
@@ -29,7 +29,7 @@ for _dt, _bufs in (
                           ident=256, Sh=128, t1=128, t2=128, t3=128, ind=8, qm=384, E=768, Dg=144, idS=768, one=48, sg=288, ne=96,
                           bdH=512, MK=144, sn=96, SV0=288, SV1=288, SV2=288, SV3=288, RV0=288, RV1=288, RV2=288)),
         ("float32", dict(detF=O + 48, Pf=96, Py=96, cw=480, K=24, c=144, xc=128, x3=384, hi=256, I2=104, I4=32, bd=512, cv=48, KT=336,
-                         dum=12, MC=12, C3=4, M=4, r3=12, nm=144, rs=288, CF=288, S2=288, idF=256, cB=48, pw=192, AB0=768, AB1=768,
+                         dum=12, MC=12, M=336, rk=112, nm=144, rs=288, CF=288, S2=288, idF=256, cB=48, pw=192, AB0=768, AB1=768,
                          col=96, colD=288, selL=144, selA0=144, selA1=144, yb=48, mN=96)),
         ("int32", dict(detI=O, pthI=96, pI=4)),
         ("uint16", dict(col16=96, site16=96, IL=12, ML0=12, ML1=12, RL=12, CL=12, A160=768, A161=768, cm=4))):
@@ -46,12 +46,12 @@ for _n in ("P0", "P1", "P2", "Q0", "Q1", "F0", "F1", "PA"):
 SEMAPHORES = (["qv", "qs", "qp", "qg"] + ["dm%d" % i for i in range(24)] + ["ls%d" % i for i in range(18)]
               + ["ar%d" % i for i in range(18)])
 
-CY = 1.04e-3
-PC = 0.55e-3
-HOP = 0.16
+CY = 0.9e-3
+PC = 0.47e-3
+HOP = 0.22
 FX = 0.0
-BWL = 250e3
-GA = 1.56
+BWL = 350e3
+GA = 1.45
 SC = 3.8
 RL0 = 1.2
 BOOST = 8.0
@@ -170,8 +170,11 @@ def build(T, rank, topo, core):
     Do = [["D0o%d" % i for i in range(nown)]] + [["D%do" % t] for t in range(1, ST)]
     No = [["N0o%d" % i for i in range(nown)]] + [["N%do" % t] for t in range(1, ST)]
     Nb = [["N%db%d" % (t, q) for q in range(1 if NSEND else 4)] for t in range(ST)]
-    Dr = [Do[t] + ["D%db" % t, "D%dz" % t] for t in range(ST)]
-    Nr = [No[t] + Nb[t] for t in range(ST)]
+    sct = [[]] + [["s0", "s1", "r0", "r1"]] * (ST - 1)
+    Ds = [["D%d%s" % (t, x) for x in sct[t]] for t in range(ST)]
+    Ns = [["N%d%s" % (t, x) for x in sct[t]] for t in range(ST)]
+    Dr = [Do[t] + ["D%db" % t, "D%dz" % t] + Ds[t] for t in range(ST)]
+    Nr = [No[t] + Nb[t] + Ns[t] for t in range(ST)]
     AB = [T.AB0, T.AB1]
     A16 = [T.A160, T.A161]
     PK = [T.P0, T.P1, T.P2]
@@ -265,7 +268,11 @@ def build(T, rank, topo, core):
     tt(T.Sh[:], T.t2[:], T.t3[:], A.mult, ["t2", "t3"], ["Sh"], 128)
     aff(k12, pm, -256.0, None, ["pm"], ["k12"], 1)
     aff(T.MC[:, 0:9], T.I4[:, 12:21], None, k12, ["I4c", "k12"], ["MC"], 9)
-    ms(T.C3[:], RC, ["C3"], 4)
+    ms(T.rk[:], 0.0, ["rk"], 112)
+    for i, v_ in ((0, 2.0 ** 25), (105, RC), (106, -RC)):
+        ms(T.rk[:, i:i + 1], v_, ["rk"], 1)
+    for b in range(3):
+        ms(T.KT[:, 112 * b + 105:112 * b + 112], 4 * RC, ["KT"], 7)
     aff(T.dum[:, 0:9], T.c[:, 0:9], 16.0, pm, ["c", "pm"], ["dum"], 9)
 
     bo[0] = 0.0
@@ -338,16 +345,19 @@ def build(T, rank, topo, core):
         DG, NG = dw(t, 0, WX), nw(t, 0, W)
         if not last:
             if NSEND:
-                remote(nw(t + 1, O, W), nw(t, O, W), Nb[t] + (Do[0] if t == 0 else []), Nb[t + 1][0], 256 * S)
-            remote(dw(t + 1, O, W), dw(t, O, W), ["D%db" % t] + (Do[0] if t == 0 else []), "D%db" % (t + 1), 256 * S * (1 + NSEND))
-            dma(nw(t + 1, 0, O), nw(t, 0, O), No[t], No[t + 1], 256 * O)
-            dma(dw(t + 1, 0, O), dw(t, 0, O), Do[t], Do[t + 1], 256 * O)
+                remote(nw(t + 1, O, W), nw(t, O, W), Nb[t] + Ns[t] + (Do[0] if t == 0 else []), Nb[t + 1][0], 256 * S)
+            remote(dw(t + 1, O, W), dw(t, O, W), ["D%db" % t] + Ds[t] + (Do[0] if t == 0 else []), "D%db" % (t + 1),
+                   256 * S * (1 + NSEND))
+            dma(nw(t + 1, 0, O), nw(t, 0, O), No[t] + Ns[t], No[t + 1], 256 * O)
+            dma(dw(t + 1, 0, O), dw(t, 0, O), Do[t] + Ds[t], Do[t + 1], 256 * O)
             for q in range(0 if NSEND else 4):
                 out, src = nw(t + 1, O + 512 * q, O + 512 * q + 512), dw(t + 1, O + 512 * q, O + 512 * q + 512)
                 if NQ[q] == "s":
                     act(out, src, AF.Relu, ["D%db" % (t + 1)], [Nb[t + 1][q]], 512, scale=-1.0)
                 else:
                     ts(out, src, -1.0, 0.0, A.mult, A.max, ["D%db" % (t + 1)], [Nb[t + 1][q]], 512, 0.5)
+        else:
+            dma(nw(1, 0, W), dw(t, 0, W), Dr[t], Nr[1], 256 * W)
         bo[0] = BOOST
         tt(T.tmp[:], DG.indirect(T.col16[:, 48 * m:48 * m + 48]), T.F16[:, 768 * m:768 * m + 768], A.min,
            Dr[t] + ["c16%d" % m] + F16r, ["tmp"], 0, dur=gv(768))
@@ -383,12 +393,12 @@ def build(T, rank, topo, core):
                     ops[-1]["boost"] = 0.0
                     z = T.Z[:, 144 * onv[j] + 15 - x:144 * onv[j] + 143 - x]
                     acc([(PK[b][:, 0:8 * R], z, T.G[:, j, h:16 * R:2]) for h in range(2)], key, ["G%d" % j, "Z0", "Z1"], [pk], 16 * R)
-                mb, r3 = T.M[:, b:b + 1], T.r3[:, 3 * b:3 * b + 3]
-                red(mb, PK[b][:, 0:105], [pk], ["m%d" % b], 105)
-                ts(r3, T.C3[:, 0:3], mb, RC, A.add, A.subtract, ["C3", "m%d" % b], ["r%d" % b], 3)
-                ts(ML[:, LCOL[b]], T.MC[:, 3 * b:3 * b + 3], mb, T.r3[:, 3 * b:3 * b + 1], A.add, A.subtract,
-                   ["MC", "m%d" % b, "r%d" % b], ["ML%d%d" % (m, b)], 3)
-                ts(T.IL[:, LCOL[b]], r3, mb, -0.0625, A.subtract, A.mult, ["m%d" % b, "r%d" % b], ["IL%d" % b], 3)
+                o_ = 112 * b
+                mb = T.M[:, o_ + 104:o_ + 105]
+                scan(T.M[:, o_:o_ + 109], T.rk[:, 0:109], PK[b][:, 0:109], ["rk", pk], ["m%d" % b], 109)
+                ts(ML[:, LCOL[b]], T.MC[:, 3 * b:3 * b + 3], mb, T.M[:, o_ + 106:o_ + 107], A.add, A.subtract,
+                   ["MC", "m%d" % b], ["ML%d%d" % (m, b)], 3)
+                ts(T.IL[:, LCOL[b]], T.M[:, o_ + 106:o_ + 109], mb, -0.0625, A.subtract, A.mult, ["m%d" % b], ["IL%d" % b], 3)
             n0, n1, n = 16 * c0, 16 * c1, 16 * (c1 - c0)
             e0, e1 = 16 * d0, 16 * (d0 + nb)
             h0, h1, hn = 48 * bs[0], 48 * (bs[-1] + 1), 48 * nb
@@ -460,28 +470,26 @@ def build(T, rank, topo, core):
                    [SOr[i]], 1)
             so = SO[:, 0:3 * nb]
             if last:
-                cp(dw(t, -LO - AL, WX).indirect(so), svd, SOr + [vd], ["fin", "jD"] + (Dr[t] if gi else []), 0, dur=sc(hn))
-                if gi == 0:
-                    fin = ops.pop()
-                else:
-                    fin["w"] = ["fin", "jD"] + Dr[t]
-                    ops.insert(len(ops) - 1, fin)
+                cp(nw(1, -LO - AL, W).indirect(so), svd, SOr + [vd] + No[1], ["fin%d" % gi], 0, dur=sc(hn))
+                ops[-1]["turn"] = "N"
                 continue
             RV, RO = T["RV%d" % t], T["RO%d%d" % (t, gi)]
             rv, ro = "RV%d%d" % (t, gi), "RO%d%d" % (t, gi)
             remote(RV[:, 2 * h0:2 * h1], SV[:, 2 * h0:2 * h1], [vd, vn], rv, 512 * hn)
             remote(RO[:], SO[:], SOr, ro, 128 * 32)
             bo[0] = 0.0
-            cp(nw(t + 1, -J, O).indirect(so), svn, SOr + [vn], No[t + 1] + ["jN"], 0, dur=sc(hn))
-            cp(dw(t + 1, -J, O).indirect(so), svd, SOr + [vd], Do[t + 1] + ["jD"], 0, dur=sc(hn))
-            cp(nw(t + 1, -LO, J + O - LO).indirect(RO[:, 0:3 * nb]), RV[:, 2 * h0 + hn:2 * h1], [rv, ro], Nr[t + 1] + ["jN"], 0,
-               dur=sc(hn))
-            cp(dw(t + 1, -LO, J + O - LO).indirect(RO[:, 0:3 * nb]), RV[:, 2 * h0:2 * h0 + hn], [rv, ro], Dr[t + 1] + ["jD"], 0,
-               dur=sc(hn))
+            cp(nw(t + 1, -J, O).indirect(so), svn, SOr + [vn] + No[t + 1], [Ns[t + 1][gi]], 0, dur=sc(hn))
+            cp(dw(t + 1, -J, O).indirect(so), svd, SOr + [vd] + Do[t + 1], [Ds[t + 1][gi]], 0, dur=sc(hn))
+            cp(nw(t + 1, -LO, J + O - LO).indirect(RO[:, 0:3 * nb]), RV[:, 2 * h0 + hn:2 * h1], [rv, ro] + No[t + 1] + Nb[t + 1],
+               [Ns[t + 1][2 + gi]], 0, dur=sc(hn))
+            cp(dw(t + 1, -LO, J + O - LO).indirect(RO[:, 0:3 * nb]), RV[:, 2 * h0:2 * h0 + hn],
+               [rv, ro, "D%db" % (t + 1), "D%dz" % (t + 1)] + Do[t + 1] + Nb[t + 1], [Ds[t + 1][2 + gi]], 0, dur=sc(hn))
+            for o_, b_ in zip(ops[-4:], "NDND"):
+                o_["turn"] = b_
             bo[0] = BOOST
         bo[0] = 0.0
         if last:
-            dma(T.yd[:], dw(t, 0, W), Dr[t], [], 256 * W)
+            dma(T.yd[:], nw(1, 0, W), ["fin0", "fin1"], [], 256 * W)
         p = T.Pf[:, 48 * m:48 * m + 48]
         pn = "P%d" % m
         pw = T.pw
@@ -620,10 +628,15 @@ def schedule(ops):
 
 
 def mark(ops, order):
-    end = {}
+    end, turn = {}, {}
     for i in order:
         if ops[i].get("group"):
             end[ops[i]["group"]] = i
+        b = ops[i].get("turn")
+        if b:
+            if b in turn and turn[b] not in ops[i]["hard"]:
+                ops[i]["hard"].append(turn[b])
+            turn[b] = i
     for i in end.values():
         ops[i]["flag"][0] = True
 

@@ -1,4 +1,5 @@
 import numpy as np
+from concourse.bass import DstId, RemoteDMATransfer
 from concourse.mybir import AluOpType as A, AxisListType as AX, ActivationFunctionType as AF
 
 O, S, W, FB, ST = 2560, 2048, 4608, 48, 4
@@ -9,28 +10,32 @@ WX = W + 16
 WB = (ST - 1) * (J + WX) + J - LO + O - WX
 NSEND = False
 PASSES = 2
-TRIES = 300
+SEED = 0
+TRIES = 1200
 URGE = (0.0, 0.25, 0.5, 1.0, 2.0)
 KEPT = {}
-CO = O - 0.5
+CO = O - 0.25
+CV = float(O + LO + AL)
 EMPTY = float(1 << 16)
 KS = 32768.0
 RC = 1.5 * 2.0 ** 38
 NV = [[8, 7, 7]] * ST
 NQ = "ssss"
 DETCH = 4
-NCH = [(O, W, "s"), (0, 1024, "v"), (1024, 2048, "v"), (2048, O, "v")]
-GROUPS = [dict(bs=(0, 1), c0=0, c1=6, d0=4, f0=0, v0=0, k0=96), dict(bs=(2,), c0=6, c1=9, d0=6, f0=192, v0=48, k0=0)]
-LCOL = [slice(0, 5, 2), slice(1, 6, 2), slice(6, 9)]
+NCH = [(O, W, "sv"), (0, 1024, "v"), (1024, 2048, "v"), (2048, O, "v")]
+GROUPS = [dict(bs=(0, 1), c0=0, c1=4, d0=2, f0=0, v0=0, k0=96), dict(bs=(2,), c0=4, c1=6, d0=4, f0=192, v0=48, k0=0)]
+LCOL = [slice(0, 3, 2), slice(1, 4, 2), slice(4, 6)]
 
-SCRATCH = {"G": ("sbuf", [128, 48, 208], "bfloat16")}
+SCRATCH = {"G": ("sbuf", [128, 48, 208], "bfloat16"), "tmp": ("sbuf", [128, 768], "bfloat16"),
+           "ne": ("sbuf", [128, 96], "bfloat16"), "qm": ("sbuf", [128, 3, 96], "bfloat16"), "E": ("sbuf", [128, 54, 16], "bfloat16"),
+           "Q0": ("psum", [128, 4, 128], "float32"), "Q1": ("psum", [128, 4, 128], "float32")}
 for _dt, _bufs in (
-        ("bfloat16", dict(D0=WX, N0=W, DB=WB, NB=WB, fvS=96, F16=1536, tmp=768, Gs=768, X=128, Ex=104, Tm=512, Z=288,
-                          ident=256, Sh=128, t1=128, t2=128, t3=128, ind=8, qm=384, E=768, Dg=144, idS=768, one=48, sg=288, ne=96,
-                          bdH=512, MK=144, sn=96, SV0=288, SV1=288, SV2=288, SV3=288, RV0=288, RV1=288, RV2=288)),
-        ("float32", dict(detF=O + 48, Pf=96, Py=96, cw=480, K=24, c=144, xc=128, x3=384, hi=256, I2=104, I4=32, bd=512, cv=48, KT=336,
-                         dum=12, MC=12, M=336, rk=112, nm=144, rs=288, CF=288, S2=288, idF=256, cB=48, pw=192, AB0=768, AB1=768,
-                         col=96, colD=288, selL=144, selA0=144, selA1=144, yb=48, mN=96)),
+        ("bfloat16", dict(D0=WX, DB=WB, NB=2 * J + O - LO, fvS=96, F16=1536, Gs=768, X=128, Ex=104, Tm=512, Z=288,
+                          ident=272, ind=8, SF=288, Dg=96, CF=288, KA=112, KB=336, yb=48, idS=768, one=48, sg=288,
+                          bdH=896, MK=144, sn=96, SV0=288, SV1=288, SV2=288, SV3=288, RV0=288, RV1=288, RV2=288)),
+        ("float32", dict(detF=O + 48, Pf=96, Py=96, cw=480, K=24, c=144, xc=144, hi=256, I2=104, I4=32, bd=384, cv=48, KT=336,
+                         dum=12, MC=12, M=336, rk=112, nm=144, rs=288, S2=288, idF=256, cB=48, pw=192, AB0=768, AB1=768, ABu=768, lw=148,
+                         col=96, colD=288, selL=144, selA0=144, selA1=144, mN=192)),
         ("int32", dict(detI=O, pthI=96, pI=4)),
         ("uint16", dict(col16=96, site16=96, IL=12, ML0=12, ML1=12, RL=12, CL=12, A160=768, A161=768, cm=4))):
     for _n, _w in _bufs.items():
@@ -40,22 +45,29 @@ for _t in range(ST):
         SCRATCH["SO%d%d" % (_t, _g)] = ("sbuf", [128, 16], "uint16")
         if _t < ST - 1:
             SCRATCH["RO%d%d" % (_t, _g)] = ("sbuf", [128, 16], "uint16")
-for _n in ("P0", "P1", "P2", "Q0", "Q1", "F0", "F1", "PA"):
+for _n in ("P0", "P1", "P2", "F0", "F1", "PA"):
     SCRATCH[_n] = ("psum", [128, 512], "float32")
 
 SEMAPHORES = (["qv", "qs", "qp", "qg"] + ["dm%d" % i for i in range(24)] + ["ls%d" % i for i in range(18)]
-              + ["ar%d" % i for i in range(18)])
+              + ["ar%d" % i for i in range(18)] + [x + str(i) for x in ("ha", "hb", "hc", "hl") for i in range(ST - 1)])
 
-CY = 0.9e-3
-PC = 0.47e-3
-HOP = 0.22
-FX = 0.0
-BWL = 350e3
-GA = 1.45
-SC = 3.8
-RL0 = 1.2
+CY = np.array([0.95, 0.85, 1.0, 1.05, 1.2, 1.15]) * 1e-3
+PC = np.array([0.55, 0.5, 0.5, 0.6, 0.55, 0.65]) * CY
+GA = np.array([1.5, 1.3, 1.7, 1.4, 1.9, 1.2])
+SC = np.array([3.8, 3.8, 2.5, 5.5, 4.5, 3.0])
+HOP = np.array([0.28, 0.27, 0.22, 0.33, 0.3, 0.36])
+BWL = np.array([400.0, 400.0, 250.0, 300.0, 300.0, 450.0]) * 1e3
+BWR = np.array([80.0, 80.0, 50.0, 100.0, 60.0, 100.0]) * 1e3
+ROWS = np.array([0.5, 0.5, 0.8, 0.4, 0.6, 0.4])
+ISS = 0.25
+RL0 = 0.5
 BOOST = 8.0
 CB = 16.0
+
+
+def helper(T, rank, topo):
+    core, dst = T.cores[rank], T.cores[(rank - 1) % len(T.cores)]
+    return [c for c in topo.cores_of(core) if topo.die(c) != topo.die(core) and topo.may_write(c, dst)][0]
 
 
 def build(T, rank, topo, core):
@@ -67,24 +79,26 @@ def build(T, rank, topo, core):
     def op(eng, fn, r, w, dur, **k):
         d = dict(eng=eng, fn=fn, r=list(r), w=list(w), dur=dur, lat=0.0, sem=None, val=1, after=[], boost=bo[0])
         d.update(k)
+        d["durs"], d["lats"] = d["dur"] + 0 * CY, d["lat"] + 0 * CY
+        d["dur"], d["lat"] = float(d["durs"][0]), float(d["lats"][0])
         ops.append(d)
         return len(ops) - 1
 
-    def small(n, f=1.0):
-        return FX + max(64, n * f) * CY
+    def small(n, f=1.0, dur=None):
+        return max(64, n * f) * CY if dur is None else dur
 
     def ts(out, in0, s1, s2, o0, o1, r, w, n, f=1.0, dur=None):
         if o1 is None:
             fn = lambda g: g.vector.tensor_scalar(out, in0, s1, None, o0)
         else:
             fn = lambda g: g.vector.tensor_scalar(out, in0, s1, s2, o0, o1)
-        return op("v", fn, r, w, dur or small(n, f))
+        return op("v", fn, r, w, small(n, f, dur))
 
     def tt(out, a, b, o, r, w, n, f=2.0, dur=None):
-        return op("v", lambda g: g.vector.tensor_tensor(out, a, b, o), r, w, dur or small(n, f))
+        return op("v", lambda g: g.vector.tensor_tensor(out, a, b, o), r, w, small(n, f, dur))
 
     def cp(out, a, r, w, n, f=1.0, dur=None):
-        return op("v", lambda g: g.vector.tensor_copy(out, a), r, w, dur or small(n, f))
+        return op("v", lambda g: g.vector.tensor_copy(out, a), r, w, small(n, f, dur))
 
     def red(out, a, r, w, n):
         return op("v", lambda g: g.vector.tensor_reduce(out, a, AX.X, A.min), r, w, small(n))
@@ -101,7 +115,7 @@ def build(T, rank, topo, core):
             k["bias"] = bias
         if scale is not None:
             k["scale"] = scale
-        return op("s", lambda g: g.scalar.activation(out, a, fu, **k), r, w, dur or small(n))
+        return op("s", lambda g: g.scalar.activation(out, a, fu, **k), r, w, small(n, 1.0, dur))
 
     def aff(out, a, scale, bias, r, w, n):
         return act(out, a, AF.Identity, r, w, n, bias=bias, scale=scale)
@@ -125,6 +139,9 @@ def build(T, rank, topo, core):
             fn = lambda g: g.iota(out, pat, base, cmul)
         return op("g", fn, [], w, 0.13 + 2 * n * CY)
 
+    def conv(out, a, r, w, n):
+        return op("g", lambda g: g.affine_select(out, a, [[0, n]], A.is_ge, 0.0, 0, 0), r, w, 0.17 + 2 * n * CY)
+
     bw = [0.0]
 
     def dma(out, a, r, w, nbytes, queued=False):
@@ -132,8 +149,7 @@ def build(T, rank, topo, core):
         nd[0] += 1
         t = nbytes / BWL
         if queued:
-            bw[0] += t
-            t = bw[0]
+            t = bw[0] = bw[0] + t
         return op("y", lambda g: g.sync.dma_start(out, a), r, w, 0.08, lat=1.8 + t, sem=s, val=16,
                   chain="load" if queued else None)
 
@@ -146,10 +162,26 @@ def build(T, rank, topo, core):
         k = nr[0]
         nr[0] += 1
         ls, ar = "ls%d" % k, "ar%d" % k
-        i = op("g", lambda g: g.remote_dma(out, a, T.sem[ar], T.sem[ls], pid, rid, mask), r, [], 0.25,
-               lat=RL0 + nbytes / 80e3, sem=ls, val=neng, own=True)
-        op(None, None, [], [land], 0.0, lat=0.6, sem=ar, val=neng, after=[i])
+        i = op("g", lambda g: g.remote_dma(out, a, T.sem[ar], T.sem[ls], pid, rid, mask), r, [], ISS,
+               lat=RL0, sem=ls, val=neng, own=True)
+        op("d", None, [], [land], ROWS + nbytes / BWR, lat=0.4, sem=ar, val=neng, after=[i], chain="d")
         return i
+
+    def block(t, r):
+        hp = helper(T, rank, topo)
+        hrid, hpid, _ = topo.addr(hp)
+        eng = [e for e in topo.engines(core, hp) if e not in topo.engines(core, dst)]
+        h, half = O + S // 2, ROWS + 128 * S / BWR
+
+        def fn(g):
+            return g.remote_dma_fused(
+                [RemoteDMATransfer(dst_ids=[DstId(rid=rid, pnc=pid)], dma_engine_mask=mask, remote_sem=T.sem["hc%d" % t],
+                                   src=dw(t, O, h), dst=dw(t + 1, O, h)),
+                 RemoteDMATransfer(dst_ids=[DstId(rid=hrid, pnc=hpid)], dma_engine_mask=sum(1 << e for e in eng),
+                                   remote_sem=T.sem["ha%d" % t], src=dw(t, h, W), dst=dw(t + 1, h, W))], local_sem=T.sem["hl%d" % t])
+        i = op("g", fn, r, ["go%d" % t], ISS, lat=RL0, sem="hl%d" % t, val=neng + len(eng), own=True)
+        op("d", None, [], [Db[t + 1][0]], half, lat=0.4, sem="hc%d" % t, val=neng, after=[i], chain="d")
+        op("e", None, [], [Db[t + 1][1]], 2 * half, lat=1.5, sem="hb%d" % t, val=len(topo.engines(hp, dst)), after=[i])
 
     def gv(n):
         return 0.05 + n * GA * CY
@@ -163,18 +195,19 @@ def build(T, rank, topo, core):
     def dw(t, a, b):
         return T.D0[:, a:b] if t == 0 else T.DB[:, t * (J + WX) - WX + a:t * (J + WX) - WX + b]
 
-    def nw(t, a, b):
-        return T.N0[:, a:b] if t == 0 else T.NB[:, t * (J + WX) - WX + a:t * (J + WX) - WX + b]
+    def nw(a, b):
+        return T.NB[:, J + a:J + b]
 
     nown = len(NCH) - 1
     Do = [["D0o%d" % i for i in range(nown)]] + [["D%do" % t] for t in range(1, ST)]
-    No = [["N0o%d" % i for i in range(nown)]] + [["N%do" % t] for t in range(1, ST)]
-    Nb = [["N%db%d" % (t, q) for q in range(1 if NSEND else 4)] for t in range(ST)]
+    No = ["No%d" % i for i in range(nown)]
+    Nb = ["Nb%d" % q for q in range(4)]
     sct = [[]] + [["s0", "s1", "r0", "r1"]] * (ST - 1)
     Ds = [["D%d%s" % (t, x) for x in sct[t]] for t in range(ST)]
     Ns = [["N%d%s" % (t, x) for x in sct[t]] for t in range(ST)]
-    Dr = [Do[t] + ["D%db" % t, "D%dz" % t] + Ds[t] for t in range(ST)]
-    Nr = [No[t] + Nb[t] + Ns[t] for t in range(ST)]
+    Db = [["D0b"]] + [["D%db0" % t, "D%db1" % t] for t in range(1, ST)]
+    Dr = [Do[t] + Db[t] + ["D%dz" % t] + Ds[t] for t in range(ST)]
+    Nr = [No + Nb + Ns[t] for t in range(ST)]
     AB = [T.AB0, T.AB1]
     A16 = [T.A160, T.A161]
     PK = [T.P0, T.P1, T.P2]
@@ -192,15 +225,16 @@ def build(T, rank, topo, core):
     pf, pm, grp, i15, pe, po, ph, kz, k6, k12, k13, k15 = (K[:, i:i + 1] for i in range(12))
     iota(T.pI[:, 0:1], [[0, 1]], 0, 1, ["pI"], 1, False)
     iota(T.c[:], [[1, 144]], 0, 0, ["c"], 144)
-    iota(T.xc[:], [[0, 8], [1, 16]], 0, 0, ["xc"], 128)
+    iota(T.xc[:], [[0, 9], [1, 16]], 0, 0, ["xc"], 144)
     iota(T.hi[:], [[1, 16], [0, 16]], 0, 0, ["hi"], 256)
-    iota(T.I4[:, 0:6], [[0, 3], [16, 2]], 0, 0, ["I4a"], 6)
-    iota(T.I4[:, 6:10], [[0, 4]], 32, 0, ["I4b"], 4)
-    iota(T.I4[:, 12:21], [[-4096, 3], [0, 3]], 0, 0, ["I4c"], 9)
+    iota(T.I4[:, 0:4], [[0, 2], [16, 2]], 0, 0, ["I4a"], 4)
+    iota(T.I4[:, 4:6], [[0, 2]], 32, 0, ["I4b"], 2)
+    iota(T.I4[:, 12:18], [[-4096, 3], [0, 2]], 0, 0, ["I4c"], 6)
     iota(T.I2[:], [[1, 13], [0, 8]], 0, 0, ["I2"], 104)
-    iota(T.KT[:], [[4096, 3], [16, 14], [1, 8]], 0, 0, ["KT"], 336)
-    iota(T.KT[:, 104:336:112], [[4096, 3]], 240 - int(KS), 0, ["KT"], 3)
-    iota(T.x3[:], [[0, 8], [1, 16], [0, 3]], 0, 0, ["x3"], 384)
+    iota(T.KA[:], [[16, 14], [1, 8]], 0, 0, ["KA"], 112)
+    iota(T.KA[:, 104:105], [[0, 1]], 240, 0, ["KA"], 1)
+    iota(T.KT[:], [[4096, 3], [0, 112]], 0, 0, ["KT"], 336)
+    iota(T.KT[:, 104:336:112], [[4096, 3]], -int(KS), 0, ["KT"], 3)
     for t in range(ST):
         iota(dw(t, W, WX), [[0, 16]], 0, 0, ["D%dz" % t], 16)
     cp(pf, T.pI[:, 0:1], ["pI"], ["pf"], 1)
@@ -220,19 +254,19 @@ def build(T, rank, topo, core):
     for t in range(ST - 1):
         for gi in range(2):
             ms(T["SO%d%d" % (t, gi)][:], 0, ["SO%d%d%d" % (t, gi, i) for i in range(6)], 16)
-    ts(T.CL[:, 0:10], T.I4[:, 0:10], pm, None, A.add, None, ["I4a", "I4b", "pm"], ["CL"], 10)
+    ts(T.CL[:, 0:6], T.I4[:, 0:6], pm, None, A.add, None, ["I4a", "I4b", "pm"], ["CL"], 6)
     ts(T.ind[:], T.c[:, 0:8], grp, None, A.is_equal, None, ["c", "grp"], ["ind"], 8)
     ts(T.Z[:, 0:144], T.c[:], kz, KS, A.is_equal, A.mult, ["c", "kz"], ["Z0"], 144)
     aff(T.Z[:, 144:288], T.Z[:, 0:144], -1.0, None, ["Z0"], ["Z1"], 144)
     ts(T.Ex[:], T.I2[:], pm, -KS, A.is_equal, A.mult, ["I2", "pm"], ["Ex"], 104)
     aff(k13, pm, 256.0, None, ["pm"], ["k13"], 1)
-    aff(T.KT[:], T.KT[:], None, k13, ["KT", "k13"], ["KT"], 336)
+    aff(T.KB[:], T.KT[:], None, k13, ["KT", "k13"], ["KB"], 336)
     ts(T.Tm[:, 0:256], T.hi[:], pm, None, A.is_equal, None, ["hi", "pm"], ["TmR"], 256)
-    ts(T.Tm[:, 256:384], T.xc[:], ph, None, A.is_equal, None, ["xc", "ph"], ["TmK0"], 128)
+    ts(T.Tm[:, 256:384], T.xc[:, 0:128], ph, None, A.is_equal, None, ["xc", "ph"], ["TmK0"], 128)
     act(T.Tm[:, 384:512], T.Tm[:, 256:384], AF.Copy, ["TmK0"], ["TmK1"], 128)
     TmR, TmK = T.Tm[:, 0:256], T.Tm[:, 256:512]
-    idp, idn = T.ident[:, 0:128], T.ident[:, 128:256]
-    ts(idp, T.c[:, 0:128], pf, None, A.is_equal, None, ["c", "pf"], ["idp"], 128)
+    up, idp, idn = T.ident[:, 0:128], T.ident[:, 1:129], T.ident[:, 144:272]
+    ts(T.ident[:, 0:129], T.c[:, 0:129], -1.0, pf, A.add, A.is_equal, ["c", "pf"], ["idp"], 129)
     aff(idn, idp, -1.0, None, ["idp"], ["idn"], 128)
     aff(T.idF[:, 0:128], idp, None, None, ["idp"], ["idF0"], 128)
     aff(T.idF[:, 128:256], idp, -1.0, None, ["idp"], ["idF1"], 128)
@@ -242,37 +276,37 @@ def build(T, rank, topo, core):
         aff(T.idS[:, 256 + 128 * t:384 + 128 * t], idp, -16384.0 - (rank + t) % len(T.cores) * S / 2, None, ["idp"],
             ["idS%d" % (2 + t)], 128)
     aff(T.one[:], T.c[:, 0:48], 0.0, 1.0, ["c"], ["one"], 48)
-    bd = [T.bd[:, 128 * i:128 * i + 128] for i in range(4)]
-    bdH = [T.bdH[:, 128 * i:128 * i + 128] for i in range(4)]
+    bd = [T.bd[:, 128 * i:128 * i + 128] for i in range(3)]
+    bdH = [T.bdH[:, 128 * i:128 * i + 128] for i in range(7)]
     ts(bd[0], T.hi[:, 0:128], grp, None, A.is_equal, None, ["hi", "grp"], ["bd0"], 128)
     aff(bd[1], bd[0], pe, None, ["bd0", "pe"], ["bd1"], 128)
     aff(bd[2], bd[0], po, None, ["bd0", "po"], ["bd2"], 128)
-    aff(k15, i15, -16.0, None, ["i15"], ["k15"], 1)
-    aff(bd[3], bd[0], k15, None, ["bd0", "k15"], ["bd3"], 128)
+    aff(k15, i15, -KS, None, ["i15"], ["k15"], 1)
+    aff(bdH[4], bd[0], k15, None, ["bd0", "k15"], ["bdH4"], 128)
+    for i in (1, 2):
+        aff(bdH[4 + i], bd[i], None, None, ["bd%d" % i], ["bdH%d" % (4 + i)], 128)
     for i in range(3):
         aff(bdH[i], bd[i], -float(AL), None, ["bd%d" % i], ["bdH%d" % i], 128)
     aff(bdH[3], bd[0], -KS, None, ["bd0"], ["bdH3"], 128)
-    ms(T.qm[:], 0.0, ["qm"], 384, 0.5)
-    for u in (0, 3, 7):
-        ts(T.qm[:, 48 * u:48 * u + 48], T.x3[:, 0:48], pm, 16384.0, A.is_le, A.mult, ["x3", "pm"], ["qm"], 48)
-    ts(T.qm[:, 192:288], T.x3[:, 0:96], pm, 16384.0, A.not_equal, A.mult, ["x3", "pm"], ["qm"], 96)
-    ms(T.rs[:], 0.0, ["rs"], 288)
-    for sl in (slice(0, 96, 16), slice(96, 240, 48), slice(240, 288, 16)):
-        ms(T.rs[:, sl], 2.0 ** 25, ["rs"], 8)
-    for a, b, src, nme, cst in ((0, 96, T.xc, "xc", CO + LO + AL), (96, 240, T.x3, "x3", 16384.0), (240, 288, T.xc, "xc", CO + LO + AL)):
-        ts(T.CF[:, a:b], src[:, 0:b - a], pm, 2.0 ** 22, A.not_equal, A.mult, [nme, "pm"], ["CF%d" % a], b - a)
-        aff(T.CF[:, a:b], T.CF[:, a:b], None, cst, ["CF%d" % a], ["CF%d" % a], b - a)
-    ts(T.t1[:], T.c[:, 0:128], -1.0, pf, A.add, A.is_equal, ["c", "pf"], ["t1"], 128)
-    tt(T.t2[:], T.t1[:], idp, A.subtract, ["t1", "idp"], ["t2"], 128)
-    ts(T.t3[:], T.xc[:], 1.0, 0.5, A.is_ge, A.mult, ["xc"], ["t3"], 128)
-    tt(T.Sh[:], T.t2[:], T.t3[:], A.mult, ["t2", "t3"], ["Sh"], 128)
+    aff(T.qm[:, :, 0:16], T.c[:, 0:48], 0.0, CV, ["c"], ["qm0"], 48)
+    aff(T.qm[:, :, 48:80], T.c[:, 0:96], 0.0, CV, ["c"], ["qm3"], 96)
+    ts(T.cw[:, 192:288], T.xc[:, 0:96], pm, None, A.is_le, None, ["xc", "pm"], ["cw10", "cw11"], 96)
+    aff(T.qm[:, :, 16:48], T.cw[:, 192:288], KS - CV, CV, ["cw10", "cw11"], ["qm1"], 96)
+    aff(T.qm[:, :, 80:96], T.cw[:, 192:240], KS - CV, CV, ["cw10", "cw11"], ["qm5"], 48)
+    qmr = ["qm%d" % u for u in (0, 1, 3, 5)]
+    iota(T.rs[:], [[0, 288]], 0, 0, ["rs"], 288)
+    for sl, n_ in ((slice(0, 96, 16), 6), (slice(96, 240, 48), 3), (slice(240, 288, 16), 3)):
+        iota(T.rs[:, sl], [[0, n_]], 16000000, 0, ["rs"], n_)
+    ts(T.cw[:, 0:144], T.xc[:], pm, None, A.not_equal, None, ["xc", "pm"], ["cw00", "cw01"], 144)
+    for a, b, cst in ((0, 96, CV), (96, 240, 16384), (240, 288, CV)):
+        aff(T.CF[:, a:b], T.cw[:, 0:b - a], 2.0 ** 22 - cst, float(cst), ["cw00", "cw01"], ["CF%d" % a], b - a)
     aff(k12, pm, -256.0, None, ["pm"], ["k12"], 1)
-    aff(T.MC[:, 0:9], T.I4[:, 12:21], None, k12, ["I4c", "k12"], ["MC"], 9)
-    ms(T.rk[:], 0.0, ["rk"], 112)
-    for i, v_ in ((0, 2.0 ** 25), (105, RC), (106, -RC)):
-        ms(T.rk[:, i:i + 1], v_, ["rk"], 1)
-    for b in range(3):
-        ms(T.KT[:, 112 * b + 105:112 * b + 112], 4 * RC, ["KT"], 7)
+    aff(T.MC[:, 0:6], T.I4[:, 12:18], None, k12, ["I4c", "k12"], ["MC"], 6)
+    iota(T.rk[:], [[0, 112]], 0, 0, ["rk"], 112)
+    iota(T.rk[:, 0:1], [[0, 1]], 16000000, 0, ["rk"], 1)
+    for i, v_ in ((105, RC), (106, -RC)):
+        aff(T.rk[:, i:i + 1], pf, 0.0, v_, ["rk", "pf"], ["rk%d" % i], 1)
+    aff(T.KA[:, 105:112], T.c[:, 0:7], 0.0, 4 * RC, ["KA", "c"], ["KA1"], 7)
     aff(T.dum[:, 0:9], T.c[:, 0:9], 16.0, pm, ["c", "pm"], ["dum"], 9)
 
     bo[0] = 0.0
@@ -280,23 +314,39 @@ def build(T, rank, topo, core):
     ts(T.Py[:], T.pthI[:], -CO, None, A.add, None, ["pthI"], ["Py"], 96)
     tt(T.Pf[:], T.Py[:], T.pw[:, 0:96], A.add, ["Py", "pwA", "pwB"], ["P0", "P1"], 96)
     for i in range(DETCH):
-        cp(T.detF[:, i * cw:(i + 1) * cw], T.detI[:, i * cw:(i + 1) * cw], ["detI%d" % i], ["detF%d" % i], cw)
+        (cp if i else conv)(T.detF[:, i * cw:(i + 1) * cw], T.detI[:, i * cw:(i + 1) * cw], ["detI%d" % i], ["detF%d" % i], cw)
     detr = ["detF%d" % i for i in range(DETCH)] + ["detFx"]
-    for (a, b, e), dn_, nn in zip(NCH, [["D0b"]] + [[x] for x in Do[0]], [Nb[0]] + [[x] for x in No[0]]):
-        if e == "s":
-            act(T.N0[:, a:b], T.D0[:, a:b], AF.Relu, dn_, nn, b - a, scale=-1.0)
-        else:
-            ts(T.N0[:, a:b], T.D0[:, a:b], -1.0, 0.0, A.mult, A.max, dn_, nn, b - a, 0.5)
+    for (a, b, e), dn_, nn in zip(NCH, [["D0b"]] + [[x] for x in Do[0]], [Nb] + [[x] for x in No]):
+        w_ = (b - a) // len(e)
+        for i, e_ in enumerate(e):
+            a_, wn = a + i * w_, nn[i * len(nn) // len(e):(i + 1) * len(nn) // len(e)]
+            if e_ == "s":
+                act(nw(a_, a_ + w_), T.D0[:, a_:a_ + w_], AF.Relu, dn_, wn, w_, scale=-1.0)
+            else:
+                ts(nw(a_, a_ + w_), T.D0[:, a_:a_ + w_], -1.0, 0.0, A.mult, A.max, dn_, wn, w_, 0.5)
     for r_ in range(16):
-        cp(T.F16[:, r_:1536:16], T.fvS[:], ["fv"], ["F16%d" % r_], 96, 0.5)
+        if r_ % 2:
+            cp(T.F16[:, r_:1536:16], T.fvS[:], ["fv"], ["F16%d" % r_], 96, 0.5)
+        else:
+            act(T.F16[:, r_:1536:16], T.fvS[:], AF.Copy, ["fv"], ["F16%d" % r_], 96)
     F16r = ["F16%d" % r_ for r_ in range(16)]
+    o_ = 0
+    for m in range(2):
+        for gr in GROUPS:
+            w_ = 16 * len(gr["bs"])
+            for ty in range(3):
+                f0 = 48 * m + 16 * gr["bs"][0]
+                mm(T.F0[:, o_:o_ + w_], idp if ty else idn, T.fvS[:, f0:f0 + w_], True, True, ["idp", "idn", "fv"], ["ps:F0"], 64)
+                o_ += w_
+    act(T.SF[:], T.F0[:, 0:288], AF.Copy, ["ps:F0"], ["SF"], 288)
 
     def first_empty(m):
         p, pn = T.Pf[:, 48 * m:48 * m + 48], "P%d" % m
         ne = T.ne[:, 48 * m:48 * m + 48]
         act(ne, p, AF.Sign, [pn], ["ne%d" % m], 48, bias=EMPTY / 2, scale=-1.0)
-        mm(T.PA[:, 96:144], T.Sh[:], ne, True, True, ["Sh", "ne%d" % m], ["ps:PA"], 64)
-        act(T.mN[:, 48 * m:48 * m + 48], T.PA[:, 96:144], AF.Copy, ["ps:PA"], ["mN%d" % m], 48)
+        mm(T.PA[:, 96:144], up, ne, True, False, ["idp", "ne%d" % m], ["ps:PA"], 64)
+        mm(T.PA[:, 96:144], idn, ne, False, True, ["idn", "ne%d" % m], ["ps:PA"], 64)
+        act(T.mN[:, 96 * m + 48:96 * m + 96], T.PA[:, 96:144], AF.Relu, ["ps:PA"], ["mN%d" % m], 48, scale=0.5)
 
     def lists(t):
         m = t % 2
@@ -320,17 +370,29 @@ def build(T, rank, topo, core):
         mm(q, T.idF[:, 0:128], col, True, False, ["idF0", "col%d" % m], ["ps:PA"], 256)
         mm(q, T.idS[:, 128:256], T.one[:], False, False, ["idS1", "one"], ["ps:PA"], 64)
         mm(q, T.idS[:, 128:256], sg[2], False, True, ["idS1", n[2]], ["ps:PA"], 64)
-        ts(T.site16[:, 48 * m:48 * m + 48], q, CO, None, A.add, None, ["ps:PA"], ["site%d" % m], 48)
-        ts(T.col16[:, 48 * m:48 * m + 48], col, CO, float(W), A.add, A.min, ["col%d" % m], ["c16%d" % m], 48)
+        if t:
+            u_ = [T.lw[:, 48 * i:48 * i + 48] for i in range(3)]
+            aff(u_[0], q, None, CO, ["ps:PA"], ["lw0"], 48)
+            conv(T.site16[:, 48 * m:48 * m + 48], u_[0], ["lw0"], ["site%d" % m], 48)
+            act(u_[1], col, AF.Relu, ["col%d" % m], ["lw1"], 48, bias=W - CO, scale=-1.0)
+            aff(u_[2], u_[1], -1.0, float(W), ["lw1"], ["lw2"], 48)
+            conv(T.col16[:, 48 * m:48 * m + 48], u_[2], ["lw2"], ["c16%d" % m], 48)
+        else:
+            ts(T.site16[:, 48 * m:48 * m + 48], q, CO, None, A.add, None, ["ps:PA"], ["site%d" % m], 48)
+            ts(T.col16[:, 48 * m:48 * m + 48], col, CO, float(W), A.add, A.min, ["col%d" % m], ["c16%d" % m], 48)
         for b in range(3):
             src = T.detF[:, 0:O + 48].indirect(T.site16[:, 48 * m + 16 * b:48 * m + 16 * b + 16])
             act(AB[m][:, 256 * b:256 * b + 256], src, AF.Identity, detr + ["site%d" % m], ["AB%d%d" % (m, b)], 0, bias=-CO, dur=gs(256))
             if t == 0 and b == 0:
                 cp(A16[m][:, 256 * b:256 * b + 256], src, detr + ["site%d" % m], ["A16%d%d" % (m, b)], 0, dur=gv(256))
+            elif t:
+                u_ = T.ABu[:, 256 * b:256 * b + 256]
+                aff(u_, AB[m][:, 256 * b:256 * b + 256], None, CO, ["AB%d%d" % (m, b)], ["ABu%d" % b], 256)
+                conv(A16[m][:, 256 * b:256 * b + 256], u_, ["ABu%d" % b], ["A16%d%d" % (m, b)], 256)
             else:
                 ts(A16[m][:, 256 * b:256 * b + 256], AB[m][:, 256 * b:256 * b + 256], CO, None, A.add, None, ["AB%d%d" % (m, b)],
                    ["A16%d%d" % (m, b)], 256)
-        act(T.colD[:, 144 * m:144 * m + 144], col.indirect(T.CL[:, 0:9]), AF.Copy, ["col%d" % m, "CL"], ["colD%d" % m], 0, dur=gs(144))
+        act(T.colD[:, 96 * m:96 * m + 96], col.indirect(T.CL[:, 0:6]), AF.Copy, ["col%d" % m, "CL"], ["colD%d" % m], 0, dur=gs(96))
         first_empty(m)
 
     lists(0)
@@ -342,22 +404,15 @@ def build(T, rank, topo, core):
         R = 12 + t // 2
         last = t == ST - 1
         SV, ML, selA = T["SV%d" % t], T["ML%d" % m], T["selA%d" % m]
-        DG, NG = dw(t, 0, WX), nw(t, 0, W)
+        DG, NG = dw(t, 0, WX), nw(0, W)
         if not last:
-            if NSEND:
-                remote(nw(t + 1, O, W), nw(t, O, W), Nb[t] + Ns[t] + (Do[0] if t == 0 else []), Nb[t + 1][0], 256 * S)
-            remote(dw(t + 1, O, W), dw(t, O, W), ["D%db" % t] + Ds[t] + (Do[0] if t == 0 else []), "D%db" % (t + 1),
-                   256 * S * (1 + NSEND))
-            dma(nw(t + 1, 0, O), nw(t, 0, O), No[t] + Ns[t], No[t + 1], 256 * O)
-            dma(dw(t + 1, 0, O), dw(t, 0, O), Do[t] + Ds[t], Do[t + 1], 256 * O)
-            for q in range(0 if NSEND else 4):
-                out, src = nw(t + 1, O + 512 * q, O + 512 * q + 512), dw(t + 1, O + 512 * q, O + 512 * q + 512)
-                if NQ[q] == "s":
-                    act(out, src, AF.Relu, ["D%db" % (t + 1)], [Nb[t + 1][q]], 512, scale=-1.0)
-                else:
-                    ts(out, src, -1.0, 0.0, A.mult, A.max, ["D%db" % (t + 1)], [Nb[t + 1][q]], 512, 0.5)
+            block(t, Db[t] + Ds[t][2:] + (Do[0] if t == 0 else []))
+            dma(dw(t + 1, 0, O), dw(t, 0, O), Do[t] + Ds[t] + ["go%d" % t], Do[t + 1], 256 * O)
+            ops[-1]["lats"] = ops[-1]["lats"] + 128 * S / BWR
+            ops[-1]["lat"] = float(ops[-1]["lats"][0])
         else:
-            dma(nw(1, 0, W), dw(t, 0, W), Dr[t], Nr[1], 256 * W)
+            dma(dw(1, 0, W), dw(t, 0, W), Dr[t], Dr[1], 256 * W)
+        late = []
         bo[0] = BOOST
         tt(T.tmp[:], DG.indirect(T.col16[:, 48 * m:48 * m + 48]), T.F16[:, 768 * m:768 * m + 768], A.min,
            Dr[t] + ["c16%d" % m] + F16r, ["tmp"], 0, dur=gv(768))
@@ -370,7 +425,7 @@ def build(T, rank, topo, core):
                     j = 16 * b + x
                     ins = g.tensor.matmul(T.F1[32 * b:32 * b + w_, x:128:16], T.Gs[:, 16 * j:16 * j + w_], T.ind[:], True, True)
                 return ins
-            op("p", subs, ["Gs", "ind"], ["ps:F1"], 16 * 40 * PC)
+            op("p", subs, ["Gs", "ind"], ["ps:F1"], 16 * w_ * PC)
         act(T.X[0:80, :], T.F1[0:80, 0:128], AF.Copy, ["ps:F1"], ["X"], 128)
         onv = [(j % 16 < NV[t][j // 16]) if j // 16 == 1 else (j % 16 >= 16 - NV[t][j // 16]) for j in range(48)]
         for gi, gr in enumerate(GROUPS):
@@ -378,7 +433,8 @@ def build(T, rank, topo, core):
             nb = len(bs)
             for b in bs:
                 pk, key = "ps:P%d" % b, (t, b)
-                mm(PK[b][:, 0:112], T.idF[:, 0:128], T.KT[:, 112 * b:112 * b + 112], True, False, ["idF0", "KT"], [pk], 448)
+                mm(PK[b][:, 0:112], idp, T.KA[:], True, False, ["idp", "KA", "KA1"], [pk], 112)
+                acc([(PK[b][:, 0:112], idp, T.KB[:, 112 * b:112 * b + 112])], key, ["idp", "KB"], [pk], 112)
                 acc([(PK[b][:, 0:8 * R], T.X[32 * b:32 * b + 16, :], T.Ex[32 * b:32 * b + 16, 0:8 * R])], key, ["X", "Ex"], [pk], 8 * R)
                 for x in range(16):
                     j = 16 * b + x
@@ -395,10 +451,10 @@ def build(T, rank, topo, core):
                     acc([(PK[b][:, 0:8 * R], z, T.G[:, j, h:16 * R:2]) for h in range(2)], key, ["G%d" % j, "Z0", "Z1"], [pk], 16 * R)
                 o_ = 112 * b
                 mb = T.M[:, o_ + 104:o_ + 105]
-                scan(T.M[:, o_:o_ + 109], T.rk[:, 0:109], PK[b][:, 0:109], ["rk", pk], ["m%d" % b], 109)
-                ts(ML[:, LCOL[b]], T.MC[:, 3 * b:3 * b + 3], mb, T.M[:, o_ + 106:o_ + 107], A.add, A.subtract,
+                scan(T.M[:, o_:o_ + 108], T.rk[:, 0:108], PK[b][:, 0:108], ["rk", "rk105", "rk106", pk], ["m%d" % b] + ["free"] * (b == 2), 108)
+                ts(ML[:, LCOL[b]], T.MC[:, 2 * b:2 * b + 2], mb, T.M[:, o_ + 106:o_ + 107], A.add, A.subtract,
                    ["MC", "m%d" % b], ["ML%d%d" % (m, b)], 3)
-                ts(T.IL[:, LCOL[b]], T.M[:, o_ + 106:o_ + 109], mb, -0.0625, A.subtract, A.mult, ["m%d" % b], ["IL%d" % b], 3)
+                ts(T.IL[:, LCOL[b]], T.M[:, o_ + 106:o_ + 108], mb, -0.0625, A.subtract, A.mult, ["m%d" % b], ["IL%d" % b], 3)
             n0, n1, n = 16 * c0, 16 * c1, 16 * (c1 - c0)
             e0, e1 = 16 * d0, 16 * (d0 + nb)
             h0, h1, hn = 48 * bs[0], 48 * (bs[-1] + 1), 48 * nb
@@ -406,60 +462,61 @@ def build(T, rank, topo, core):
             sl, sa = "selL%d" % gi, "selA%d%d" % (m, gi)
             Qp, Fp, qn, fn_ = T["Q%d" % gi], T["F%d" % gi], "ps:Q%d" % gi, "ps:F%d" % gi
             act(T.MK[:, n0:n1], TmK.indirect(ML[:, c0:c1]), AF.Copy, ["TmK0", "TmK1"] + MLr, ["MK%d" % gi], 0, dur=gs(n))
-            tt(T.selL[:, n0:n1], TmR.indirect(ML[:, c0:c1]), T.colD[:, 144 * m + n0:144 * m + n1], A.mult,
+            tt(T.selL[:, n0:n1], TmR.indirect(ML[:, c0:c1]), T.colD[:, 96 * m + n0:96 * m + n1], A.mult,
                ["TmR", "colD%d" % m] + MLr, [sl], 0, dur=gv(n))
             tt(selA[:, n0:n1], AB[m][:, 0:768].indirect(T.IL[:, c0:c1]), T.MK[:, n0:n1], A.mult,
                ["AB%d%d" % (m, b) for b in range(3)] + ["IL%d" % b for b in bs] + ["MK%d" % gi], [sa], 0, dur=gv(n))
             srcs = [(T.selL, sl), (selA, sa), (selA, sa)]
-            mm(Qp[:, 0:3 * n], idp, T.qm[:, 3 * n0 - 48 * gi:3 * n1 - 48 * gi], True, False, ["idp", "qm"], [qn], 3 * n)
+            v0, k0, f0 = gr["v0"], gr["k0"], gr["f0"]
+            Dp, dn_ = PK[1 + gi], "ps:P%d" % (1 + gi)
+            mm(Dp[:, 128:128 + hn], idp, T.CF[:, 0:hn], True, False, ["idp", "CF0"], [dn_], max(64, hn))
             for ty, (s_, sn_) in enumerate(srcs):
-                mm(Qp[:, ty:3 * n:3], bd[ty], s_[:, n0:n1], False, ty == 2, ["bd%d" % ty, sn_], [qn], 4 * max(64, n))
-            u0 = 3 * (e0 - n0)
-            for ty in range(3):
-                scan(T.nm[:, h0 + 16 * nb * ty:h0 + 16 * nb * (ty + 1)], T.rs[:, 0:16 * nb], Qp[:, u0 + ty:u0 + hn:3], ["rs", qn],
-                     ["nm%d%d" % (gi, ty)], 16 * nb)
-            nmr = ["nm%d%d" % (gi, ty) for ty in range(3)]
+                mm(Dp[:, 128 + 16 * nb * ty:128 + 16 * nb * (ty + 1)], bd[ty], s_[:, e0:e1], False, ty == 2, ["bd%d" % ty, sn_], [dn_], 256)
+            mm(Qp[:, 0:3, 0:n], idp, T.qm[:, :, n0:n1], True, False, ["idp"] + qmr, [qn], 3 * n)
+            for ty, (s_, sn_) in enumerate(srcs):
+                mm(Qp[:, ty, 0:n], bd[ty], s_[:, n0:n1], False, ty == 2, ["bd%d" % ty, sn_], [qn], 256)
+            scan(T.nm[:, h0:h1], T.rs[:, 0:hn], Dp[:, 128:128 + hn], ["rs", dn_], ["nm%d" % gi], hn)
+            nmr = ["nm%d" % gi]
             l0 = 6 * gi
-            ts(T.RL[:, l0:l0 + 3 * nb], T.nm[:, h0 + 15:h1:16], CO, float(W), A.add, A.min, nmr, ["RL%d" % gi], 6)
-            act(T.Dg[:, h0:h1], DG.indirect(T.RL[:, l0:l0 + 3 * nb]), AF.Copy, Dr[t] + ["RL%d" % gi], ["Dg%d" % gi], 0, dur=gs(hn))
-            pv, pvn = PK[gi][:, 128:128 + hn], "ps:P%d" % gi
-            mm(pv, idp, T.Dg[:, h0:h1], True, False, ["idp", "Dg%d" % gi], [pvn], max(64, hn))
-            for ty in range(3):
-                mm(PK[gi][:, 128 + 16 * nb * ty:128 + 16 * nb * (ty + 1)], idp if ty else idn,
-                   T.fvS[:, 48 * m + 16 * bs[0]:48 * m + 16 * bs[0] + 16 * nb], False, ty == 2, ["idp", "idn", "fv"], [pvn], 64)
+            ts(T.RL[:, l0:l0 + 3 * nb], T.nm[:, h0 + 15:h1:16], CO - CV, float(W), A.add, A.min, nmr, ["RL%d" % gi], 6)
             svd, svn = SV[:, 2 * h0:2 * h0 + hn], SV[:, 2 * h0 + hn:2 * h1]
             vd, vn = "SVd%d%d" % (t, gi), "SVn%d%d" % (t, gi)
+            sf, src = T.SF[:, 144 * m + h0:144 * m + h1], DG.indirect(T.RL[:, l0:l0 + 3 * nb])
+            if gi:
+                tt(svd, src, sf, A.add, Dr[t] + ["RL1", "SF"], [vd], 0, dur=gv(hn))
+            else:
+                act(T.Dg[:], src, AF.Copy, Dr[t] + ["RL0"], ["Dg"], 0, dur=gs(hn))
+                mm(T.P0[:, 128:128 + hn], idp, T.Dg[:], True, False, ["idp", "Dg"], ["ps:P0"], hn)
+                mm(T.P0[:, 128:128 + hn], idp, sf, False, True, ["idp", "SF"], ["ps:P0"], hn)
+                act(svd, T.P0[:, 128:128 + hn], AF.Copy, ["ps:P0"], [vd], hn)
             if not last:
-                act(svn, pv, AF.Relu, [pvn], [vn], hn, scale=-1.0)
-            act(svd, pv, AF.Copy, [pvn], [vd], hn)
-            v0, k0, f0 = gr["v0"], gr["k0"], gr["f0"]
-            mm(Fp[:, 0:2 * hn], T.idF[:, 0:128], T.CF[:, f0:f0 + 2 * hn], True, False, ["idF0", "CF0", "CF96", "CF240"], [fn_], 8 * hn)
+                act(svn, svd, AF.Relu, [vd], [vn], hn, scale=-1.0)
+            mm(Fp[:, 0:2 * hn], idp, T.CF[:, f0:f0 + 2 * hn], True, False, ["idp", "CF0", "CF96", "CF240"], [fn_], 2 * hn)
             for ty, (s_, sn_) in enumerate(srcs):
                 mm(Fp[:, v0 + 16 * nb * ty:v0 + 16 * nb * (ty + 1)], bd[ty], s_[:, e0:e1], False, False, ["bd%d" % ty, sn_], [fn_], 256)
-            mm(Fp[:, k0:k0 + hn:3], bd[3], T.selL[:, e0:e1], False, False, ["bd3", sl], [fn_], 256)
-            sgA = T.sn[:, 48 + e0 - 64:48 + e1 - 64]
+            sgA = T.sn[:, 48 + e0 - 32:48 + e1 - 32]
             act(sgA, selA[:, e0:e1], AF.Sign, [sa], ["snA%d" % gi], 32)
+            sgL = T.sn[:, e0 - 32:e1 - 32]
+            act(sgL, T.selL[:, e0:e1], AF.Sign, [sl], ["snL%d" % gi], 32)
+            for i in range(nb):
+                mm(Fp[:, k0 + 48 * i:k0 + 48 * i + 16], bdH[4], T.sn[:, e0 - 32 + 16 * i:e0 - 16 + 16 * i], False, False,
+                   ["bdH4", "snL%d" % gi], [fn_], 64)
             if not last:
-                sgL = T.sn[:, e0 - 64:e1 - 64]
-                act(sgL, T.selL[:, e0:e1], AF.Sign, [sl], ["snL%d" % gi], 32)
                 for ty in range(3):
                     mm(Fp[:, v0 + 16 * nb * ty:v0 + 16 * nb * (ty + 1)], bdH[ty], sgA if ty else sgL, False, False,
                        ["bdH%d" % ty, ("snA%d" if ty else "snL%d") % gi], [fn_], 64)
-            cmpl = [(0, 0, 96, 0), (1, 144, 48, 48)] if gi == 0 else [(0, 48, 48, 0), (1, 48, 48, 0), (2, 96, 48, 0)]
-            eo = 432 * gi
+            cmpl = [(0, 2, 2, 0), (1, 1, 1, 1)] if gi == 0 else [(0, 0, 1, 0), (1, 0, 1, 0), (2, 1, 1, 0)]
+            eo = 27 * gi
             for ci, (bl, q0, w_, o_) in enumerate(cmpl):
                 for ty in range(3):
-                    gl = 0 if bl < 2 else 1
                     x_ = (32 * ty + 16 * bl + 15) if bl < 2 else (96 + 16 * ty + 15)
                     en = "E%d" % eo
-                    if eo + w_ > 768:
-                        eo = 0
-                        en = "E0"
-                    ts(T.E[:, eo:eo + w_], Qp[:, q0:q0 + w_], T.nm[:, x_:x_ + 1], None, A.is_equal, None, [qn, "nm%d%d" % (gl, ty)],
-                       ["E%d" % i for i in range(eo, eo + w_, 48)], w_)
-                    mm(Fp[:, k0 + o_:k0 + o_ + w_], bdH[3], T.E[:, eo:eo + w_], False, ci == len(cmpl) - 1 and ty == 2,
-                       ["bdH3"] + ["E%d" % i for i in range(eo, eo + w_, 48)], [fn_], max(64, w_))
-                    eo += w_
+                    ts(T.E[:, eo:eo + 3 * w_, :], Qp[:, 0:3, 16 * q0:16 * (q0 + w_)], T.nm[:, x_:x_ + 1], None, A.is_equal, None,
+                       [qn, "nm%d" % (bl // 2)], [en], 48 * w_)
+                    for i in range(w_):
+                        mm(Fp[:, k0 + 48 * (o_ + i):k0 + 48 * (o_ + i + 1)], bdH[3], T.E[:, eo + i:eo + 3 * w_:w_, :], False,
+                           ci == len(cmpl) - 1 and ty == 2, ["bdH3", en], [fn_], 64)
+                    eo += 3 * w_
             scan(T.S2[:, f0:f0 + 2 * hn], T.rs[:, f0:f0 + 2 * hn], Fp[:, 0:2 * hn], ["rs", fn_], ["S2%d" % gi], 2 * hn)
             SO = T["SO%d%d" % (t, gi)]
             SOr = ["SO%d%d%d" % (t, gi, i) for i in range(3 * nb)]
@@ -470,45 +527,58 @@ def build(T, rank, topo, core):
                    [SOr[i]], 1)
             so = SO[:, 0:3 * nb]
             if last:
-                cp(nw(1, -LO - AL, W).indirect(so), svd, SOr + [vd] + No[1], ["fin%d" % gi], 0, dur=sc(hn))
-                ops[-1]["turn"] = "N"
+                cp(dw(1, -LO - AL, W).indirect(so), svd, SOr + [vd] + Do[1], ["fin%d" % gi], 0, dur=sc(hn))
+                ops[-1]["turn"] = "D"
                 continue
             RV, RO = T["RV%d" % t], T["RO%d%d" % (t, gi)]
             rv, ro = "RV%d%d" % (t, gi), "RO%d%d" % (t, gi)
-            remote(RV[:, 2 * h0:2 * h1], SV[:, 2 * h0:2 * h1], [vd, vn], rv, 512 * hn)
+            remote(RV[:, 2 * h0:2 * h0 + hn], svd, [vd], rv, 256 * hn)
             remote(RO[:], SO[:], SOr, ro, 128 * 32)
+            act(RV[:, 2 * h0 + hn:2 * h1], RV[:, 2 * h0:2 * h0 + hn], AF.Relu, [rv], [rv + "n"], hn, scale=-1.0)
             bo[0] = 0.0
-            cp(nw(t + 1, -J, O).indirect(so), svn, SOr + [vn] + No[t + 1], [Ns[t + 1][gi]], 0, dur=sc(hn))
+            cp(nw(-J, O).indirect(so), svn, SOr + [vn, "free"], [Ns[t + 1][gi]], 0, dur=sc(hn))
             cp(dw(t + 1, -J, O).indirect(so), svd, SOr + [vd] + Do[t + 1], [Ds[t + 1][gi]], 0, dur=sc(hn))
-            cp(nw(t + 1, -LO, J + O - LO).indirect(RO[:, 0:3 * nb]), RV[:, 2 * h0 + hn:2 * h1], [rv, ro] + No[t + 1] + Nb[t + 1],
-               [Ns[t + 1][2 + gi]], 0, dur=sc(hn))
+            cp(nw(-LO, J + O - LO).indirect(RO[:, 0:3 * nb]), RV[:, 2 * h0 + hn:2 * h1], [rv + "n", ro] + Nb, [Ns[t + 1][2 + gi]], 0,
+               dur=sc(hn))
             cp(dw(t + 1, -LO, J + O - LO).indirect(RO[:, 0:3 * nb]), RV[:, 2 * h0:2 * h0 + hn],
-               [rv, ro, "D%db" % (t + 1), "D%dz" % (t + 1)] + Do[t + 1] + Nb[t + 1], [Ds[t + 1][2 + gi]], 0, dur=sc(hn))
+               [rv, ro, "D%dz" % (t + 1)] + Db[t + 1] + Do[t + 1] + Nb, [Ds[t + 1][2 + gi]], 0, dur=sc(hn))
             for o_, b_ in zip(ops[-4:], "NDND"):
                 o_["turn"] = b_
+            late += ops[-4:]
+            del ops[-4:]
             bo[0] = BOOST
         bo[0] = 0.0
         if last:
-            dma(T.yd[:], nw(1, 0, W), ["fin0", "fin1"], [], 256 * W)
+            dma(T.yd[:], dw(1, 0, W), ["fin0", "fin1"], [], 256 * W)
+        else:
+            for q in range(4):
+                act(nw(O + 512 * q, O + 512 * q + 512), dw(t + 1, O + 512 * q, O + 512 * q + 512), AF.Relu,
+                    [Db[t + 1][q // 2]], [Nb[q]], 512, scale=-1.0)
+            ops.extend(late)
         p = T.Pf[:, 48 * m:48 * m + 48]
         pn = "P%d" % m
         pw = T.pw
         sar = ["selA%d0" % m, "selA%d1" % m]
-        ts(T.cm[:, 0:3], T.S2[:, 143:240:48], 0.0, None, A.is_gt, None, ["S20", "S21"], ["cm"], 3)
+        if last:
+            ts(T.cm[:, 0:3], T.S2[:, 143:240:48], 0.0, None, A.is_gt, None, ["S20", "S21"], ["cm"], 3)
+        else:
+            act(T.lw[:, 144:147], T.S2[:, 143:240:48], AF.Relu, ["S20", "S21"], ["lw3"], 3, scale=1.0 / 16384)
+            conv(T.cm[:, 0:3], T.lw[:, 144:147], ["lw3"], ["cm"], 3)
         act(T.cB[:], T.c[:, 0:16].indirect(T.cm[:, 0:3]), AF.Copy, ["c", "cm"], ["cB"], 0, dur=gs(48))
         act(T.yb[:], T.sn[:, 48:96], AF.Relu, ["snA0", "snA1"], ["yb"], 48, scale=float(B * S))
-        tt(pw[:, 0:48], TmR.indirect(ML[:, 4:7]), T.cB[:], A.mult, ["TmR", "cB"] + ["ML%d%d" % (m, b) for b in range(3)], ["pwA"], 0,
-           dur=gv(48))
-        tt(pw[:, 48:96], T.mN[:, 48 * m:48 * m + 48], T.cB[:], A.mult, ["mN%d" % m, "cB"], ["pwB"], 48)
+        act(T.mN[:, 96 * m:96 * m + 48], TmR.indirect(ML[:, 2:5]), AF.Copy, ["TmR"] + ["ML%d%d" % (m, b) for b in range(3)], ["mR%d" % m],
+            0, dur=gs(48))
         for h in range(2):
             o_ = T.PA[:, 48 * h:48 * h + 48]
-            mm(o_, bd[1 + h], selA[:, 64:112], True, False, ["bd%d" % (1 + h)] + sar, ["ps:PA"], 256)
-            mm(o_, bd[1 + h], T.yb[:], False, False, ["bd%d" % (1 + h), "yb"], ["ps:PA"], 256)
+            mm(o_, bd[1 + h], selA[:, 32:80], True, False, ["bd%d" % (1 + h)] + sar, ["ps:PA"], 256)
+            mm(o_, bdH[5 + h], T.yb[:], False, False, ["bdH%d" % (5 + h), "yb"], ["ps:PA"], 64)
             mm(o_, T.idF[:, 128:256], p, False, True, ["idF1", pn], ["ps:PA"], 256)
-        tt(pw[:, 96:192], T.PA[:, 0:96], pw[:, 0:96], A.mult, ["ps:PA", "pwA", "pwB"], ["pwU"], 96, 1.0)
-        mm(T.PA[:, 240:288], T.idF[:, 0:128], p, True, False, ["idF0", pn], ["ps:PA"], 256)
+        tt(pw[:, 0:96], T.PA[:, 0:96], T.mN[:, 96 * m:96 * m + 96], A.mult, ["ps:PA", "mR%d" % m, "mN%d" % m], ["pwA", "pwB"], 96, 1.0)
         for h in range(2):
-            mm(T.PA[:, 240:288], T.idF[:, 0:128], pw[:, 96 + 48 * h:144 + 48 * h], False, h == 1, ["idF0", "pwU"], ["ps:PA"], 256)
+            mm(T.PA[:, 192:240], T.idF[:, 0:128], pw[:, 48 * h:48 * h + 48], h == 0, h == 1, ["idF0", "pwA"], ["ps:PA"], 256)
+        tt(pw[:, 96:144], T.PA[:, 192:240], T.cB[:], A.mult, ["ps:PA", "cB"], ["pwU"], 48, 1.0)
+        mm(T.PA[:, 240:288], T.idF[:, 0:128], p, True, False, ["idF0", pn], ["ps:PA"], 256)
+        mm(T.PA[:, 240:288], T.idF[:, 0:128], pw[:, 96:144], False, True, ["idF0", "pwU"], ["ps:PA"], 256)
         act(p, T.PA[:, 240:288], AF.Copy, ["ps:PA"], [pn], 48)
         if t + 2 < ST:
             lists(t + 2)
@@ -530,7 +600,7 @@ def depend(ops):
                 soft.add(ch[o["chain"]])
             ch[o["chain"]] = i
         for a in o["after"]:
-            (soft if o["eng"] is None else hard).add(a)
+            o["sent"] = a
         for x in o["r"] + o["w"]:
             if x.startswith("ps:"):
                 prev, cur = ps.get(x, ([], []))
@@ -564,8 +634,8 @@ def schedule(ops):
     pred = [[] for _ in range(n)]
     succ = [[] for _ in range(n)]
     for k, o in enumerate(ops):
-        for i in o["hard"] + o["soft"]:
-            lag = 0.0 if i in o["soft"] and o["eng"] is not None else ops[i]["lat"] + HOP
+        for i in o["hard"] + o["soft"] + o["after"]:
+            lag = 0.0 if i in o["soft"] else ops[i]["lat"] + (0.0 if i in o["after"] else float(HOP[0]))
             pred[k].append((i, lag))
             succ[i].append((k, lag))
 
@@ -607,24 +677,58 @@ def schedule(ops):
         pr[i] = ops[i]["dur"] + max([lag + pr[k] for k, lag in succ[i]], default=ops[i]["lat"])
     if n not in KEPT:
         best = None
-        rng = np.random.default_rng(0)
+        rng = np.random.default_rng(SEED)
+        names = [str(o["eng"]) + (o["w"] + o["r"])[0].rstrip("0123456789") for o in ops]
+        kinds = sorted(set(names))
+        kind = np.array([kinds.index(x) for x in names])
         for trial in range(len(URGE) + TRIES):
             if trial < len(URGE):
                 key = [-pr[i] - URGE[trial] * ops[i]["boost"] for i in range(n)]
             else:
                 mid, amp = float(rng.random()) * best[0], float(rng.random()) * 2.0
-                z = rng.random(n)
-                key = [best[1][i] + (amp * float(z[i]) if abs(best[1][i] - mid) < 6.0 else 0.0) for i in range(n)]
+                z = amp * rng.random(n)
+                if trial % 2:
+                    z = 0.1 * z + (4.0 * amp * (rng.random(len(kinds)) - 0.5) * (rng.random(len(kinds)) < 0.2))[kind]
+                s0 = np.array(best[1])
+                key = (s0 + z * (np.abs(s0 - mid) < 8.0)).tolist()
             for _ in range(PASSES):
                 st = sweep(key, pred, succ, [0.0] * n)
                 end = max(st[i] + ops[i]["dur"] + ops[i]["lat"] for i in range(n))
-                if best is None or end < best[0] + 1e-6:
-                    best = (end, st)
+                if best is None or end < best[0] + 0.8:
+                    ends = replay(ops, sorted(range(n), key=lambda i: (st[i], i)))
+                    if best is None:
+                        first = ends
+                    if best is None or float(np.sum(ends / first)) < best[2] + 1e-9:
+                        best = (end, st, float(np.sum(ends / first)))
                 back = sweep([-st[i] - ops[i]["dur"] for i in range(n)], succ, pred, [o["lat"] for o in ops])
                 key = [-back[i] - ops[i]["dur"] for i in range(n)]
         KEPT[n] = best[1]
     st = KEPT[n]
     return sorted(range(n), key=lambda i: (st[i], i)), st
+
+
+def replay(ops, order):
+    free, end, turn = {}, [None] * len(ops), {}
+    last = 0 * CY
+    for i in order:
+        o = ops[i]
+        t = free.get(o["eng"], 0 * CY)
+        if o["hard"]:
+            x = end[o["hard"][0]]
+            for k in o["hard"][1:]:
+                x = np.maximum(x, end[k])
+            t = np.maximum(t, x + HOP)
+        for k in o["after"]:
+            t = np.maximum(t, end[k])
+        if o.get("turn"):
+            if o["turn"] in turn:
+                t = np.maximum(t, end[turn[o["turn"]]] + HOP)
+            turn[o["turn"]] = i
+        free[o["eng"]] = t + o["durs"]
+        end[i] = free[o["eng"]] + o["lats"]
+        if o["eng"] == "y":
+            last = np.maximum(last, end[i])
+    return last
 
 
 def mark(ops, order):
@@ -649,7 +753,7 @@ def emit(g, T, ops, order):
     for i in order:
         o = ops[i]
         e = o["eng"]
-        if e is None:
+        if e in "de":
             cnt[o["sem"]] = o["val"]
             done[i] = (o["sem"], o["val"], {o["sem"]: o["val"]})
             continue
@@ -679,9 +783,25 @@ def emit(g, T, ops, order):
             g.wait_ge(T.sem[s], v)
 
 
+def hand_on(g, core, T, topo, r):
+    src, dst = T.cores[r], T.cores[(r - 1) % len(T.cores)]
+    rid, pid, _se = topo.addr(dst)
+    came = len([e for e in topo.engines(src, core) if e not in topo.engines(src, dst)])
+    for t in range(ST - 1):
+        a = (t + 1) * (J + WX) - WX + O
+        half = T.DB[:, a + S // 2:a + S]
+        g.wait_ge(T.sem["ha%d" % t], came)
+        g.remote_dma(half, half, T.sem["hb%d" % t], T.sem["hl%d" % t], pid, rid, topo.mask(core, dst))
+    for t in range(ST - 1):
+        g.wait_ge(T.sem["hl%d" % t], len(topo.engines(core, dst)))
+
+
 def rank_program(g, core, T, topo):
     rank = T.rank_of(core)
     if rank is None:
+        for r in range(len(T.cores)):
+            if helper(T, r, topo) == core:
+                hand_on(g, core, T, topo, r)
         return
     ops = build(T, rank, topo, core)
     depend(ops)

import numpy as np
from concourse.bass import DstId, RemoteDMATransfer
from concourse.mybir import AluOpType as A, AxisListType as AX, ActivationFunctionType as AF

O, S, W, FB, ST = 2560, 2048, 4608, 48, 4
LO = 160
AL = 2432
J = LO + 2 * AL
WX = W + 16
WB = (ST - 1) * (J + WX) + J - LO + O - WX
NSEND = False
PASSES = 2
SEED = 0
TRIES = 1200
URGE = (0.0, 0.25, 0.5, 1.0, 2.0)
KEPT = {}
CO = O - 0.25
CV = float(O + LO + AL)
EMPTY = float(1 << 16)
KS = 32768.0
RC = 1.5 * 2.0 ** 38
NV = [[8, 7, 7]] * ST
NQ = "ssss"
DETCH = 4
NCH = [(O, W, "sv"), (0, 1024, "v"), (1024, 2048, "v"), (2048, O, "v")]
GROUPS = [dict(bs=(0, 1), c0=0, c1=4, d0=2, f0=0, v0=0, k0=96), dict(bs=(2,), c0=4, c1=6, d0=4, f0=192, v0=48, k0=0)]
LCOL = [slice(0, 3, 2), slice(1, 4, 2), slice(4, 6)]

SCRATCH = {"G": ("sbuf", [128, 48, 208], "bfloat16"), "tmp": ("sbuf", [128, 768], "bfloat16"),
           "ne": ("sbuf", [128, 96], "bfloat16"), "qm": ("sbuf", [128, 3, 96], "bfloat16"), "E": ("sbuf", [128, 54, 16], "bfloat16"),
           "Q0": ("psum", [128, 4, 128], "float32"), "Q1": ("psum", [128, 4, 128], "float32")}
for _dt, _bufs in (
        ("bfloat16", dict(D0=WX, DB=WB, NB=2 * J + O - LO, fvS=96, F16=1536, Gs=768, X=128, Ex=104, Tm=512, Z=288,
                          ident=272, ind=8, SF=288, Dg=96, CF=288, KA=112, KB=336, yb=48, idS=768, one=48, sg=288,
                          bdH=896, MK=144, sn=96, SV0=288, SV1=288, SV2=288, SV3=288, RV0=288, RV1=288, RV2=288)),
        ("float32", dict(detF=O + 48, Pf=96, Py=96, cw=480, K=24, c=144, xc=144, hi=256, I2=104, I4=32, bd=384, cv=48, KT=336,
                         dum=12, MC=12, M=336, rk=112, nm=144, rs=288, S2=288, idF=256, cB=48, pw=192, AB0=768, AB1=768, ABu=768, lw=148,
                         col=96, colD=288, selL=144, selA0=144, selA1=144, mN=192)),
        ("int32", dict(detI=O, pthI=96, pI=4)),
        ("uint16", dict(col16=96, site16=96, IL=12, ML0=12, ML1=12, RL=12, CL=12, A160=768, A161=768, cm=4))):
    for _n, _w in _bufs.items():
        SCRATCH[_n] = ("sbuf", [128, _w], _dt)
for _t in range(ST):
    for _g in range(2):
        SCRATCH["SO%d%d" % (_t, _g)] = ("sbuf", [128, 16], "uint16")
        if _t < ST - 1:
            SCRATCH["RO%d%d" % (_t, _g)] = ("sbuf", [128, 16], "uint16")
for _n in ("P0", "P1", "P2", "F0", "F1", "PA"):
    SCRATCH[_n] = ("psum", [128, 512], "float32")

SEMAPHORES = (["qv", "qs", "qp", "qg"] + ["dm%d" % i for i in range(24)] + ["ls%d" % i for i in range(18)]
              + ["ar%d" % i for i in range(18)] + [x + str(i) for x in ("ha", "hb", "hc", "hl") for i in range(ST - 1)])

CY = np.array([0.95, 0.85, 1.0, 1.05, 1.2, 1.15]) * 1e-3
PC = np.array([0.55, 0.5, 0.5, 0.6, 0.55, 0.65]) * CY
GA = np.array([1.5, 1.3, 1.7, 1.4, 1.9, 1.2])
SC = np.array([3.8, 3.8, 2.5, 5.5, 4.5, 3.0])
HOP = np.array([0.28, 0.27, 0.22, 0.33, 0.3, 0.36])
BWL = np.array([400.0, 400.0, 250.0, 300.0, 300.0, 450.0]) * 1e3
BWR = np.array([80.0, 80.0, 50.0, 100.0, 60.0, 100.0]) * 1e3
ROWS = np.array([0.5, 0.5, 0.8, 0.4, 0.6, 0.4])
ISS = 0.25
RL0 = 0.5
BOOST = 8.0
CB = 16.0


def helper(T, rank, topo):
    core, dst = T.cores[rank], T.cores[(rank - 1) % len(T.cores)]
    return [c for c in topo.cores_of(core) if topo.die(c) != topo.die(core) and topo.may_write(c, dst)][0]


def build(T, rank, topo, core):
    ops = []
    nd = [0]
    nr = [0]
    bo = [0.0]

    def op(eng, fn, r, w, dur, **k):
        d = dict(eng=eng, fn=fn, r=list(r), w=list(w), dur=dur, lat=0.0, sem=None, val=1, after=[], boost=bo[0])
        d.update(k)
        d["durs"], d["lats"] = d["dur"] + 0 * CY, d["lat"] + 0 * CY
        d["dur"], d["lat"] = float(d["durs"][0]), float(d["lats"][0])
        ops.append(d)
        return len(ops) - 1

    def small(n, f=1.0, dur=None):
        return max(64, n * f) * CY if dur is None else dur

    def ts(out, in0, s1, s2, o0, o1, r, w, n, f=1.0, dur=None):
        if o1 is None:
            fn = lambda g: g.vector.tensor_scalar(out, in0, s1, None, o0)
        else:
            fn = lambda g: g.vector.tensor_scalar(out, in0, s1, s2, o0, o1)
        return op("v", fn, r, w, small(n, f, dur))

    def tt(out, a, b, o, r, w, n, f=2.0, dur=None):
        return op("v", lambda g: g.vector.tensor_tensor(out, a, b, o), r, w, small(n, f, dur))

    def cp(out, a, r, w, n, f=1.0, dur=None):
        return op("v", lambda g: g.vector.tensor_copy(out, a), r, w, small(n, f, dur))

    def red(out, a, r, w, n):
        return op("v", lambda g: g.vector.tensor_reduce(out, a, AX.X, A.min), r, w, small(n))

    def scan(out, a, b, r, w, n):
        return op("v", lambda g: g.vector.tensor_tensor_scan(out, a, b, 0.0, A.add, A.min), r, w, small(n))

    def ms(ap, val, w, n, f=1.0):
        return op("v", lambda g: g.vector.memset(ap, val), [], w, small(n, f))

    def act(out, a, fu, r, w, n, bias=None, scale=None, dur=None):
        k = {}
        if bias is not None:
            k["bias"] = bias
        if scale is not None:
            k["scale"] = scale
        return op("s", lambda g: g.scalar.activation(out, a, fu, **k), r, w, small(n, 1.0, dur))

    def aff(out, a, scale, bias, r, w, n):
        return act(out, a, AF.Identity, r, w, n, bias=bias, scale=scale)

    def mm(out, l, rh, st, sp, r, w, cyc):
        return op("p", lambda g: g.tensor.matmul(out, l, rh, st, sp), r, w, cyc * PC)

    def acc(parts, key, r, w, cyc):
        flag = [False]

        def fn(g):
            for i, (out, l, rh) in enumerate(parts):
                ins = g.tensor.matmul(out, l, rh, False, flag[0] and i == len(parts) - 1)
            return ins
        return op("p", fn, r, w, cyc * PC, free=True, group=key, flag=flag)

    def iota(out, pat, base, cmul, w, n, fl=True):
        if fl:
            fn = lambda g: g.iota(out, pat, base, cmul, allow_small_or_imprecise_dtypes=True)
        else:
            fn = lambda g: g.iota(out, pat, base, cmul)
        return op("g", fn, [], w, 0.13 + 2 * n * CY)

    def conv(out, a, r, w, n):
        return op("g", lambda g: g.affine_select(out, a, [[0, n]], A.is_ge, 0.0, 0, 0), r, w, 0.17 + 2 * n * CY)

    bw = [0.0]

    def dma(out, a, r, w, nbytes, queued=False):
        s = "dm%d" % nd[0]
        nd[0] += 1
        t = nbytes / BWL
        if queued:
            t = bw[0] = bw[0] + t
        return op("y", lambda g: g.sync.dma_start(out, a), r, w, 0.08, lat=1.8 + t, sem=s, val=16,
                  chain="load" if queued else None)

    dst = T.cores[(rank - 1) % len(T.cores)]
    rid, pid, _se = topo.addr(dst)
    mask = topo.mask(core, dst)
    neng = len(topo.engines(core, dst))

    def remote(out, a, r, land, nbytes):
        k = nr[0]
        nr[0] += 1
        ls, ar = "ls%d" % k, "ar%d" % k
        i = op("g", lambda g: g.remote_dma(out, a, T.sem[ar], T.sem[ls], pid, rid, mask), r, [], ISS,
               lat=RL0, sem=ls, val=neng, own=True)
        op("d", None, [], [land], ROWS + nbytes / BWR, lat=0.4, sem=ar, val=neng, after=[i], chain="d")
        return i

    def block(t, r):
        hp = helper(T, rank, topo)
        hrid, hpid, _ = topo.addr(hp)
        eng = [e for e in topo.engines(core, hp) if e not in topo.engines(core, dst)]
        h, half = O + S // 2, ROWS + 128 * S / BWR

        def fn(g):
            return g.remote_dma_fused(
                [RemoteDMATransfer(dst_ids=[DstId(rid=rid, pnc=pid)], dma_engine_mask=mask, remote_sem=T.sem["hc%d" % t],
                                   src=dw(t, O, h), dst=dw(t + 1, O, h)),
                 RemoteDMATransfer(dst_ids=[DstId(rid=hrid, pnc=hpid)], dma_engine_mask=sum(1 << e for e in eng),
                                   remote_sem=T.sem["ha%d" % t], src=dw(t, h, W), dst=dw(t + 1, h, W))], local_sem=T.sem["hl%d" % t])
        i = op("g", fn, r, ["go%d" % t], ISS, lat=RL0, sem="hl%d" % t, val=neng + len(eng), own=True)
        op("d", None, [], [Db[t + 1][0]], half, lat=0.4, sem="hc%d" % t, val=neng, after=[i], chain="d")
        op("e", None, [], [Db[t + 1][1]], 2 * half, lat=1.5, sem="hb%d" % t, val=len(topo.engines(hp, dst)), after=[i])

    def gv(n):
        return 0.05 + n * GA * CY

    def gs(n):
        return 0.065 + n * GA * CY

    def sc(n):
        return 0.05 + n * SC * CY

    def dw(t, a, b):
        return T.D0[:, a:b] if t == 0 else T.DB[:, t * (J + WX) - WX + a:t * (J + WX) - WX + b]

    def nw(a, b):
        return T.NB[:, J + a:J + b]

    nown = len(NCH) - 1
    Do = [["D0o%d" % i for i in range(nown)]] + [["D%do" % t] for t in range(1, ST)]
    No = ["No%d" % i for i in range(nown)]
    Nb = ["Nb%d" % q for q in range(4)]
    sct = [[]] + [["s0", "s1", "r0", "r1"]] * (ST - 1)
    Ds = [["D%d%s" % (t, x) for x in sct[t]] for t in range(ST)]
    Ns = [["N%d%s" % (t, x) for x in sct[t]] for t in range(ST)]
    Db = [["D0b"]] + [["D%db0" % t, "D%db1" % t] for t in range(1, ST)]
    Dr = [Do[t] + Db[t] + ["D%dz" % t] + Ds[t] for t in range(ST)]
    Nr = [No + Nb + Ns[t] for t in range(ST)]
    AB = [T.AB0, T.AB1]
    A16 = [T.A160, T.A161]
    PK = [T.P0, T.P1, T.P2]

    dma(T.pthI[:], T.pth[:], [], ["pthI"], 49152, True)
    dma(T.fvS[:], T.fv[:], [], ["fv"], 24576, True)
    cw = O // DETCH
    for i in range(DETCH):
        dma(T.detI[:, i * cw:(i + 1) * cw], T.det[:, i * cw:(i + 1) * cw], [], ["detI%d" % i], 512 * cw, True)
    for (a, b, e), nme in zip(NCH, ["D0b"] + Do[0]):
        dma(T.D0[:, a:b], T.dn[:, a:b], [], [nme], 256 * (b - a), True)

    bo[0] = CB
    K = T.K
    pf, pm, grp, i15, pe, po, ph, kz, k6, k12, k13, k15 = (K[:, i:i + 1] for i in range(12))
    iota(T.pI[:, 0:1], [[0, 1]], 0, 1, ["pI"], 1, False)
    iota(T.c[:], [[1, 144]], 0, 0, ["c"], 144)
    iota(T.xc[:], [[0, 9], [1, 16]], 0, 0, ["xc"], 144)
    iota(T.hi[:], [[1, 16], [0, 16]], 0, 0, ["hi"], 256)
    iota(T.I4[:, 0:4], [[0, 2], [16, 2]], 0, 0, ["I4a"], 4)
    iota(T.I4[:, 4:6], [[0, 2]], 32, 0, ["I4b"], 2)
    iota(T.I4[:, 12:18], [[-4096, 3], [0, 2]], 0, 0, ["I4c"], 6)
    iota(T.I2[:], [[1, 13], [0, 8]], 0, 0, ["I2"], 104)
    iota(T.KA[:], [[16, 14], [1, 8]], 0, 0, ["KA"], 112)
    iota(T.KA[:, 104:105], [[0, 1]], 240, 0, ["KA"], 1)
    iota(T.KT[:], [[4096, 3], [0, 112]], 0, 0, ["KT"], 336)
    iota(T.KT[:, 104:336:112], [[4096, 3]], -int(KS), 0, ["KT"], 3)
    for t in range(ST):
        iota(dw(t, W, WX), [[0, 16]], 0, 0, ["D%dz" % t], 16)
    cp(pf, T.pI[:, 0:1], ["pI"], ["pf"], 1)
    ts(T.pI[:, 1:2], T.pI[:, 0:1], 15, None, A.bitwise_and, None, ["pI"], ["pI1"], 1)
    ts(T.pI[:, 2:3], T.pI[:, 0:1], 1, None, A.bitwise_and, None, ["pI"], ["pI2"], 1)
    cp(pm, T.pI[:, 1:2], ["pI1"], ["pm"], 1)
    cp(po, T.pI[:, 2:3], ["pI2"], ["po"], 1)
    aff(pe, po, -1.0, 1.0, ["po"], ["pe"], 1)
    ts(ph, pm, po, 0.5, A.subtract, A.mult, ["pm", "po"], ["ph"], 1)
    ts(grp, pf, pm, 0.0625, A.subtract, A.mult, ["pf", "pm"], ["grp"], 1)
    ts(i15, pm, 15.0, None, A.is_equal, None, ["pm"], ["i15"], 1)
    aff(kz, grp, 16.0, 15.0, ["grp"], ["kz"], 1)
    ts(T.cw[:, 432:480], T.c[:, 0:48], 512.0, i15, A.add, A.mult, ["c", "i15"], ["cv0"], 48)
    aff(T.cv[:], T.cw[:, 432:480], None, W - CO, ["cv0"], ["cv"], 48)
    aff(k6, pm, 48.0, 4624.0, ["pm"], ["k6"], 1)
    aff(T.detF[:, O:O + 48], T.c[:, 0:48], None, k6, ["c", "k6"], ["detFx"], 48)
    for t in range(ST - 1):
        for gi in range(2):
            ms(T["SO%d%d" % (t, gi)][:], 0, ["SO%d%d%d" % (t, gi, i) for i in range(6)], 16)
    ts(T.CL[:, 0:6], T.I4[:, 0:6], pm, None, A.add, None, ["I4a", "I4b", "pm"], ["CL"], 6)
    ts(T.ind[:], T.c[:, 0:8], grp, None, A.is_equal, None, ["c", "grp"], ["ind"], 8)
    ts(T.Z[:, 0:144], T.c[:], kz, KS, A.is_equal, A.mult, ["c", "kz"], ["Z0"], 144)
    aff(T.Z[:, 144:288], T.Z[:, 0:144], -1.0, None, ["Z0"], ["Z1"], 144)
    ts(T.Ex[:], T.I2[:], pm, -KS, A.is_equal, A.mult, ["I2", "pm"], ["Ex"], 104)
    aff(k13, pm, 256.0, None, ["pm"], ["k13"], 1)
    aff(T.KB[:], T.KT[:], None, k13, ["KT", "k13"], ["KB"], 336)
    ts(T.Tm[:, 0:256], T.hi[:], pm, None, A.is_equal, None, ["hi", "pm"], ["TmR"], 256)
    ts(T.Tm[:, 256:384], T.xc[:, 0:128], ph, None, A.is_equal, None, ["xc", "ph"], ["TmK0"], 128)
    act(T.Tm[:, 384:512], T.Tm[:, 256:384], AF.Copy, ["TmK0"], ["TmK1"], 128)
    TmR, TmK = T.Tm[:, 0:256], T.Tm[:, 256:512]
    up, idp, idn = T.ident[:, 0:128], T.ident[:, 1:129], T.ident[:, 144:272]
    ts(T.ident[:, 0:129], T.c[:, 0:129], -1.0, pf, A.add, A.is_equal, ["c", "pf"], ["idp"], 129)
    aff(idn, idp, -1.0, None, ["idp"], ["idn"], 128)
    aff(T.idF[:, 0:128], idp, None, None, ["idp"], ["idF0"], 128)
    aff(T.idF[:, 128:256], idp, -1.0, None, ["idp"], ["idF1"], 128)
    aff(T.idS[:, 0:128], idp, 16384.0, None, ["idp"], ["idS0"], 128)
    aff(T.idS[:, 128:256], idp, -O / 2, None, ["idp"], ["idS1"], 128)
    for t in range(ST):
        aff(T.idS[:, 256 + 128 * t:384 + 128 * t], idp, -16384.0 - (rank + t) % len(T.cores) * S / 2, None, ["idp"],
            ["idS%d" % (2 + t)], 128)
    aff(T.one[:], T.c[:, 0:48], 0.0, 1.0, ["c"], ["one"], 48)
    bd = [T.bd[:, 128 * i:128 * i + 128] for i in range(3)]
    bdH = [T.bdH[:, 128 * i:128 * i + 128] for i in range(7)]
    ts(bd[0], T.hi[:, 0:128], grp, None, A.is_equal, None, ["hi", "grp"], ["bd0"], 128)
    aff(bd[1], bd[0], pe, None, ["bd0", "pe"], ["bd1"], 128)
    aff(bd[2], bd[0], po, None, ["bd0", "po"], ["bd2"], 128)
    aff(k15, i15, -KS, None, ["i15"], ["k15"], 1)
    aff(bdH[4], bd[0], k15, None, ["bd0", "k15"], ["bdH4"], 128)
    for i in (1, 2):
        aff(bdH[4 + i], bd[i], None, None, ["bd%d" % i], ["bdH%d" % (4 + i)], 128)
    for i in range(3):
        aff(bdH[i], bd[i], -float(AL), None, ["bd%d" % i], ["bdH%d" % i], 128)
    aff(bdH[3], bd[0], -KS, None, ["bd0"], ["bdH3"], 128)
    aff(T.qm[:, :, 0:16], T.c[:, 0:48], 0.0, CV, ["c"], ["qm0"], 48)
    aff(T.qm[:, :, 48:80], T.c[:, 0:96], 0.0, CV, ["c"], ["qm3"], 96)
    ts(T.cw[:, 192:288], T.xc[:, 0:96], pm, None, A.is_le, None, ["xc", "pm"], ["cw10", "cw11"], 96)
    aff(T.qm[:, :, 16:48], T.cw[:, 192:288], KS - CV, CV, ["cw10", "cw11"], ["qm1"], 96)
    aff(T.qm[:, :, 80:96], T.cw[:, 192:240], KS - CV, CV, ["cw10", "cw11"], ["qm5"], 48)
    qmr = ["qm%d" % u for u in (0, 1, 3, 5)]
    iota(T.rs[:], [[0, 288]], 0, 0, ["rs"], 288)
    for sl, n_ in ((slice(0, 96, 16), 6), (slice(96, 240, 48), 3), (slice(240, 288, 16), 3)):
        iota(T.rs[:, sl], [[0, n_]], 16000000, 0, ["rs"], n_)
    ts(T.cw[:, 0:144], T.xc[:], pm, None, A.not_equal, None, ["xc", "pm"], ["cw00", "cw01"], 144)
    for a, b, cst in ((0, 96, CV), (96, 240, 16384), (240, 288, CV)):
        aff(T.CF[:, a:b], T.cw[:, 0:b - a], 2.0 ** 22 - cst, float(cst), ["cw00", "cw01"], ["CF%d" % a], b - a)
    aff(k12, pm, -256.0, None, ["pm"], ["k12"], 1)
    aff(T.MC[:, 0:6], T.I4[:, 12:18], None, k12, ["I4c", "k12"], ["MC"], 6)
    iota(T.rk[:], [[0, 112]], 0, 0, ["rk"], 112)
    iota(T.rk[:, 0:1], [[0, 1]], 16000000, 0, ["rk"], 1)
    for i, v_ in ((105, RC), (106, -RC)):
        aff(T.rk[:, i:i + 1], pf, 0.0, v_, ["rk", "pf"], ["rk%d" % i], 1)
    aff(T.KA[:, 105:112], T.c[:, 0:7], 0.0, 4 * RC, ["KA", "c"], ["KA1"], 7)
    aff(T.dum[:, 0:9], T.c[:, 0:9], 16.0, pm, ["c", "pm"], ["dum"], 9)

    bo[0] = 0.0
    ts(T.pw[:, 0:96], T.pthI[:], 0.0, EMPTY + CO + 1.0, A.is_lt, A.mult, ["pthI"], ["pwA", "pwB"], 96)
    ts(T.Py[:], T.pthI[:], -CO, None, A.add, None, ["pthI"], ["Py"], 96)
    tt(T.Pf[:], T.Py[:], T.pw[:, 0:96], A.add, ["Py", "pwA", "pwB"], ["P0", "P1"], 96)
    for i in range(DETCH):
        (cp if i else conv)(T.detF[:, i * cw:(i + 1) * cw], T.detI[:, i * cw:(i + 1) * cw], ["detI%d" % i], ["detF%d" % i], cw)
    detr = ["detF%d" % i for i in range(DETCH)] + ["detFx"]
    for (a, b, e), dn_, nn in zip(NCH, [["D0b"]] + [[x] for x in Do[0]], [Nb] + [[x] for x in No]):
        w_ = (b - a) // len(e)
        for i, e_ in enumerate(e):
            a_, wn = a + i * w_, nn[i * len(nn) // len(e):(i + 1) * len(nn) // len(e)]
            if e_ == "s":
                act(nw(a_, a_ + w_), T.D0[:, a_:a_ + w_], AF.Relu, dn_, wn, w_, scale=-1.0)
            else:
                ts(nw(a_, a_ + w_), T.D0[:, a_:a_ + w_], -1.0, 0.0, A.mult, A.max, dn_, wn, w_, 0.5)
    for r_ in range(16):
        if r_ % 2:
            cp(T.F16[:, r_:1536:16], T.fvS[:], ["fv"], ["F16%d" % r_], 96, 0.5)
        else:
            act(T.F16[:, r_:1536:16], T.fvS[:], AF.Copy, ["fv"], ["F16%d" % r_], 96)
    F16r = ["F16%d" % r_ for r_ in range(16)]
    o_ = 0
    for m in range(2):
        for gr in GROUPS:
            w_ = 16 * len(gr["bs"])
            for ty in range(3):
                f0 = 48 * m + 16 * gr["bs"][0]
                mm(T.F0[:, o_:o_ + w_], idp if ty else idn, T.fvS[:, f0:f0 + w_], True, True, ["idp", "idn", "fv"], ["ps:F0"], 64)
                o_ += w_
    act(T.SF[:], T.F0[:, 0:288], AF.Copy, ["ps:F0"], ["SF"], 288)

    def first_empty(m):
        p, pn = T.Pf[:, 48 * m:48 * m + 48], "P%d" % m
        ne = T.ne[:, 48 * m:48 * m + 48]
        act(ne, p, AF.Sign, [pn], ["ne%d" % m], 48, bias=EMPTY / 2, scale=-1.0)
        mm(T.PA[:, 96:144], up, ne, True, False, ["idp", "ne%d" % m], ["ps:PA"], 64)
        mm(T.PA[:, 96:144], idn, ne, False, True, ["idn", "ne%d" % m], ["ps:PA"], 64)
        act(T.mN[:, 96 * m + 48:96 * m + 96], T.PA[:, 96:144], AF.Relu, ["ps:PA"], ["mN%d" % m], 48, scale=0.5)

    def lists(t):
        m = t % 2
        B = (rank + t) % len(T.cores)
        p = T.Pf[:, 48 * m:48 * m + 48]
        col = T.col[:, 48 * m:48 * m + 48]
        sg = [T.sg[:, 144 * m + 48 * i:144 * m + 48 * i + 48] for i in range(3)]
        n = ["sg%d%d" % (m, i) for i in range(3)]
        pn = "P%d" % m
        act(sg[0], p, AF.Sign, [pn], [n[0]], 48)
        act(sg[1], p, AF.Sign, [pn], [n[1]], 48, bias=-float(B * S))
        q, hi_, lo_ = T.PA[:, 288:336], T.idS[:, 0:128], T.idS[:, 256 + 128 * t:384 + 128 * t]
        mm(q, T.idF[:, 0:128], p, True, False, ["idF0", pn], ["ps:PA"], 256)
        mm(q, hi_, T.one[:], False, False, ["idS0", "one"], ["ps:PA"], 64)
        mm(q, lo_, T.one[:], False, False, ["idS%d" % (2 + t), "one"], ["ps:PA"], 64)
        mm(q, hi_, sg[0], False, False, ["idS0", n[0]], ["ps:PA"], 64)
        mm(q, lo_, sg[1], False, True, ["idS%d" % (2 + t), n[1]], ["ps:PA"], 64)
        tt(col, q, T.cv[:], A.min, ["ps:PA", "cv"], ["col%d" % m], 48, 1.0)
        act(sg[2], col, AF.Sign, ["col%d" % m], [n[2]], 48)
        q = T.PA[:, 336:384]
        mm(q, T.idF[:, 0:128], col, True, False, ["idF0", "col%d" % m], ["ps:PA"], 256)
        mm(q, T.idS[:, 128:256], T.one[:], False, False, ["idS1", "one"], ["ps:PA"], 64)
        mm(q, T.idS[:, 128:256], sg[2], False, True, ["idS1", n[2]], ["ps:PA"], 64)
        if t:
            u_ = [T.lw[:, 48 * i:48 * i + 48] for i in range(3)]
            aff(u_[0], q, None, CO, ["ps:PA"], ["lw0"], 48)
            conv(T.site16[:, 48 * m:48 * m + 48], u_[0], ["lw0"], ["site%d" % m], 48)
            act(u_[1], col, AF.Relu, ["col%d" % m], ["lw1"], 48, bias=W - CO, scale=-1.0)
            aff(u_[2], u_[1], -1.0, float(W), ["lw1"], ["lw2"], 48)
            conv(T.col16[:, 48 * m:48 * m + 48], u_[2], ["lw2"], ["c16%d" % m], 48)
        else:
            ts(T.site16[:, 48 * m:48 * m + 48], q, CO, None, A.add, None, ["ps:PA"], ["site%d" % m], 48)
            ts(T.col16[:, 48 * m:48 * m + 48], col, CO, float(W), A.add, A.min, ["col%d" % m], ["c16%d" % m], 48)
        for b in range(3):
            src = T.detF[:, 0:O + 48].indirect(T.site16[:, 48 * m + 16 * b:48 * m + 16 * b + 16])
            act(AB[m][:, 256 * b:256 * b + 256], src, AF.Identity, detr + ["site%d" % m], ["AB%d%d" % (m, b)], 0, bias=-CO, dur=gs(256))
            if t == 0 and b == 0:
                cp(A16[m][:, 256 * b:256 * b + 256], src, detr + ["site%d" % m], ["A16%d%d" % (m, b)], 0, dur=gv(256))
            elif t:
                u_ = T.ABu[:, 256 * b:256 * b + 256]
                aff(u_, AB[m][:, 256 * b:256 * b + 256], None, CO, ["AB%d%d" % (m, b)], ["ABu%d" % b], 256)
                conv(A16[m][:, 256 * b:256 * b + 256], u_, ["ABu%d" % b], ["A16%d%d" % (m, b)], 256)
            else:
                ts(A16[m][:, 256 * b:256 * b + 256], AB[m][:, 256 * b:256 * b + 256], CO, None, A.add, None, ["AB%d%d" % (m, b)],
                   ["A16%d%d" % (m, b)], 256)
        act(T.colD[:, 96 * m:96 * m + 96], col.indirect(T.CL[:, 0:6]), AF.Copy, ["col%d" % m, "CL"], ["colD%d" % m], 0, dur=gs(96))
        first_empty(m)

    lists(0)
    lists(1)

    for t in range(ST):
        m = t % 2
        B = (rank + t) % len(T.cores)
        R = 12 + t // 2
        last = t == ST - 1
        SV, ML, selA = T["SV%d" % t], T["ML%d" % m], T["selA%d" % m]
        DG, NG = dw(t, 0, WX), nw(0, W)
        if not last:
            block(t, Db[t] + Ds[t][2:] + (Do[0] if t == 0 else []))
            dma(dw(t + 1, 0, O), dw(t, 0, O), Do[t] + Ds[t] + ["go%d" % t], Do[t + 1], 256 * O)
            ops[-1]["lats"] = ops[-1]["lats"] + 128 * S / BWR
            ops[-1]["lat"] = float(ops[-1]["lats"][0])
        else:
            dma(dw(1, 0, W), dw(t, 0, W), Dr[t], Dr[1], 256 * W)
        late = []
        bo[0] = BOOST
        tt(T.tmp[:], DG.indirect(T.col16[:, 48 * m:48 * m + 48]), T.F16[:, 768 * m:768 * m + 768], A.min,
           Dr[t] + ["c16%d" % m] + F16r, ["tmp"], 0, dur=gv(768))
        ts(T.Gs[:], T.tmp[:], 0.0, None, A.max, None, ["tmp"], ["Gs"], 768, 0.5)
        for b in range(3):
            w_ = 32 if b < 2 else 16

            def subs(g, b=b, w_=w_):
                for x in range(16):
                    j = 16 * b + x
                    ins = g.tensor.matmul(T.F1[32 * b:32 * b + w_, x:128:16], T.Gs[:, 16 * j:16 * j + w_], T.ind[:], True, True)
                return ins
            op("p", subs, ["Gs", "ind"], ["ps:F1"], 16 * w_ * PC)
        act(T.X[0:80, :], T.F1[0:80, 0:128], AF.Copy, ["ps:F1"], ["X"], 128)
        onv = [(j % 16 < NV[t][j // 16]) if j // 16 == 1 else (j % 16 >= 16 - NV[t][j // 16]) for j in range(48)]
        for gi, gr in enumerate(GROUPS):
            bs, c0, c1, d0 = gr["bs"], gr["c0"], gr["c1"], gr["d0"]
            nb = len(bs)
            for b in bs:
                pk, key = "ps:P%d" % b, (t, b)
                mm(PK[b][:, 0:112], idp, T.KA[:], True, False, ["idp", "KA", "KA1"], [pk], 112)
                acc([(PK[b][:, 0:112], idp, T.KB[:, 112 * b:112 * b + 112])], key, ["idp", "KB"], [pk], 112)
                acc([(PK[b][:, 0:8 * R], T.X[32 * b:32 * b + 16, :], T.Ex[32 * b:32 * b + 16, 0:8 * R])], key, ["X", "Ex"], [pk], 8 * R)
                for x in range(16):
                    j = 16 * b + x
                    src = NG.indirect(A16[m][:, 16 * j:16 * j + R])
                    f = T.fvS[:, 48 * m + j:48 * m + j + 1]
                    rr = Nr[t] + ["A16%d%d" % (m, b), "fv"]
                    if onv[j]:
                        ts(T.G[:, j, 0:16 * R], src, f, 0.0, A.subtract, A.min, rr, ["G%d" % j], 0, dur=gv(16 * R))
                    else:
                        act(T.G[:, j, 0:16 * R], src, AF.Relu, rr, ["G%d" % j], 0, bias=f, scale=-1.0, dur=gs(16 * R))
                    ops[-1]["chain"] = ops[-1]["eng"]
                    ops[-1]["boost"] = 0.0
                    z = T.Z[:, 144 * onv[j] + 15 - x:144 * onv[j] + 143 - x]
                    acc([(PK[b][:, 0:8 * R], z, T.G[:, j, h:16 * R:2]) for h in range(2)], key, ["G%d" % j, "Z0", "Z1"], [pk], 16 * R)
                o_ = 112 * b
                mb = T.M[:, o_ + 104:o_ + 105]
                scan(T.M[:, o_:o_ + 108], T.rk[:, 0:108], PK[b][:, 0:108], ["rk", "rk105", "rk106", pk], ["m%d" % b] + ["free"] * (b == 2), 108)
                ts(ML[:, LCOL[b]], T.MC[:, 2 * b:2 * b + 2], mb, T.M[:, o_ + 106:o_ + 107], A.add, A.subtract,
                   ["MC", "m%d" % b], ["ML%d%d" % (m, b)], 3)
                ts(T.IL[:, LCOL[b]], T.M[:, o_ + 106:o_ + 108], mb, -0.0625, A.subtract, A.mult, ["m%d" % b], ["IL%d" % b], 3)
            n0, n1, n = 16 * c0, 16 * c1, 16 * (c1 - c0)
            e0, e1 = 16 * d0, 16 * (d0 + nb)
            h0, h1, hn = 48 * bs[0], 48 * (bs[-1] + 1), 48 * nb
            MLr = ["ML%d%d" % (m, b) for b in bs]
            sl, sa = "selL%d" % gi, "selA%d%d" % (m, gi)
            Qp, Fp, qn, fn_ = T["Q%d" % gi], T["F%d" % gi], "ps:Q%d" % gi, "ps:F%d" % gi
            act(T.MK[:, n0:n1], TmK.indirect(ML[:, c0:c1]), AF.Copy, ["TmK0", "TmK1"] + MLr, ["MK%d" % gi], 0, dur=gs(n))
            tt(T.selL[:, n0:n1], TmR.indirect(ML[:, c0:c1]), T.colD[:, 96 * m + n0:96 * m + n1], A.mult,
               ["TmR", "colD%d" % m] + MLr, [sl], 0, dur=gv(n))
            tt(selA[:, n0:n1], AB[m][:, 0:768].indirect(T.IL[:, c0:c1]), T.MK[:, n0:n1], A.mult,
               ["AB%d%d" % (m, b) for b in range(3)] + ["IL%d" % b for b in bs] + ["MK%d" % gi], [sa], 0, dur=gv(n))
            srcs = [(T.selL, sl), (selA, sa), (selA, sa)]
            v0, k0, f0 = gr["v0"], gr["k0"], gr["f0"]
            Dp, dn_ = PK[1 + gi], "ps:P%d" % (1 + gi)
            mm(Dp[:, 128:128 + hn], idp, T.CF[:, 0:hn], True, False, ["idp", "CF0"], [dn_], max(64, hn))
            for ty, (s_, sn_) in enumerate(srcs):
                mm(Dp[:, 128 + 16 * nb * ty:128 + 16 * nb * (ty + 1)], bd[ty], s_[:, e0:e1], False, ty == 2, ["bd%d" % ty, sn_], [dn_], 256)
            mm(Qp[:, 0:3, 0:n], idp, T.qm[:, :, n0:n1], True, False, ["idp"] + qmr, [qn], 3 * n)
            for ty, (s_, sn_) in enumerate(srcs):
                mm(Qp[:, ty, 0:n], bd[ty], s_[:, n0:n1], False, ty == 2, ["bd%d" % ty, sn_], [qn], 256)
            scan(T.nm[:, h0:h1], T.rs[:, 0:hn], Dp[:, 128:128 + hn], ["rs", dn_], ["nm%d" % gi], hn)
            nmr = ["nm%d" % gi]
            l0 = 6 * gi
            ts(T.RL[:, l0:l0 + 3 * nb], T.nm[:, h0 + 15:h1:16], CO - CV, float(W), A.add, A.min, nmr, ["RL%d" % gi], 6)
            svd, svn = SV[:, 2 * h0:2 * h0 + hn], SV[:, 2 * h0 + hn:2 * h1]
            vd, vn = "SVd%d%d" % (t, gi), "SVn%d%d" % (t, gi)
            sf, src = T.SF[:, 144 * m + h0:144 * m + h1], DG.indirect(T.RL[:, l0:l0 + 3 * nb])
            if gi:
                tt(svd, src, sf, A.add, Dr[t] + ["RL1", "SF"], [vd], 0, dur=gv(hn))
            else:
                act(T.Dg[:], src, AF.Copy, Dr[t] + ["RL0"], ["Dg"], 0, dur=gs(hn))
                mm(T.P0[:, 128:128 + hn], idp, T.Dg[:], True, False, ["idp", "Dg"], ["ps:P0"], hn)
                mm(T.P0[:, 128:128 + hn], idp, sf, False, True, ["idp", "SF"], ["ps:P0"], hn)
                act(svd, T.P0[:, 128:128 + hn], AF.Copy, ["ps:P0"], [vd], hn)
            if not last:
                act(svn, svd, AF.Relu, [vd], [vn], hn, scale=-1.0)
            mm(Fp[:, 0:2 * hn], idp, T.CF[:, f0:f0 + 2 * hn], True, False, ["idp", "CF0", "CF96", "CF240"], [fn_], 2 * hn)
            for ty, (s_, sn_) in enumerate(srcs):
                mm(Fp[:, v0 + 16 * nb * ty:v0 + 16 * nb * (ty + 1)], bd[ty], s_[:, e0:e1], False, False, ["bd%d" % ty, sn_], [fn_], 256)
            sgA = T.sn[:, 48 + e0 - 32:48 + e1 - 32]
            act(sgA, selA[:, e0:e1], AF.Sign, [sa], ["snA%d" % gi], 32)
            sgL = T.sn[:, e0 - 32:e1 - 32]
            act(sgL, T.selL[:, e0:e1], AF.Sign, [sl], ["snL%d" % gi], 32)
            for i in range(nb):
                mm(Fp[:, k0 + 48 * i:k0 + 48 * i + 16], bdH[4], T.sn[:, e0 - 32 + 16 * i:e0 - 16 + 16 * i], False, False,
                   ["bdH4", "snL%d" % gi], [fn_], 64)
            if not last:
                for ty in range(3):
                    mm(Fp[:, v0 + 16 * nb * ty:v0 + 16 * nb * (ty + 1)], bdH[ty], sgA if ty else sgL, False, False,
                       ["bdH%d" % ty, ("snA%d" if ty else "snL%d") % gi], [fn_], 64)
            cmpl = [(0, 2, 2, 0), (1, 1, 1, 1)] if gi == 0 else [(0, 0, 1, 0), (1, 0, 1, 0), (2, 1, 1, 0)]
            eo = 27 * gi
            for ci, (bl, q0, w_, o_) in enumerate(cmpl):
                for ty in range(3):
                    x_ = (32 * ty + 16 * bl + 15) if bl < 2 else (96 + 16 * ty + 15)
                    en = "E%d" % eo
                    ts(T.E[:, eo:eo + 3 * w_, :], Qp[:, 0:3, 16 * q0:16 * (q0 + w_)], T.nm[:, x_:x_ + 1], None, A.is_equal, None,
                       [qn, "nm%d" % (bl // 2)], [en], 48 * w_)
                    for i in range(w_):
                        mm(Fp[:, k0 + 48 * (o_ + i):k0 + 48 * (o_ + i + 1)], bdH[3], T.E[:, eo + i:eo + 3 * w_:w_, :], False,
                           ci == len(cmpl) - 1 and ty == 2, ["bdH3", en], [fn_], 64)
                    eo += 3 * w_
            scan(T.S2[:, f0:f0 + 2 * hn], T.rs[:, f0:f0 + 2 * hn], Fp[:, 0:2 * hn], ["rs", fn_], ["S2%d" % gi], 2 * hn)
            SO = T["SO%d%d" % (t, gi)]
            SOr = ["SO%d%d%d" % (t, gi, i) for i in range(3 * nb)]
            for i in range(3 * nb):
                v_ = f0 + v0 + 16 * i + 15
                s_ = 143 + 48 * bs[i % nb]
                ts(SO[:, i:i + 1], T.S2[:, v_:v_ + 1], T.S2[:, s_:s_ + 1], T.dum[:, i:i + 1], A.min, A.max, ["S2%d" % gi, "dum"],
                   [SOr[i]], 1)
            so = SO[:, 0:3 * nb]
            if last:
                cp(dw(1, -LO - AL, W).indirect(so), svd, SOr + [vd] + Do[1], ["fin%d" % gi], 0, dur=sc(hn))
                ops[-1]["turn"] = "D"
                continue
            RV, RO = T["RV%d" % t], T["RO%d%d" % (t, gi)]
            rv, ro = "RV%d%d" % (t, gi), "RO%d%d" % (t, gi)
            remote(RV[:, 2 * h0:2 * h0 + hn], svd, [vd], rv, 256 * hn)
            remote(RO[:], SO[:], SOr, ro, 128 * 32)
            act(RV[:, 2 * h0 + hn:2 * h1], RV[:, 2 * h0:2 * h0 + hn], AF.Relu, [rv], [rv + "n"], hn, scale=-1.0)
            bo[0] = 0.0
            cp(nw(-J, O).indirect(so), svn, SOr + [vn, "free"], [Ns[t + 1][gi]], 0, dur=sc(hn))
            cp(dw(t + 1, -J, O).indirect(so), svd, SOr + [vd] + Do[t + 1], [Ds[t + 1][gi]], 0, dur=sc(hn))
            cp(nw(-LO, J + O - LO).indirect(RO[:, 0:3 * nb]), RV[:, 2 * h0 + hn:2 * h1], [rv + "n", ro] + Nb, [Ns[t + 1][2 + gi]], 0,
               dur=sc(hn))
            cp(dw(t + 1, -LO, J + O - LO).indirect(RO[:, 0:3 * nb]), RV[:, 2 * h0:2 * h0 + hn],
               [rv, ro, "D%dz" % (t + 1)] + Db[t + 1] + Do[t + 1] + Nb, [Ds[t + 1][2 + gi]], 0, dur=sc(hn))
            for o_, b_ in zip(ops[-4:], "NDND"):
                o_["turn"] = b_
            late += ops[-4:]
            del ops[-4:]
            bo[0] = BOOST
        bo[0] = 0.0
        if last:
            dma(T.yd[:], dw(1, 0, W), ["fin0", "fin1"], [], 256 * W)
        else:
            for q in range(4):
                act(nw(O + 512 * q, O + 512 * q + 512), dw(t + 1, O + 512 * q, O + 512 * q + 512), AF.Relu,
                    [Db[t + 1][q // 2]], [Nb[q]], 512, scale=-1.0)
            ops.extend(late)
        p = T.Pf[:, 48 * m:48 * m + 48]
        pn = "P%d" % m
        pw = T.pw
        sar = ["selA%d0" % m, "selA%d1" % m]
        if last:
            ts(T.cm[:, 0:3], T.S2[:, 143:240:48], 0.0, None, A.is_gt, None, ["S20", "S21"], ["cm"], 3)
        else:
            act(T.lw[:, 144:147], T.S2[:, 143:240:48], AF.Relu, ["S20", "S21"], ["lw3"], 3, scale=1.0 / 16384)
            conv(T.cm[:, 0:3], T.lw[:, 144:147], ["lw3"], ["cm"], 3)
        act(T.cB[:], T.c[:, 0:16].indirect(T.cm[:, 0:3]), AF.Copy, ["c", "cm"], ["cB"], 0, dur=gs(48))
        act(T.yb[:], T.sn[:, 48:96], AF.Relu, ["snA0", "snA1"], ["yb"], 48, scale=float(B * S))
        act(T.mN[:, 96 * m:96 * m + 48], TmR.indirect(ML[:, 2:5]), AF.Copy, ["TmR"] + ["ML%d%d" % (m, b) for b in range(3)], ["mR%d" % m],
            0, dur=gs(48))
        for h in range(2):
            o_ = T.PA[:, 48 * h:48 * h + 48]
            mm(o_, bd[1 + h], selA[:, 32:80], True, False, ["bd%d" % (1 + h)] + sar, ["ps:PA"], 256)
            mm(o_, bdH[5 + h], T.yb[:], False, False, ["bdH%d" % (5 + h), "yb"], ["ps:PA"], 64)
            mm(o_, T.idF[:, 128:256], p, False, True, ["idF1", pn], ["ps:PA"], 256)
        tt(pw[:, 0:96], T.PA[:, 0:96], T.mN[:, 96 * m:96 * m + 96], A.mult, ["ps:PA", "mR%d" % m, "mN%d" % m], ["pwA", "pwB"], 96, 1.0)
        for h in range(2):
            mm(T.PA[:, 192:240], T.idF[:, 0:128], pw[:, 48 * h:48 * h + 48], h == 0, h == 1, ["idF0", "pwA"], ["ps:PA"], 256)
        tt(pw[:, 96:144], T.PA[:, 192:240], T.cB[:], A.mult, ["ps:PA", "cB"], ["pwU"], 48, 1.0)
        mm(T.PA[:, 240:288], T.idF[:, 0:128], p, True, False, ["idF0", pn], ["ps:PA"], 256)
        mm(T.PA[:, 240:288], T.idF[:, 0:128], pw[:, 96:144], False, True, ["idF0", "pwU"], ["ps:PA"], 256)
        act(p, T.PA[:, 240:288], AF.Copy, ["ps:PA"], [pn], 48)
        if t + 2 < ST:
            lists(t + 2)
        else:
            y, y2 = T.cw[:, 192 * m:192 * m + 48], T.cw[:, 192 * m + 48:192 * m + 96]
            ts(y, p, EMPTY / 2, -EMPTY - CO - 1.0, A.is_ge, A.mult, [pn], ["cw%d0" % m], 48)
            aff(y2, p, None, CO, [pn], ["cw%d1" % m], 48)
            tt(T.Py[:, 48 * m:48 * m + 48], y2, y, A.add, ["cw%d0" % m, "cw%d1" % m, "Py"], ["Py%d" % m], 48)
            dma(T.yp[:, 48 * m:48 * m + 48], T.Py[:, 48 * m:48 * m + 48], ["Py%d" % m], [], 128 * 192)
    return ops


def depend(ops):
    lw, rd, ps, ch = {}, {}, {}, {}
    for i, o in enumerate(ops):
        hard, soft = set(), set()
        if o.get("chain"):
            if o["chain"] in ch:
                soft.add(ch[o["chain"]])
            ch[o["chain"]] = i
        for a in o["after"]:
            o["sent"] = a
        for x in o["r"] + o["w"]:
            if x.startswith("ps:"):
                prev, cur = ps.get(x, ([], []))
                if cur and ops[cur[-1]]["eng"] != o["eng"]:
                    prev, cur = cur, []
                hard.update(prev)
                if cur and o["eng"] == "p":
                    soft.add(cur[0] if o.get("free") else cur[-1])
                ps[x] = (prev, cur + [i])
        for x in o["r"]:
            if not x.startswith("ps:") and x in lw:
                hard.add(lw[x])
        for x in o["w"]:
            if not x.startswith("ps:"):
                if x in lw:
                    hard.add(lw[x])
                hard.update(rd.get(x, []))
        for x in o["r"]:
            if not x.startswith("ps:"):
                rd.setdefault(x, []).append(i)
        for x in o["w"]:
            if not x.startswith("ps:"):
                lw[x] = i
                rd[x] = []
        hard.discard(i)
        o["hard"], o["soft"] = sorted(hard), sorted(soft - hard)


def schedule(ops):
    n = len(ops)
    pred = [[] for _ in range(n)]
    succ = [[] for _ in range(n)]
    for k, o in enumerate(ops):
        for i in o["hard"] + o["soft"] + o["after"]:
            lag = 0.0 if i in o["soft"] else ops[i]["lat"] + (0.0 if i in o["after"] else float(HOP[0]))
            pred[k].append((i, lag))
            succ[i].append((k, lag))

    def sweep(key, before, after, head):
        left = [len(x) for x in before]
        rdy = list(head)
        st = [0.0] * n
        busy = {}
        heap = sorted((key[i], i) for i in range(n) if left[i] == 0)
        while heap:
            i = heap.pop(0)[1]
            t0, d = rdy[i], ops[i]["dur"]
            if ops[i]["eng"] is not None:
                q = busy.setdefault(ops[i]["eng"], [])
                lo, hi = 0, len(q)
                while lo < hi:
                    mid = (lo + hi) // 2
                    if q[mid][1] <= t0:
                        lo = mid + 1
                    else:
                        hi = mid
                while lo < len(q) and q[lo][0] < t0 + d - 1e-9:
                    t0 = max(t0, q[lo][1])
                    lo += 1
                q.insert(lo, (t0, t0 + d))
            st[i] = t0
            new = []
            for k, lag in after[i]:
                rdy[k] = max(rdy[k], t0 + d + lag)
                left[k] -= 1
                if left[k] == 0:
                    new.append((key[k], k))
            if new:
                heap = sorted(heap + new)
        return st

    pr = [0.0] * n
    for i in range(n - 1, -1, -1):
        pr[i] = ops[i]["dur"] + max([lag + pr[k] for k, lag in succ[i]], default=ops[i]["lat"])
    if n not in KEPT:
        best = None
        rng = np.random.default_rng(SEED)
        names = [str(o["eng"]) + (o["w"] + o["r"])[0].rstrip("0123456789") for o in ops]
        kinds = sorted(set(names))
        kind = np.array([kinds.index(x) for x in names])
        for trial in range(len(URGE) + TRIES):
            if trial < len(URGE):
                key = [-pr[i] - URGE[trial] * ops[i]["boost"] for i in range(n)]
            else:
                mid, amp = float(rng.random()) * best[0], float(rng.random()) * 2.0
                z = amp * rng.random(n)
                if trial % 2:
                    z = 0.1 * z + (4.0 * amp * (rng.random(len(kinds)) - 0.5) * (rng.random(len(kinds)) < 0.2))[kind]
                s0 = np.array(best[1])
                key = (s0 + z * (np.abs(s0 - mid) < 8.0)).tolist()
            for _ in range(PASSES):
                st = sweep(key, pred, succ, [0.0] * n)
                end = max(st[i] + ops[i]["dur"] + ops[i]["lat"] for i in range(n))
                if best is None or end < best[0] + 0.8:
                    ends = replay(ops, sorted(range(n), key=lambda i: (st[i], i)))
                    if best is None:
                        first = ends
                    if best is None or float(np.sum(ends / first)) < best[2] + 1e-9:
                        best = (end, st, float(np.sum(ends / first)))
                back = sweep([-st[i] - ops[i]["dur"] for i in range(n)], succ, pred, [o["lat"] for o in ops])
                key = [-back[i] - ops[i]["dur"] for i in range(n)]
        KEPT[n] = best[1]
    st = KEPT[n]
    return sorted(range(n), key=lambda i: (st[i], i)), st


def replay(ops, order):
    free, end, turn = {}, [None] * len(ops), {}
    last = 0 * CY
    for i in order:
        o = ops[i]
        t = free.get(o["eng"], 0 * CY)
        if o["hard"]:
            x = end[o["hard"][0]]
            for k in o["hard"][1:]:
                x = np.maximum(x, end[k])
            t = np.maximum(t, x + HOP)
        for k in o["after"]:
            t = np.maximum(t, end[k])
        if o.get("turn"):
            if o["turn"] in turn:
                t = np.maximum(t, end[turn[o["turn"]]] + HOP)
            turn[o["turn"]] = i
        free[o["eng"]] = t + o["durs"]
        end[i] = free[o["eng"]] + o["lats"]
        if o["eng"] == "y":
            last = np.maximum(last, end[i])
    return last


def mark(ops, order):
    end, turn = {}, {}
    for i in order:
        if ops[i].get("group"):
            end[ops[i]["group"]] = i
        b = ops[i].get("turn")
        if b:
            if b in turn and turn[b] not in ops[i]["hard"]:
                ops[i]["hard"].append(turn[b])
            turn[b] = i
    for i in end.values():
        ops[i]["flag"][0] = True


def emit(g, T, ops, order):
    q = {"v": g.vector, "s": g.scalar, "p": g.tensor, "g": g, "y": g.sync}
    cnt = {}
    clock = {e: {} for e in q}
    done = {}
    for i in order:
        o = ops[i]
        e = o["eng"]
        if e in "de":
            cnt[o["sem"]] = o["val"]
            done[i] = (o["sem"], o["val"], {o["sem"]: o["val"]})
            continue
        ck = clock[e]
        need = {}
        for k in o["hard"]:
            s, v, _c = done[k]
            if ck.get(s, 0) < v and (s not in need or need[s][0] < v):
                need[s] = (v, k)
        for s, (v, k) in sorted(need.items(), key=lambda z: -z[1][1]):
            if ck.get(s, 0) >= v:
                continue
            q[e].wait_ge(T.sem[s], v)
            for s2, v2 in done[k][2].items():
                if ck.get(s2, 0) < v2:
                    ck[s2] = v2
        ins = o["fn"](g)
        s = o["sem"] or "q" + e
        cnt[s] = cnt.get(s, 0) + o["val"]
        if not o.get("own"):
            ins.then_inc(T.sem[s], o["val"])
        c = dict(ck)
        c[s] = cnt[s]
        done[i] = (s, cnt[s], c)
    for s, v in cnt.items():
        if max(clock[e].get(s, 0) for e in q) < v:
            g.wait_ge(T.sem[s], v)


def hand_on(g, core, T, topo, r):
    src, dst = T.cores[r], T.cores[(r - 1) % len(T.cores)]
    rid, pid, _se = topo.addr(dst)
    came = len([e for e in topo.engines(src, core) if e not in topo.engines(src, dst)])
    for t in range(ST - 1):
        a = (t + 1) * (J + WX) - WX + O
        half = T.DB[:, a + S // 2:a + S]
        g.wait_ge(T.sem["ha%d" % t], came)
        g.remote_dma(half, half, T.sem["hb%d" % t], T.sem["hl%d" % t], pid, rid, topo.mask(core, dst))
    for t in range(ST - 1):
        g.wait_ge(T.sem["hl%d" % t], len(topo.engines(core, dst)))


def rank_program(g, core, T, topo):
    rank = T.rank_of(core)
    if rank is None:
        for r in range(len(T.cores)):
            if helper(T, r, topo) == core:
                hand_on(g, core, T, topo, r)
        return
    ops = build(T, rank, topo, core)
    depend(ops)
    order, _st = schedule(ops)
    mark(ops, order)
    emit(g, T, ops, order)
